import numpy as np, ml_dtypes
CORES = [1,5,17,21,33,37,49,53]
N = 8
BF = ml_dtypes.bfloat16
def gentries(a):
    return np.ascontiguousarray(a.reshape(8, 16, -1).transpose(0, 2, 1)).reshape(8, -1)
def gtable(e):
    e = np.asarray(e); return np.ascontiguousarray(e.reshape(8, -1, 16).transpose(0, 2, 1)).reshape(128, -1).astype(np.int32)
P, H, S, ST, RO, CAP = 3072, 2048, 256, 4, 2, 48
def parts(rng):
    x = rng.integers(0, 256, (N, 8, 16, P)); l = rng.integers(0, P, (N, 8, 16, H)); w = rng.integers(0, H, (N, 8, P))
    hs = np.ascontiguousarray(np.argsort(rng.random((N, 8, RO, H)), axis=-1)[..., :S])
    a = rng.choice(np.array([0.5, 0.7, 0.9, 1.1]), (N, 8, 1, RO, 1)) + 0.4 * (rng.random((N, 8, 1, RO, S)) - 0.5)
    d = np.minimum((256 * rng.random((N, 8, 16, RO, S)) ** a).astype(np.int64), 255)
    return x, l, w, hs, d
def lanes(rng, l, w, hs):
    K = (P - 2) // ((ST + 1) * S); steps = np.zeros((N, 8, ST + 1, S, K), np.int64)
    for q in range(N):
        for g in range(8):
            o = (4 + rng.permutation(H - 8)[:(ST + 1) * S]).reshape(ST + 1, S)
            c = (1 + rng.permutation(P - 2)[:(ST + 1) * S * K]).reshape(ST + 1, S, K)
            u = rng.integers(0, K, (16, ST + 1, S))
            l[q, g][:, o] = c[np.arange(ST + 1)[:, None], np.arange(S), u]
            w[q, g][c[:ST]] = o[1:, :, None]
            hs[q, g, 0] = o[0]; steps[q, g] = c
    return steps
def levels(rng):
    x = rng.integers(0, 100, (N, 8, 16, P)); x[1::2] += 150
    x[:, 4:] = rng.integers(0, 30, (N, 4, 16, P)); x[1::2, 4:] += 225
    return x
def pack(x, l, w, hs, d):
    return {"xs": x.reshape(N, 128, P).astype(np.float32).astype(BF), "hl": np.ascontiguousarray(l.reshape(N, 128, H)).astype(np.int32), "wr": np.ascontiguousarray(w).astype(np.int32),
            "ho": np.stack([gtable(a.reshape(8, -1)) for a in hs]), "dm": d.reshape(N, 128, RO * S).astype(np.float32).astype(BF)}
def setup_inputs(rng):
    return pack(*parts(rng))
def setup_inputs_room(rng):
    x, l, w, hs, d = parts(rng); x = levels(rng); c = lanes(rng, l, w, hs)
    for q in range(N):
        for g in range(8):
            n = int(rng.choice(np.array([0, 1, CAP - 1, CAP, CAP + 1, S])))
            if q == 0: n = (CAP, CAP + 1, S, CAP - 1, 1, 0, CAP, CAP + 1)[g]
            v = d[q, g, :, 0]; v[:] = 0
            v[:, rng.permutation(S)[:n]] = rng.integers(100, 150, (16, n)) if q % 2 == 0 else 255
            if q == 2 and g < 4:
                i = 1 + rng.permutation(S) % ST; v[:] = rng.integers(100, 150, (16, S))
                x[q, g][:, c[q, g][i, np.arange(S)]] += 150
    return pack(x, l, w, hs, d)
def setup_inputs_trade(rng):
    x, l, w, hs, d = parts(rng); x = levels(rng); c = lanes(rng, l, w, hs); ends = np.array([0, 1, 2, 3, H - 4, H - 3, H - 2, H - 1])
    for q in range(N):
        for g in range(8):
            last = c[q, g, ST]; w[q, g][last] = rng.choice(ends, last.shape)
            m = rng.random(S) < 0.5; m[:3] = True
            if q % 2 == 1 and g >= 6: m[CAP // 2:] = False
            d[q, g, :, 0] = np.where(m, rng.integers(100, 150, (16, S)) if q % 2 == 0 else 255, 0)
            if g >= 4: w[q, g][last[:3]] = np.array([1, H - 1, 0])[:, None]
            if q % 2 == 1:
                own = l[q, g][0, hs[q, g, 0]][m]
                l[q, g][:, ends] = rng.permutation(np.concatenate([rng.choice(own, 64), rng.integers(0, P, 64)])).reshape(16, 8)
                if g >= 4:
                    l[q, g][:, np.array([1, H - 1, 0])] = np.array([own[0], P - 1, 0])
                    hs[q, g, 1] = hs[q, g, 0]
                    d[q, g, :, 1] = np.where(m, 255, 0) if q % 4 == 1 else 0
                    if q % 4 == 3: x[q, g][:, own[0]] = 255
    return pack(x, l, w, hs, d)
def setup_inputs_ties(rng):
    x, l, w, hs, d = parts(rng); pal = rng.integers(0, 255, (N, 8, 16, 7))
    x = np.take_along_axis(pal, rng.integers(0, 7, (N, 8, 1, P)), 3)
    for t in range(RO):
        e = np.take_along_axis(l[:, :, t], hs[:, :, t], 2); v = np.take_along_axis(x, e[:, :, None, :], 3)
        o = np.argsort(rng.random((N, 8, 16, S)), axis=2)
        d[:, :, :, t] = v + (o >= rng.integers(8, 11, (N, 8, 1, S)))
    if RO > 2:
        q = int(rng.integers(0, N)); d[q, :, :, :2] = 255; d[q, 0, :, 0, 0] = 0
        w[q, 0, l[q, 0, 0, hs[q, 0, 0, 0]]] = np.setdiff1d(np.arange(H), hs[q, 0, 0])[0]
    return pack(x, l, w, hs, d)
def setup_inputs_alike(rng):
    x, l, w, hs, d = parts(rng)
    w[:, 0] = rng.choice(rng.permutation(H)[:40], (N, P))
    l[:, 2] = rng.choice(np.concatenate([np.array([0, P - 1]), 1 + rng.permutation(P - 2)[:60]]), (N, 16, H))
    x[:, 3] = rng.integers(0, 16, (N, 16, P)); v = rng.integers(0, 256, x[1::2, 3].shape)
    x[1::2, 3] = np.where(np.argsort(rng.random(v.shape), axis=1) < 12, 255, v); d[::2, 3, :, 0] = 0
    w[:, 4] = np.take_along_axis(hs[:, 4, 0], rng.integers(0, S, (N, P)), 1)
    x[:, 5] = rng.choice(np.array([0, 1, 254, 255]), (N, 16, P))
    for q in range(N):
        e = l[q, 6][0, hs[q, 6, 0]]
        l[q, 6][rng.integers(1, 16, S), w[q, 6][e]] = e
    w[:, 7, ::2] = rng.choice(np.array([0, H - 1]), (N, (P + 1) // 2))
    return pack(x, l, w, hs, d)
def setup_inputs_spread(rng):
    x, l, w, hs, d = parts(rng)
    x = np.minimum(np.exp2(8 * rng.random((N, 8, 1, P))) * (0.25 + 1.5 * rng.random((N, 8, 16, P))), 255).astype(np.int64)
    d = np.minimum(np.exp2(8 * rng.random((N, 8, 1, RO, S))) * (0.25 + 1.5 * rng.random((N, 8, 16, RO, S))), 255).astype(np.int64)
    w = np.minimum((H * rng.random((N, 8, P)) ** 2).astype(np.int64), H - 1)
    q = rng.permutation(N); d[q[0]] = 0; d[q[1]] = 255
    return pack(x, l, w, hs, d)
def check_inputs(d):
    bad = []
    for k in ("xs", "dm"):
        v = np.asarray(d[k]).astype(np.float32)
        if not np.all((v >= 0) & (v <= 255) & (v == np.floor(v))): bad.append("whole numbers of " + k)
    for k, hi in (("hl", P - 1), ("wr", H - 1), ("ho", H - 1)):
        if np.min(d[k]) < 0 or np.max(d[k]) > hi: bad.append("range of " + k)
    e = np.sort(np.stack([gentries(a) for a in d["ho"]]).reshape(N, 8, RO, S), axis=-1)
    if np.any(e[..., 1:] == e[..., :-1]): bad.append("different holders of a round in ho")
    return bad
def nearest(x, lc, x0):
    dist = np.add.reduce(np.abs(x[:, lc] - x0[:, None, :]), axis=0)
    j = np.argmin(dist, axis=0)
    return j, lc[j, np.arange(lc.shape[1])]
def lowest(key, on, size):
    k = np.arange(key.shape[0]); first = np.full(size, key.shape[0]); np.minimum.at(first, key[on], k[on])
    return on & (first[key] == k)
def climb(x, l, w, h0, d, t, need):
    k = np.arange(S); e0 = l[t, h0]; x0 = x[:, e0]
    vouched = np.zeros(H, bool); vouched[h0] = True
    hv, jv, ev = [h0], [np.full(S, t)], [e0]
    up = np.ones(S, bool); m = np.zeros(S, np.int64); h = w[e0]
    for i in range(1, ST + 1):
        up = lowest(h, up, H) & ~vouched[h]
        vouched[h[up]] = True
        j, e = nearest(x, l[:, h], x0)
        able = up & (np.add.reduce((x[:, e] >= d).astype(np.int64), axis=0) >= need)
        m[able] = i; up = up & ~able
        hv.append(h); jv.append(j); ev.append(e); h = w[e]
    for i in range(ST + 1):
        c = (m > 0) & (m >= i)
        v = np.where(m > i, ev[min(i + 1, ST)], e0)
        l[jv[i][c], hv[i][c]] = v[c]
        if i > 0: w[ev[i][m > i]] = hv[i][m > i]
    c = m > 0
    w[e0[c]] = np.stack(hv)[m, k][c]
    u = np.flatnonzero(up)[:CAP]
    return int(np.count_nonzero(c)), (e0[u], x0[:, u], d[:, u], h[u])
def reference(xs, hl, wr, ho, dm):
    x = xs.astype(np.float32).astype(np.int64).reshape(N, 8, 16, P); l = hl.astype(np.int64).reshape(N, 8, 16, H); w = wr.astype(np.int64)
    hs = np.stack([gentries(a) for a in ho]).astype(np.int64).reshape(N, 8, RO, S); d = dm.astype(np.float32).astype(np.int64).reshape(N, 8, 16, RO, S)
    odd = [0] * N
    for t in range(RO):
        paid = [0] * N; sent = {}
        for a in range(N):
            for g in range(8):
                n, sent[a, g] = climb(x[a, g], l[a, g], w[a, g], hs[a, g, t], d[a, g, :, t], t, 9 + odd[a])
                paid[a] += n
        swaps = []
        for a in range(N):
            b = (a + 1 + t % (N - 1)) % N
            for g in range(8):
                e0, x0, dd, h = sent[a, g]
                j, e1 = nearest(x[b, g], l[b, g][:, h], x0)
                able = np.add.reduce((x[b, g][:, e1] >= dd).astype(np.int64), axis=0) >= 9 + odd[b]
                ok = lowest(e1, able & ~np.isin(e1, sent[b, g][0]), P)
                swaps.append((a, b, g, e0[ok], e1[ok]))
        for a, b, g, e0, e1 in swaps:
            va, vb = x[a, g][:, e0], x[b, g][:, e1]
            x[a, g][:, e0] = vb; x[b, g][:, e1] = va
        odd = [n & 1 for n in paid]
    return {"yx": x.reshape(N, 128, P).astype(np.float32).astype(BF), "yl": l.reshape(N, 128, H).astype(np.float32), "yw": w.astype(np.float32)}

@@ -1,0 +1,661 @@
+import numpy as np
+from concourse.mybir import AluOpType as OP, AxisListType, ActivationFunctionType as AF
+
+N = 8
+NP, NHD = 3072, 2048
+N3 = 44
+C1 = 28
+C3 = 22
+REPA = 6
+NENG = 8
+F, B, H, I, U = "float32", "bfloat16", "float16", "int32", "uint16"
+SB = {
+    "X": (NP + 96, B), "Li": (NHD, I), "L": (NHD + 1280, F), "Lo": (NHD, F), "W": (NP + 1024, F), "V": (NHD + 1280, F),
+    "wi": (192, I), "wc": (192, H), "hoi": (32, I), "hou": (32, U), "dem": (544, B),
+    "ones": (256, B), "idn": (128, B), "nidn": (128, B), "bo": (128, B), "boh": (128, H),
+    "nboh": (128, H), "bob": (128, B), "sel": (8, B), "Q": (144, B), "ST": (2048, H),
+    "pi": (4, I), "pf": (8, F), "ar": (256, F), "oh16": (16, F), "cse": (128, B),
+    "csh": (128, H), "rst": (128, F), "jrow": (128, B), "p0": (128, B), "ii": (64, I), "cu": (64, U),
+    "wr32": (256, F), "wrb": (256, B), "nthr": (256, B), "wC": (16, F), "dL": (80, F), "dW": (64, F), "K1": (64, F),
+    "K2": (64, F), "dX": (12, F), "mk": (512, F), "need": (2, F),
+    "hoff": (80, U), "Lu": (256, U), "Lg": (1280, F), "dd": (4096, B), "da": (4096, B), "h32": (1024, F), "ag": (1024, B),
+    "x0": (272, B), "xr": (4096, B), "pm": (256, F), "mn": (16, F), "st0": (144, B), "st1": (144, B), "OH": (1280, B),
+    "em": (1280, H), "es": (1280, F), "eoff": (80, U), "eC": (80, F), "hr": (1024, H), "hs": (1024, H), "hC": (80, F),
+    "E0": (272, F), "H5": (272, F), "Tv": (2064, F), "E": (2176, B), "vg": (512, B), "sg": (1024, B), "fl": (64, F),
+    "up": (16, F), "sv": (80, F), "pd": (80, F), "gt": (80, F), "wu": (16, F), "s1": (80, F), "s2": (80, F),
+    "s3": (240, F), "s4": (80, F), "s5": (80, F), "s6": (80, F), "oL": (80, U), "oT": (80, U), "oW": (64, U), "tl": (1280, F),
+    "ed": (64, F), "e0d": (64, F), "uph": (16, H), "prb": (256, B), "jk": (768, B), "ac": (4, F), "uo": (32, U),
+    "rd": (4, F), "rb": (4, B), "ri": (4, I),
+    "rq0": (144, F), "rq1": (144, F), "lq0": (144, F), "lq1": (144, F), "rs0": (48, B), "rs1": (48, B),
+    "ls0": (48, B), "ls1": (48, B), "xs0": (48, B), "y1": (48, F), "y2": (48, F), "y3": (48, F), "y5": (48, F),
+    "e0c": (4, F), "fC": (4, F), "z1": (4, F), "z2": (4, F), "z3": (4, F), "dx": (48, B), "fr": (48, F),
+    "b1": (48, B), "b2": (48, B), "b3": (48, B), "E2": (288, B),
+}
+PS = ["pa", "pb", "pk0", "pk1", "pc", "pdd", "pm0", "pm1"]
+SCRATCH = {k: ("sbuf", [128, w], d) for k, (w, d) in SB.items()}
+for _k in PS:
+    SCRATCH[_k] = ("psum", [128, 512], F)
+NDMA = 11
+SEMAPHORES = ["cD", "cA", "cP", "cG"] + ["dm%d" % k for k in range(NDMA)] + ["ar%d" % k for k in range(4)] + ["lc"]
+SIZE = {F: 4, I: 4, B: 2, H: 2, U: 2}
+COSTS = [dict(cyc=1.0, g=1.56, sc=3.8, pe=0.6, hop=90.0, rem=3000.0), dict(cyc=1.0, g=1.1, sc=2.0, pe=0.9, hop=150.0, rem=4000.0),
+         dict(cyc=1.0, g=2.0, sc=5.5, pe=0.45, hop=60.0, rem=2500.0)]
+RND = 1.5 * 2 ** 23
+NLOAD = 7
+BIAS = {"send": 5000.0, "came": 5000.0}
+TRIES, SEED, WIN = 2500, 1, 0.3
+
+
+def v(name, lo=0, hi=None, step=1, p=None):
+    if hi is None:
+        hi = SB[name][0] if name in SB else 512
+    return (name, lo, hi, step, p)
+
+
+def ind(win, off):
+    return ("I", win, off)
+
+
+def ap(T, x):
+    if not isinstance(x, tuple):
+        return x
+    if x[0] == "I":
+        return ap(T, x[1]).indirect(ap(T, x[2]))
+    name, lo, hi, step, p = x
+    ps = slice(None) if p is None else slice(*p)
+    return T[name][ps, lo:hi:step] if step > 1 else T[name][ps, lo:hi]
+
+
+def cnt(x):
+    if x[0] == "I":
+        return 16 * cnt(x[2])
+    return (x[2] - x[1] + x[3] - 1) // x[3]
+
+
+def wide(x):
+    return x[0] in PS or SIZE[SB[x[0]][1]] == 4
+
+
+def regs(*xs):
+    out = []
+    for x in xs:
+        if isinstance(x, tuple):
+            out += [x[1], x[2]] if x[0] == "I" else [x]
+    return out
+
+
+def program(c):
+    ops, tag = [], ["", 0]
+
+    def add(eng, fn, out, ins, cost, lat=0.0, kind="c", extra=()):
+        W = [out[1]] if out[0] == "I" else [out]
+        R = regs(*ins) + ([out[2]] if out[0] == "I" else [])
+        ops.append(dict(e=eng, fn=fn, R=R, W=W + list(extra), cost=cost, lat=lat, kind=kind, tag=tuple(tag)))
+
+    def vcost(out, in0, others, two=False, fix=50.0):
+        n = cnt(out)
+        if out[0] == "I":
+            return fix + n * c["sc"] * c["cyc"]
+        if in0[0] == "I":
+            return fix + n * c["g"] * c["cyc"]
+        if two:
+            f = 1.0 if any(x[0] in PS for x in [in0] + others) else 2.0
+        else:
+            f = 1.0 if any(wide(x) for x in [out, in0] + others) else 0.5
+        return max(64, n * f) * c["cyc"]
+
+    def tt(out, a, b, op):
+        add("D", lambda g, T, x: g.vector.tensor_tensor(ap(T, out), ap(T, a), ap(T, b), op), out, [a, b], vcost(out, a, [b], True))
+
+    def ts(out, a, s1, op0, s2=None, op1=None):
+        if op1 is None:
+            fn = lambda g, T, x: g.vector.tensor_scalar(ap(T, out), ap(T, a), ap(T, s1), None, op0)
+        else:
+            fn = lambda g, T, x: g.vector.tensor_scalar(ap(T, out), ap(T, a), ap(T, s1), ap(T, s2), op0, op1)
+        add("D", fn, out, [a, s1, s2], vcost(out, a, []))
+
+    def cp(out, a):
+        add("D", lambda g, T, x: g.vector.tensor_copy(ap(T, out), ap(T, a)), out, [a], vcost(out, a, []))
+
+    def scan(out, d0, d1, init, op0, op1):
+        add("D", lambda g, T, x: g.vector.tensor_tensor_scan(ap(T, out), ap(T, d0), ap(T, d1), init, op0, op1), out, [d0, d1],
+            vcost(out, d0, [d1]))
+
+    def ms(out, val):
+        add("D", lambda g, T, x: g.vector.memset(ap(T, out), val), out, [], vcost(out, out, []))
+
+    def act(out, a, func, bias=None, scale=None, accum=None, more=0.0):
+        def fn(g, T, x):
+            kw = {}
+            if bias is not None:
+                kw["bias"] = ap(T, bias)
+            if scale is not None:
+                kw["scale"] = scale
+            if accum is not None:
+                kw["accum_out"] = ap(T, accum)
+            return g.scalar.activation(ap(T, out), ap(T, a), func, **kw)
+        k = vcost(out, a, [], fix=65.0) if "I" in (out[0], a[0]) else max(64, cnt(out)) * c["cyc"] + 30
+        add("A", fn, out, [a, bias], k + more, extra=[accum] if accum else [])
+
+    def mm(lst):
+        def fn(g, T, x):
+            for o, l, r, st, sp in lst:
+                ins = g.tensor.matmul(ap(T, o), ap(T, l), ap(T, r), st, sp)
+            return ins
+        k = sum(max(min(64, cnt(l)), cnt(r)) for o, l, r, st, sp in lst) * c["pe"]
+        add("P", fn, lst[0][0], [l for o, l, r, st, sp in lst] + [r for o, l, r, st, sp in lst], k, lat=60.0,
+            extra=[o for o, l, r, st, sp in lst[1:]])
+
+    def iota(out, pat, base, ch):
+        kw = {} if SB[out[0]][1] == I else {"allow_small_or_imprecise_dtypes": True}
+        add("G", lambda g, T, x: g.iota(ap(T, out), pat, base, ch, **kw), out, [], 130 + 2 * cnt(out) * c["cyc"])
+
+    def asel(out, a, pat, cmp, base, ch):
+        add("G", lambda g, T, x: g.affine_select(ap(T, out), ap(T, a), pat, cmp, 0.0, base, ch), out, [a], 170 + 2 * cnt(out) * c["cyc"])
+
+    def load(q, out, src, nbytes):
+        add(q, lambda g, T, x: (g.sync if q == "S" else g.scalar).dma_start(ap(T, out), src(T)), out, [], 60.0, lat=nbytes, kind="d")
+
+    def store(q, dst, a, nbytes):
+        add(q, lambda g, T, x: (g.sync if q == "S" else g.scalar).dma_start(dst(T), ap(T, a)), ("out%d" % len(ops), 0, 1, 1, None), [a],
+            60.0, lat=nbytes, kind="d")
+
+    def send(k, out, a, shift):
+        def fn(g, T, x):
+            dst = T.cores[(x["rank"] + shift) % N]
+            rid, pid, _ = x["topo"].addr(dst)
+            m = sum(1 << e for e in x["topo"].engines(x["core"], dst)[:NENG])
+            return g.remote_dma(ap(T, out), ap(T, a), T.sem["ar%d" % k], T.sem.lc, pid, rid, m)
+        add("G", fn, out, [a], 300.0, lat=c["rem"], kind="r")
+        ops[-1]["k"] = k
+
+    load("S", v("wi"), lambda T: T.wr[:], 98e3)
+    load("A", v("hoi"), lambda T: T.ho[:], 16e3)
+    load("S", v("Li", 0, 1024), lambda T: T.hl[:, 0:1024], 524e3)
+    load("A", v("Li", 1024, 2048), lambda T: T.hl[:, 1024:2048], 524e3)
+    load("S", v("X", 0, NP), lambda T: T.xs[:], 786e3)
+    load("S", v("dem", 0, 256), lambda T: T.dm[:, 0:256], 65e3)
+    load("S", v("dem", 272, 528), lambda T: T.dm[:, 256:512], 65e3)
+    ms(v("ones"), 1.0)
+    asel(v("jk", 0, 128), v("ones", 0, 128), [[-16, 8], [0, 16]], OP.is_ge, 0, 1)
+    asel(v("bo"), v("jk", 0, 128), [[16, 8], [0, 16]], OP.is_ge, 15, -1)
+    asel(v("idn"), v("ones", 0, 128), [[-1, 128]], OP.is_equal, 0, 1)
+    iota(v("pi", 0, 1), [[0, 1]], 0, 1)
+    iota(v("ar"), [[0, 16], [1, 16]], 0, 0)
+    iota(v("ii", 8, 56), [[1, 48]], 0, 0)
+    iota(v("s1"), [[16, 80]], 0, 0)
+    iota(v("s2", 0, 64), [[512, 4], [16, 16]], -2048, 0)
+    ts(v("pi", 1, 2), v("pi", 0, 1), 15, OP.bitwise_and)
+    pa, pa1, fixe, fixh = v("pf", 0, 1), v("pf", 1, 2), v("pf", 2, 3), v("pf", 3, 4)
+    cp(pa, v("pi", 1, 2))
+    ts(v("oh16"), v("ar", 0, 16), pa, OP.is_equal)
+    cp(v("boh"), v("bo"))
+    for a in range(16):
+        ts(v("ST", 128 * a, 128 * a + 128), v("boh"), v("oh16", a, a + 1), OP.mult)
+    cp(v("wc"), v("wi"))
+    for b in range(8):
+        mm([(v(PS[b], 192 * k, 192 * k + 192), v("ST", 128 * (2 * b + k), 128 * (2 * b + k + 1)), v("wc"), True, True) for k in range(2)])
+        act(v("W", 384 * b, 384 * b + 384), v(PS[b], 0, 384), AF.Identity, bias=32.0)
+    cp(v("hou"), v("hoi"))
+    for k in range(2):
+        ts(v("L", 1024 * k, 1024 * k + 1024), v("Li", 1024 * k, 1024 * k + 1024), -1024.0, OP.add)
+    ts(v("pf", 4, 5), v("oh16", 15, 16), -16.0, OP.mult, 1.0, OP.add)
+    tt(pa1, pa, v("pf", 4, 5), OP.add)
+    ts(fixe, v("oh16", 15, 16), -4096.0, OP.mult, 5120.0, OP.add)
+    ts(fixh, v("oh16", 15, 16), -2048.0, OP.mult, 2048.0, OP.add)
+    ts(v("pm", 0, 128), v("ar", 0, 128), pa, OP.is_equal, 8192.0, OP.mult)
+    ts(v("es", 0, 128), v("ar", 0, 128), pa1, OP.is_equal, -2048.0, OP.mult)
+    tt(v("pm", 128, 256), v("pm", 0, 128), v("es", 0, 128), OP.add)
+    cp(v("csh"), v("pm", 128, 256))
+    tt(v("cse"), v("pm", 128, 256), v("es", 0, 128), OP.add)
+    ts(v("rst"), v("ar", 0, 128), 0.0, OP.is_equal, 8192.0, OP.mult)
+    ts(v("p0"), v("ar", 0, 128), 0.0, OP.is_equal)
+    ts(v("jrow"), v("ar", 0, 128), 1.0 / 32, OP.mult)
+    ts(v("nidn"), v("idn"), -1.0, OP.mult)
+    ts(v("nboh"), v("bo"), -1.0, OP.mult)
+    ts(v("bob"), v("bo"), 2.0 ** 55, OP.mult, 2.0 ** 55, OP.mult)
+    cp(v("sel"), v("bo", 0, 128, 16))
+    ms(v("Q"), 0.0)
+    cp(v("Q", 15, 143, 16), v("bo", 0, 128, 16))
+    cp(v("cu", 8, 56), v("ii", 8, 56))
+    ms(v("mk", 0, 256), 1.0)
+    ms(v("mk", 256, 512), 20.0)
+    ms(v("es", 256, 512), 1.0 / 1.7)
+    scan(v("wr32"), v("es", 256, 512), v("mk", 0, 256), 1.7 ** 129, OP.mult, OP.mult)
+    cp(v("wrb"), v("wr32"))
+    ts(v("nthr"), v("wrb"), -2.56, OP.mult)
+
+    def S(a):
+        return v("Q", 15 - a, 143 - a)
+
+    def rep48(lo, hi):
+        return v("cu", 8 + lo, 8 + hi)
+
+    mm([(v("pdd", 0, 16), S(a), v("wrb", a, 256, 16), a == 0, a == 15) for a in range(16)])
+    ts(v("wC"), v("pdd", 0, 16), 1.0 / 16, OP.mult)
+    ts(v("dL"), v("s1"), pa, OP.add, 2048.0, OP.add)
+    ts(v("dW"), v("s1", 0, 64), pa, OP.add, 3072.0, OP.add)
+    ts(v("K1"), v("s2", 0, 64), pa, OP.add)
+    ts(v("K2"), v("s2", 0, 64), pa, OP.add, 256.0, OP.add)
+    ts(v("dX", 0, 6), v("s1", 0, 6), pa, OP.add, 3072.0, OP.add)
+    ts(v("dX", 8, 11), v("dL", 0, 3), -1.0, OP.mult, 2047.5, OP.add)
+    iota(v("V", 0, NHD), [[0, NHD]], 0, 0)
+    ms(v("need", 0, 1), 8.5)
+    ms(v("dem", 256, 272), 300.0)
+    ms(v("dem", 528, 544), 300.0)
+    ms(v("x0", 256, 272), 0.0)
+    ms(v("E0", 256, 272), 2500.0)
+    ms(v("H5", 256, 272), 0.0)
+    ms(v("Tv", 2048, 2064), 0.0)
+    ms(v("st0", 0, 16), 1.0)
+    ms(v("st1", 0, 16), 1.0)
+    ms(v("gt", 64, 80), 0.0)
+
+    Xw, Lw, Ww = v("X", 0, NP), v("L", 0, NHD), v("W", 0, NP)
+    one1 = v("ones", 0, 128, 1, (0, 1))
+    rot = [0]
+
+    def argmin(pk, st, base, ns, pmv):
+        jr = (v(pk, 0, 128), one1, v("jrow", 0, 128, 1, (0, 1)))
+        mm([jr + (True, False)])
+        mm([(v(pk, j, 128, 16, (0, ns)), v("da", base + j, base + 16 * ns, 16), v("sel"), False, False) for j in range(16)] + [jr + (False, True)])
+        scan(pmv, v("rst"), v(pk, 0, 128), 0.0, OP.add, OP.min)
+        mn = v("mn", pmv[1] // 16, pmv[1] // 16 + 8)
+        cp(mn, v("pm", pmv[1] + 15, pmv[2], 16))
+        tt(v(st, 16, 144), ind(mn, rep48(0, 8)), pmv, OP.is_equal)
+        mm([(v(pk, 128, 128 + ns), v("p0", 0, 128, 1, (0, 1)), v("ones", 0, ns, 1, (0, 1)), True, False),
+            (v(pk, 128, 128 + ns), v(st, 16, 144, 1, (0, ns)), v("idn", 0, ns, 1, (0, ns)), False, False),
+            (v(pk, 128, 128 + ns), v(st, 15, 143, 1, (0, ns)), v("nidn", 0, ns, 1, (0, ns)), False, True)])
+
+    def after_e(t, i, hf):
+        pk, o, oc = PS[2 + hf], 256 * i + 128 * hf, 16 * i + 8 * hf
+        mm([(v(pk, 256, 384), v("boh"), v("em", o, o + 128), True, True)])
+        scan(v("es", o, o + 128), v("cse"), v(pk, 256, 384), 0.0, OP.add, OP.min)
+        eo = v("eoff", oc, oc + 8)
+        ts(eo, v("es", o + 15, o + 128, 16), fixe, OP.add)
+        if i < 4:
+            act(v("h32", o, o + 128), ind(Ww, eo), AF.Copy)
+            ts(v("hr", o, o + 128), v("h32", o, o + 128), RND - 32.0, OP.add, -RND, OP.add)
+            scan(v("hs", o, o + 128), v("csh"), v("hr", o, o + 128), 0.0, OP.add, OP.min)
+            ts(v("hoff", oc + 16, oc + 24), v("hs", o + 15, o + 128, 16), fixh, OP.add)
+        else:
+            act(v("H5", 128 * hf, 128 * hf + 128), ind(Ww, eo), AF.Identity, bias=-32.0)
+        if i == 0:
+            act(v("x0", o, o + 128), ind(Xw, eo), AF.Copy)
+            act(v("E0", o, o + 128), v(pk, 256, 384), AF.Copy)
+        else:
+            q = 512 * (i % 2) + 256 + 128 * hf
+            tt(v("sg", q, q + 128), ind(Xw, eo), v("dem", 272 * t + 128 * hf, 272 * t + 128 * hf + 128), OP.is_ge)
+            act(v("OH", o, o + 128), v(pk, 128, 256), AF.Copy)
+
+    def chunks(lo, hi, k):
+        m = (hi - lo + k - 1) // k
+        return [(lo + (hi - lo) * q // m // 2 * 2, lo + (hi - lo) * (q + 1) // m // 2 * 2) for q in range(m)] if m else []
+
+    for t in range(2):
+        need = v("need", t, t + 1)
+        tag[:] = ["first", 10 * t]
+        mark = v("mk", 256 * t, 256 * t + 256)
+        h0 = v("hou", 16 * t, 16 * t + 16)
+        cp(v("oL", 0, 16), v("hoi", 16 * t, 16 * t + 16))
+        act(ind(v("V"), h0), mark, AF.Silu, more=1300.0 if t == 0 else 0.0)
+        ts(v("OH", 0, 256), v("ones"), v("oh16", t, t + 1), OP.mult)
+        act(v("Lg", 0, 256), ind(Lw, h0), AF.Copy)
+        ts(v("em", 0, 256), v("Lg", 0, 256), v("oh16", t, t + 1), OP.mult)
+        for hf in range(2):
+            after_e(t, 0, hf)
+        ts(v("eC", 0, 16), v("es", 15, 256, 16), fixe, OP.add)
+        for j in range(16):
+            o, a = v("xr", j, 4096, 16), v("x0", 0, 256)
+            if j < REPA:
+                act(o, a, AF.Copy)
+            else:
+                cp(o, a)
+        for i in range(1, 5):
+            q = 16 * i
+            tag[:] = ["death", 10 * t + i]
+            hC, sv, dl, ol, pdi, eC = [v(nm, q, q + 16) for nm in ("hC", "sv", "dL", "oL", "pd", "eC")]
+            so, fo, vg = 512 * (i % 2), 32 * (i % 2), v("vg", 256 * (i % 2), 256 * (i % 2) + 256)
+            ts(hC, v("hs", 256 * i - 241, 256 * i, 16), fixh, OP.add)
+            act(vg, ind(v("V", 0, NHD), v("hoff", q, q + 16)), AF.Relu, bias=-0.25 - 0.75 * t)
+            lst, o = [], 0
+            for cc in range(16):
+                w = 256 - 16 * cc
+                ts(v("E", o, o + w), v("hr", 256 * (i - 1) + 16 * cc, 256 * i), v("hC", q + cc, q + cc + 1), OP.is_equal,
+                   v("wC" if i == 1 else "wu", cc, cc + 1), OP.mult)
+                lst.append((v("pc", 16 * cc, 256), v("bo"), v("E", o, o + w), cc == 0, False))
+                o += w
+                if cc % 4 == 3:
+                    mm(lst)
+                    lst = []
+            mm([(v("pc", 0, 256), v("idn"), v("nthr"), False, False), (v("pc", 0, 256), v("bob"), vg, False, True)])
+            act(v("sg", so, so + 256), v("pc", 0, 256), AF.Sign, scale=-1.0)
+            mm([(v("pdd", 0, 16), S(a), v("sg", so + a, so + 256, 16), a == 0, a == 15) for a in range(16)])
+            if i == 1:
+                ts(sv, v("pdd", 0, 16), 0.0, OP.is_ge)
+            else:
+                ts(v("fl", fo, fo + 16), v("pdd", 0, 16), 0.0, OP.is_ge)
+                tt(sv, v("fl", fo, fo + 16), v("up"), OP.mult)
+            tt(v("s3", q, q + 16), hC, dl, OP.subtract)
+            tt(v("s3", 80 + q, 96 + q), v("s3", q, q + 16), sv, OP.mult)
+            tt(v("s3", 160 + q, 176 + q), v("s3", 80 + q, 96 + q), dl, OP.add)
+            cp(ol, v("s3", 160 + q, 176 + q))
+            if i < 4:
+                act(ind(v("V"), ol), mark, AF.Silu)
+            else:
+                ts(v("uph"), sv, -32.0, OP.mult)
+                mm([(v("pm1", 0, 256), one1, v("ones", 0, 256, 1, (0, 1)), True, False)] +
+                   [(v("pm1", a, 256, 16), v("ST", 128 * a, 128 * a + 128), v("uph"), False, False) for a in range(16)])
+            for hf in range(2):
+                pk, st, o = PS[2 + hf], "st%d" % hf, 128 * hf
+                tag[0] = "near%d" % hf
+                ho = v("hoff", q + 8 * hf, q + 8 * hf + 8)
+                lg = v("Lg", 256 * i + o, 256 * i + o + 128)
+                act(lg, ind(Lw, ho), AF.Copy)
+                ts(v("Lu", o, o + 128), lg, 1024.0, OP.add)
+                c3 = chunks(0, N3, C3) if hf == 0 else chunks(256 - N3, 256, C3)
+                c1 = chunks(N3, 128, C1) if hf == 0 else chunks(128, 256 - N3, C1)
+                for a, b in c3:
+                    r = rot[0] % 2
+                    rot[0] += 1
+                    w = 16 * (b - a)
+                    ag = v("ag", 512 * r, 512 * r + w)
+                    act(ag, ind(Xw, v("Lu", a, b)), AF.Copy)
+                    mm([(v(PS[r], 0, w), v("nidn"), v("xr", 16 * a, 16 * b), True, False)])
+                    mm([(v(PS[r], 0, w), v("idn"), ag, False, True)])
+                    act(v("da", 16 * a, 16 * b), v(PS[r], 0, w), AF.Abs)
+                for a, b in c1:
+                    d = v("dd", 16 * a, 16 * b)
+                    tt(d, ind(Xw, v("Lu", a, b)), v("xr", 16 * a, 16 * b), OP.subtract)
+                    act(v("da", 16 * a, 16 * b), d, AF.Abs)
+                tag[0] = "chain%d" % hf
+                argmin(pk, st, 16 * o, 128, v("pm", o, o + 128))
+                tt(v("em", 256 * i + o, 256 * i + o + 128), lg, v(pk, 128, 256), OP.mult)
+                after_e(t, i, hf)
+            tag[0] = "tv"
+            ts(eC, v("es", 256 * i + 15, 256 * i + 256, 16), fixe, OP.add)
+            emi, emp, em0 = v("em", 256 * i, 256 * i + 256), v("em", 256 * i - 256, 256 * i), v("em", 0, 256)
+            mm([(v("pm0", 0, 256), v("boh"), emi, True, False), (v("pm0", 0, 256), v("nboh"), emp, False, True),
+                (v("pm0", 256, 512), v("boh"), em0, True, False), (v("pm0", 256, 512), v("nboh"), emi, False, True)])
+            tt(v("Tv", 512 * i - 512, 512 * i - 256), v("OH", 256 * i - 256, 256 * i), v("pm0", 0, 256), OP.mult)
+            tt(v("Tv", 512 * i - 256, 512 * i), v("OH", 256 * i, 256 * i + 256), v("pm0", 256, 512), OP.mult)
+            tt(v("e0d", q - 16, q), v("eC", 0, 16), v("dW", q - 16, q), OP.subtract)
+            tag[0] = "paid"
+            if i == 4:
+                mm([(v("pm1", 0, 256), v("bo"), v("sg", so + 256, so + 512), False, True)])
+            mm([(v("pdd", 16, 32), S(a), v("sg", so + 256 + a, so + 512, 16), a == 0, a == 15) for a in range(16)])
+            ts(v("fl", fo + 16, fo + 32), v("pdd", 16, 32), need, OP.is_ge)
+            tt(pdi, sv, v("fl", fo + 16, fo + 32), OP.mult)
+            if i < 4:
+                tt(v("up"), sv, pdi, OP.subtract)
+                tt(v("wu"), v("wC"), v("up"), OP.mult)
+        tag[:] = ["send", 10 * t + 5]
+        rq, lq, rs, ls = "rq%d" % t, "lq%d" % t, "rs%d" % t, "ls%d" % t
+        ts(v("vg", 0, 256), v("pm1", 0, 256), 31.0, OP.add, need, OP.is_lt)
+        scan(v("prb"), v("ones"), v("vg", 0, 256), 0.0, OP.mult, OP.add)
+        for k in range(3):
+            act(v("jk", 256 * k, 256 * k + 256), v("prb"), AF.Sign, bias=v("dX", 8 + k, 9 + k), accum=v("ac", k, k + 1))
+        ix = v("uo", 0, 3)
+        ts(ix, v("ac", 0, 3), -0.5, OP.mult, 128.0, OP.add)
+        ts(v("y1"), ind(v("H5"), ix), RND, OP.add, -RND, OP.add)
+        scan(v(rq, 96, 144), v("csh", 0, 48), v("y1"), 0.0, OP.add, OP.min)
+        act(v(rq, 0, 48), ind(v("x0"), ix), AF.Copy)
+        act(v(rq, 48, 96), ind(v("dem", 272 * t, 272 * t + 272), ix), AF.Copy)
+        send(2 * t, v(lq), v(rq), t + 1)
+        act(v("xs0"), ind(v("x0"), ix), AF.Copy)
+        act(v("y2"), ind(v("E0"), ix), AF.Copy)
+        scan(v("y3"), v("cse", 0, 48), v("y2"), 0.0, OP.add, OP.min)
+        ts(v("e0c", 0, 3), v("y3", 15, 48, 16), fixe, OP.add)
+        tt(v("z1", 0, 3), v("e0c", 0, 3), v("dX", 0, 3), OP.min)
+        eo0 = v("uo", 4, 7)
+        cp(eo0, v("z1", 0, 3))
+        tag[0] = "payl"
+        cp(v("gt", 48, 64), v("pd", 64, 80))
+        for i in (2, 1, 0):
+            tt(v("gt", 16 * i, 16 * i + 16), v("gt", 16 * i + 16, 16 * i + 32), v("pd", 16 * i + 16, 16 * i + 32), OP.add)
+        tt(v("s4", 0, 64), v("gt", 0, 64), v("K1"), OP.mult)
+        ms(v("s4", 64, 80), 0.0)
+        tt(v("s5", 16, 80), v("pd", 16, 80), v("K2"), OP.mult)
+        tt(v("s4", 16, 80), v("s4", 16, 80), v("s5", 16, 80), OP.add)
+        ts(v("oT"), v("s4"), 2048.0, OP.add)
+        for a, b in ((0, 8), (8, 20), (20, 32), (32, 48), (48, 64), (64, 80)):
+            act(v("tl", 16 * a, 16 * b), ind(v("Tv"), v("oT", a, b)), AF.Copy)
+            tt(ind(v("L"), v("oL", a, b)), v("Lg", 16 * a, 16 * b), v("tl", 16 * a, 16 * b), OP.add)
+        tag[0] = "payw"
+        tt(v("ed"), v("eC", 16, 80), v("dW"), OP.subtract)
+        tt(v("s5", 0, 64), v("gt", 16, 80), v("ed"), OP.mult)
+        tt(v("s6", 0, 64), v("pd", 16, 80), v("e0d"), OP.mult)
+        tt(v("s5", 0, 64), v("s5", 0, 64), v("s6", 0, 64), OP.add)
+        tt(v("s6", 0, 64), v("s5", 0, 64), v("dW"), OP.add)
+        cp(v("oW"), v("s6", 0, 64))
+        for k in range(8):
+            act(ind(v("W"), v("oW", 8 * k, 8 * k + 8)), v("h32", 128 * k, 128 * k + 128), AF.Silu)
+        if t == 0:
+            add("D", lambda g, T, x: g.vector.tensor_reduce(ap(T, v("rd", 0, 1)), ap(T, v("gt", 0, 16)), AxisListType.X, OP.add),
+                v("rd", 0, 1), [v("gt", 0, 16)], 64.0)
+            cp(v("rb", 0, 1), v("rd", 0, 1))
+            mm([(v("pm0", 0, 1), v("ones", 0, 128), v("rb", 0, 1), True, True)])
+            cp(v("ri", 0, 1), v("pm0", 0, 1))
+            ts(v("ri", 1, 2), v("ri", 0, 1), 1, OP.bitwise_and)
+            ts(v("need", 1, 2), v("ri", 1, 2), 8.5, OP.add)
+        else:
+            act(v("Lo", 0, 1024), v("L", 0, 1024), AF.Identity, bias=1024.0)
+            act(v("Lo", 1024, 2048), v("L", 1024, 2048), AF.Identity, bias=1024.0)
+            store("S", lambda T: T.yl[:], v("Lo"), 1048e3)
+            for k in range(6):
+                w = v("W", 512 * k, 512 * k + 512)
+                ts(w, w, RND - 32.0, OP.add, -RND, OP.add)
+            store("S", lambda T: T.yw[:], v("W", 0, NP, 1, (0, 128, 16)), 98e3)
+        tag[0] = "came"
+        hq = v("uo", 8, 11)
+        ts(hq, v(lq, 96 + 15, 144, 16), fixh, OP.add)
+        ts(v("Lu", 0, 48), ind(Lw, hq), 1024.0, OP.add)
+        for k in range(2):
+            a, b = 384 * k, 384 * k + 384
+            act(v("xr", a, b), ind(v(lq, 0, 48), rep48(24 * k, 24 * k + 24)), AF.Copy)
+            tt(v("dd", a, b), ind(Xw, v("Lu", 24 * k, 24 * k + 24)), v("xr", a, b), OP.subtract)
+        for k in range(2):
+            a, b = 384 * k, 384 * k + 384
+            act(v("da", a, b), v("dd", a, b), AF.Abs)
+        cp(v("y1"), ind(Lw, hq))
+        argmin("pk0", "st0", 0, 48, v("pm", 0, 128))
+        tt(v("em", 0, 48), v("y1"), v("pk0", 128, 176), OP.mult)
+        mm([(v("pk0", 256, 304), v("boh"), v("em", 0, 48), True, True)])
+        scan(v("y3"), v("cse", 0, 48), v("pk0", 256, 304), 0.0, OP.add, OP.min)
+        fo = v("uo", 12, 15)
+        ts(fo, v("y3", 15, 48, 16), fixe, OP.add)
+        act(v("fr"), v("pk0", 256, 304), AF.Identity, bias=1024.0)
+        tt(v("b1"), ind(Xw, fo), v(lq, 48, 96), OP.is_ge)
+        tt(v("dx"), ind(Xw, fo), v(lq, 0, 48), OP.subtract)
+        ts(v("fC", 0, 3), v("y3", 15, 48, 16), fixe, OP.add)
+        mm([(v("pk1", 0, 48), v("bo"), v("b1"), True, True)])
+        scan(v("y2"), v("csh", 0, 48), v("pk1", 0, 48), 0.0, OP.add, OP.min)
+        ts(v("b2"), v("pk1", 0, 48), need, OP.is_lt)
+        ts(v("z2", 0, 3), v("y2", 15, 48, 16), fixh, OP.add, need, OP.is_ge)
+        lst = [(v("pc", 0, 48), v("idn"), v("nthr", 0, 48), True, False)]
+        for k in range(3):
+            ts(v("E2", 48 * k, 48 * k + 48), v("fr"), v("e0c", k, k + 1), OP.is_equal)
+            lst.append((v("pc", 0, 48), v("bob"), v("E2", 48 * k, 48 * k + 48), False, False))
+        lst.append((v("pc", 0, 48), v("bob"), v("b2"), False, False))
+        mm(lst)
+        tt(v("z3", 0, 3), v("z2", 0, 3), v("wC", 0, 3), OP.mult)
+        lst = []
+        for k in (2, 1, 0):
+            o = 144 + 48 * k
+            ts(v("E2", o, o + 48 - 16 * k), v("fr", 16 * k, 48), v("fC", k, k + 1), OP.is_equal, v("z3", k, k + 1), OP.mult)
+            lst.append((v("pc", 16 * k, 48), v("bo"), v("E2", o, o + 48 - 16 * k), False, k == 0))
+        mm(lst)
+        ts(v("b3"), v("pc", 0, 48), 0.0, OP.is_lt)
+        tt(v(rs), v("dx"), v("b3"), OP.mult)
+        send(2 * t + 1, v(ls), v(rs), -(t + 1))
+        scan(v("y5"), v("csh", 0, 48), v("b3"), 0.0, OP.add, OP.min)
+        tt(v("z2", 0, 3), v("fC", 0, 3), v("dX", 3, 6), OP.subtract)
+        ts(v("z3", 0, 3), v("y5", 15, 48, 16), fixh, OP.add)
+        tt(v("z3", 0, 3), v("z3", 0, 3), v("z2", 0, 3), OP.mult)
+        tt(v("z2", 0, 3), v("z3", 0, 3), v("dX", 3, 6), OP.add)
+        fo2 = v("uo", 16, 19)
+        cp(fo2, v("z2", 0, 3))
+        cp(ind(v("X"), fo2), v(lq, 0, 48))
+        tt(ind(v("X"), eo0), v("xs0"), v(ls), OP.add)
+    store("S", lambda T: T.yx[:, 0:NP // 2], v("X", 0, NP // 2), 393e3)
+    store("A", lambda T: T.yx[:, NP // 2:NP], v("X", NP // 2, NP), 393e3)
+    return ops
+
+
+def meet(a, b):
+    if a[1] >= b[2] or b[1] >= a[2]:
+        return False
+    return not (a[3] == b[3] and a[3] > 1 and (a[1] - b[1]) % a[3])
+
+
+def depend(ops):
+    acc, deps = {}, []
+    for k, o in enumerate(ops):
+        d = set()
+        for x, wr in [(x, False) for x in o["R"]] + [(x, True) for x in o["W"]]:
+            for k2, y, wr2 in acc.get(x[0], ()):
+                if x[0] in PS and (ops[k2]["e"] != o["e"] or o["e"] == "P"):
+                    d.add(k2)
+                elif (wr or wr2) and meet(x, y):
+                    d.add(k2)
+        for x, wr in [(x, False) for x in o["R"]] + [(x, True) for x in o["W"]]:
+            acc.setdefault(x[0], []).append((k, x, wr))
+        deps.append(sorted(d))
+    full = [set(d) for d in deps]
+    above = []
+    for k in range(len(ops)):
+        above.append(set(deps[k]).union(*[above[p] for p in deps[k]]))
+        deps[k] = [p for p in deps[k] if not any(p in above[p2] for p2 in deps[k])]
+    return deps, full
+
+
+def schedule(ops, deps, succ, hop, win, rnd, order=None):
+    n = len(ops)
+    late = [2000.0 + o["lat"] / 200.0 if o["kind"] == "d" else o["lat"] for o in ops]
+    eng = [o["e"] for o in ops]
+    cost = [o["cost"] for o in ops]
+
+    def gap(p, k):
+        return 0.0 if eng[p] == "P" and eng[k] == "P" else late[p] + hop
+
+    pr = [0.0] * n
+    if order is None:
+        for k in range(n - 1, -1, -1):
+            pr[k] = cost[k] + max([gap(k, s) + pr[s] for s in succ[k]] + [late[k]])
+        pr = [p + float(r) for p, r in zip(pr, rnd)]
+        for k in range(NLOAD):
+            pr[k] += 1e7 - 1e5 * k
+    left = [len(d) for d in deps]
+    est = [0.0] * n
+    ready = [k for k in range(n) if not left[k]]
+    free = {e: 0.0 for e in "DAPGS"}
+    dmafree = 0.0
+    out, start, end = [], [0.0] * n, 0.0
+    for it in range(n):
+        if order is None:
+            k0 = min(ready, key=lambda k: max(est[k], free[eng[k]]))
+            e = eng[k0]
+            tm = max(est[k0], free[e])
+            now = max((k for k in ready if eng[k] == e and est[k] <= tm + 40.0), key=lambda k: (pr[k], -k))
+            k = max((k for k in ready if eng[k] == e and est[k] <= tm + 40.0 + win * cost[now]), key=lambda k: (pr[k], -k))
+            ready.remove(k)
+        else:
+            k = order[it]
+        start[k] = max(est[k], free[eng[k]])
+        fin = free[eng[k]] = start[k] + cost[k]
+        if ops[k]["kind"] == "d":
+            dmafree = max(dmafree, fin + 2000.0) + ops[k]["lat"] / 200.0
+            late[k] = dmafree - fin
+        end = max(end, fin + late[k])
+        out.append(k)
+        for s in succ[k]:
+            est[s] = max(est[s], fin + gap(k, s))
+            left[s] -= 1
+            if not left[s] and order is None:
+                ready.append(s)
+    return out, start, end
+
+
+def plan(tries=None):
+    alts = [program(c) for c in COSTS]
+    ops = alts[0]
+    deps, full = depend(ops)
+    succ = [[] for _ in ops]
+    for k in range(len(ops)):
+        for p in deps[k]:
+            succ[p].append(k)
+    best = None
+    rng = np.random.default_rng(SEED)
+    names = sorted(set(o["W"][0][0] for o in ops))
+    part, step = np.array([o["tag"][0] for o in ops]), np.array([o["tag"][1] for o in ops])
+    kind = np.array([names.index(o["W"][0][0]) for o in ops])
+    for it in range(tries or TRIES):
+        off = np.array([BIAS.get(o["tag"][0], 0.0) for o in ops]) if best is None else best[3].copy()
+        if it:
+            k, u = rng.integers(len(ops)), rng.random(4)
+            m = np.ones(len(ops), bool)
+            if u[0] < 0.5:
+                m &= kind == kind[k]
+            if u[1] < 0.7 or u[0] >= 0.5:
+                m &= part == part[k]
+            if u[2] < 0.7:
+                m &= step == step[k]
+            off[m] += rng.normal() * (3000.0 if u[3] < 0.5 else 600.0)
+        order, start, end = schedule(ops, deps, succ, COSTS[0]["hop"], WIN, off)
+        if best is not None and end > best[2][0] * 1.01:
+            continue
+        ends = [end] + [schedule(a, deps, succ, c["hop"], 0, 0, order)[2] for a, c in zip(alts[1:], COSTS[1:])]
+        if best is None or sum(ends) + end <= sum(best[2]) + best[2][0]:
+            best = (order, start, ends, off)
+    order, start, end = best[0], best[1], best[2][0]
+    count = {e: 0 for e in "DAPG"}
+    known = {e: {} for e in "DAPGS"}
+    nd = 0
+    for k in order:
+        o = ops[k]
+        kn, waits = known[o["e"]], []
+        for p in sorted(full[k], key=lambda p: -start[p]):
+            if ops[p]["e"] == "P" and o["e"] == "P":
+                continue
+            s, val = ops[p]["sig"]
+            if kn.get(s, 0) < val:
+                waits.append((s, val))
+                kn[s] = val
+                for s2, v2 in ops[p]["kn"].items():
+                    kn[s2] = max(kn.get(s2, 0), v2)
+        o["waits"], o["kn"] = waits, dict(kn)
+        if o["kind"] == "c":
+            count[o["e"]] += 1
+            o["sig"] = ("c" + o["e"], count[o["e"]])
+        elif o["kind"] == "d":
+            o["sig"] = ("dm%d" % nd, 16)
+            nd += 1
+        else:
+            o["sig"], o["kn"] = ("ar%d" % o["k"], NENG), {}
+    last = [("c" + e, count[e]) for e in "DAPG"] + [("dm%d" % k, 16) for k in range(nd)]
+    last += [("ar%d" % k, NENG) for k in range(4)] + [("lc", 4 * NENG)]
+    return dict(ops=ops, order=order, last=last, start=start, end=end, best=best[2:])
+
+
+PLAN = {}
+
+
+def rank_program(g, core, T, topo):
+    rank = T.rank_of(core)
+    if rank is None:
+        return
+    if not PLAN:
+        PLAN.update(plan())
+    q = {"D": g.vector, "A": g.scalar, "P": g.tensor, "G": g, "S": g.sync}
+    x = dict(rank=rank, core=core, topo=topo)
+    for k in PLAN["order"]:
+        o = PLAN["ops"][k]
+        for s, val in o["waits"]:
+            q[o["e"]].wait_ge(T.sem[s], val)
+        ins = o["fn"](g, T, x)
+        if o["kind"] == "c":
+            ins.then_inc(T.sem[o["sig"][0]], 1)
+        elif o["kind"] == "d":
+            ins.then_inc(T.sem[o["sig"][0]], 16)
+    for s, val in PLAN["last"]:
+        g.wait_ge(T.sem[s], val)

@@ -3,17 +3,17 @@ from concourse.mybir import AluOpType as OP, AxisListType, ActivationFunctionTyp
 
 N = 8
 NP, NHD = 3072, 2048
-N3 = 44
-C1 = 28
-C3 = 22
-REPA = 6
+N3 = 52
+C1 = 38
+C3 = 26
+REPA = 4
 NENG = 8
 F, B, H, I, U = "float32", "bfloat16", "float16", "int32", "uint16"
 SB = {
     "X": (NP + 96, B), "Li": (NHD, I), "L": (NHD + 1280, F), "Lo": (NHD, F), "W": (NP + 1024, F), "V": (NHD + 1280, F),
     "wi": (192, I), "wc": (192, H), "hoi": (32, I), "hou": (32, U), "dem": (544, B),
     "ones": (256, B), "idn": (128, B), "nidn": (128, B), "bo": (128, B), "boh": (128, H),
-    "nboh": (128, H), "bob": (128, B), "sel": (8, B), "Q": (144, B), "ST": (2048, H),
+    "nboh": (128, H), "bk": (256, B), "bob": (128, B), "sel": (8, B), "Q": (144, B), "ST": (2048, H),
     "pi": (4, I), "pf": (8, F), "ar": (256, F), "oh16": (16, F), "cse": (128, B),
     "csh": (128, H), "rst": (128, F), "jrow": (128, B), "p0": (128, B), "ii": (64, I), "cu": (64, U),
     "wr32": (256, F), "wrb": (256, B), "nthr": (256, B), "wC": (16, F), "dL": (80, F), "dW": (64, F), "K1": (64, F),
@@ -27,7 +27,7 @@ SB = {
     "ed": (64, F), "e0d": (64, F), "uph": (16, H), "prb": (256, B), "jk": (768, B), "ac": (4, F), "uo": (32, U),
     "rd": (4, F), "rb": (4, B), "ri": (4, I),
     "rq0": (144, F), "rq1": (144, F), "lq0": (144, F), "lq1": (144, F), "rs0": (48, B), "rs1": (48, B),
-    "ls0": (48, B), "ls1": (48, B), "xs0": (48, B), "y1": (48, F), "y2": (48, F), "y3": (48, F), "y5": (48, F),
+    "ls0": (48, B), "ls1": (48, B), "xs0": (48, B), "y1": (48, F), "y2": (48, F), "y3": (48, F),
     "e0c": (4, F), "fC": (4, F), "z1": (4, F), "z2": (4, F), "z3": (4, F), "dx": (48, B), "fr": (48, F),
     "b1": (48, B), "b2": (48, B), "b3": (48, B), "E2": (288, B),
 }
@@ -38,12 +38,15 @@ for _k in PS:
 NDMA = 11
 SEMAPHORES = ["cD", "cA", "cP", "cG"] + ["dm%d" % k for k in range(NDMA)] + ["ar%d" % k for k in range(4)] + ["lc"]
 SIZE = {F: 4, I: 4, B: 2, H: 2, U: 2}
-COSTS = [dict(cyc=1.0, g=1.56, sc=3.8, pe=0.6, hop=90.0, rem=3000.0), dict(cyc=1.0, g=1.1, sc=2.0, pe=0.9, hop=150.0, rem=4000.0),
-         dict(cyc=1.0, g=2.0, sc=5.5, pe=0.45, hop=60.0, rem=2500.0)]
+COSTS = [dict(cyc=0.9, g=1.56, sc=3.8, pe=0.55, hop=150.0, rem=5000.0, fix=25.0, pfix=8.0),
+         dict(cyc=0.83, g=1.56, sc=3.8, pe=0.42, hop=250.0, rem=4000.0, fix=0.0, pfix=0.0),
+         dict(cyc=0.9, g=1.3, sc=2.5, pe=0.9, hop=100.0, rem=4000.0, fix=0.0, pfix=0.0),
+         dict(cyc=0.83, g=1.56, sc=3.8, pe=0.42, hop=100.0, rem=4000.0, fix=50.0, pfix=0.0),
+         dict(cyc=1.0, g=2.0, sc=5.5, pe=0.55, hop=120.0, rem=5000.0, fix=20.0, pfix=8.0)]
 RND = 1.5 * 2 ** 23
 NLOAD = 7
 BIAS = {"send": 5000.0, "came": 5000.0}
-TRIES, SEED, WIN = 2500, 1, 0.3
+TRIES, SEED, WIN = 4000, 1, 0.3
 
 
 def v(name, lo=0, hi=None, step=1, p=None):
@@ -90,7 +93,7 @@ def program(c):
     def add(eng, fn, out, ins, cost, lat=0.0, kind="c", extra=()):
         W = [out[1]] if out[0] == "I" else [out]
         R = regs(*ins) + ([out[2]] if out[0] == "I" else [])
-        ops.append(dict(e=eng, fn=fn, R=R, W=W + list(extra), cost=cost, lat=lat, kind=kind, tag=tuple(tag)))
+        ops.append(dict(e=eng, fn=fn, R=R, W=W + list(extra), cost=cost + c["fix"] * (eng in "DA"), lat=lat, kind=kind, tag=tuple(tag)))
 
     def vcost(out, in0, others, two=False, fix=50.0):
         n = cnt(out)
@@ -142,7 +145,7 @@ def program(c):
             for o, l, r, st, sp in lst:
                 ins = g.tensor.matmul(ap(T, o), ap(T, l), ap(T, r), st, sp)
             return ins
-        k = sum(max(min(64, cnt(l)), cnt(r)) for o, l, r, st, sp in lst) * c["pe"]
+        k = sum(max(min(64, cnt(l)), cnt(r)) * c["pe"] + c["pfix"] for o, l, r, st, sp in lst)
         add("P", fn, lst[0][0], [l for o, l, r, st, sp in lst] + [r for o, l, r, st, sp in lst], k, lat=60.0,
             extra=[o for o, l, r, st, sp in lst[1:]])
 
@@ -214,6 +217,8 @@ def program(c):
     ts(v("nidn"), v("idn"), -1.0, OP.mult)
     ts(v("nboh"), v("bo"), -1.0, OP.mult)
     ts(v("bob"), v("bo"), 2.0 ** 55, OP.mult, 2.0 ** 55, OP.mult)
+    for k in (1, 2):
+        ts(v("bk", 128 * k - 128, 128 * k), v("bo"), 1.7 ** (-16 * k), OP.mult)
     cp(v("sel"), v("bo", 0, 128, 16))
     ms(v("Q"), 0.0)
     cp(v("Q", 15, 143, 16), v("bo", 0, 128, 16))
@@ -300,13 +305,17 @@ def program(c):
         cp(v("oL", 0, 16), v("hoi", 16 * t, 16 * t + 16))
         act(ind(v("V"), h0), mark, AF.Silu, more=1300.0 if t == 0 else 0.0)
         ts(v("OH", 0, 256), v("ones"), v("oh16", t, t + 1), OP.mult)
-        act(v("Lg", 0, 256), ind(Lw, h0), AF.Copy)
+        if t == 0:
+            ts(v("Lg", 0, 256), ind(v("Li"), h0), -1024.0, OP.add)
+        else:
+            act(v("Lg", 0, 256), ind(Lw, h0), AF.Copy)
         ts(v("em", 0, 256), v("Lg", 0, 256), v("oh16", t, t + 1), OP.mult)
         for hf in range(2):
             after_e(t, 0, hf)
         ts(v("eC", 0, 16), v("es", 15, 256, 16), fixe, OP.add)
-        for j in range(16):
-            o, a = v("xr", j, 4096, 16), v("x0", 0, 256)
+        for j in range(32):
+            hf, j = j // 16, j % 16
+            o, a = v("xr", 2048 * hf + j, 2048 * hf + 2048, 16), v("x0", 128 * hf, 128 * hf + 128)
             if j < REPA:
                 act(o, a, AF.Copy)
             else:
@@ -352,7 +361,7 @@ def program(c):
                 ho = v("hoff", q + 8 * hf, q + 8 * hf + 8)
                 lg = v("Lg", 256 * i + o, 256 * i + o + 128)
                 act(lg, ind(Lw, ho), AF.Copy)
-                ts(v("Lu", o, o + 128), lg, 1024.0, OP.add)
+                ts(v("Lu", o, o + 128), ind(Lw, ho), 1024.0, OP.add)
                 c3 = chunks(0, N3, C3) if hf == 0 else chunks(256 - N3, 256, C3)
                 c1 = chunks(N3, 128, C1) if hf == 0 else chunks(128, 256 - N3, C1)
                 for a, b in c3:
@@ -471,26 +480,26 @@ def program(c):
         mm([(v("pk1", 0, 48), v("bo"), v("b1"), True, True)])
         scan(v("y2"), v("csh", 0, 48), v("pk1", 0, 48), 0.0, OP.add, OP.min)
         ts(v("b2"), v("pk1", 0, 48), need, OP.is_lt)
-        ts(v("z2", 0, 3), v("y2", 15, 48, 16), fixh, OP.add, need, OP.is_ge)
+        ts(v("pf", 5, 6), fixh, -1.0, OP.mult, need, OP.add)
         lst = [(v("pc", 0, 48), v("idn"), v("nthr", 0, 48), True, False)]
         for k in range(3):
             ts(v("E2", 48 * k, 48 * k + 48), v("fr"), v("e0c", k, k + 1), OP.is_equal)
             lst.append((v("pc", 0, 48), v("bob"), v("E2", 48 * k, 48 * k + 48), False, False))
         lst.append((v("pc", 0, 48), v("bob"), v("b2"), False, False))
         mm(lst)
-        tt(v("z3", 0, 3), v("z2", 0, 3), v("wC", 0, 3), OP.mult)
+        ts(v("z3", 0, 3), v("y2", 15, 48, 16), v("pf", 5, 6), OP.is_ge, v("wC", 0, 1), OP.mult)
         lst = []
         for k in (2, 1, 0):
             o = 144 + 48 * k
             ts(v("E2", o, o + 48 - 16 * k), v("fr", 16 * k, 48), v("fC", k, k + 1), OP.is_equal, v("z3", k, k + 1), OP.mult)
-            lst.append((v("pc", 16 * k, 48), v("bo"), v("E2", o, o + 48 - 16 * k), False, k == 0))
+            lst.append((v("pc", 16 * k, 48), v("bk", 128 * k - 128, 128 * k) if k else v("bo"), v("E2", o, o + 48 - 16 * k), False, k == 0))
         mm(lst)
         ts(v("b3"), v("pc", 0, 48), 0.0, OP.is_lt)
         tt(v(rs), v("dx"), v("b3"), OP.mult)
         send(2 * t + 1, v(ls), v(rs), -(t + 1))
-        scan(v("y5"), v("csh", 0, 48), v("b3"), 0.0, OP.add, OP.min)
+        scan(v("y1"), v("csh", 0, 48), v("b3"), 0.0, OP.add, OP.min)
         tt(v("z2", 0, 3), v("fC", 0, 3), v("dX", 3, 6), OP.subtract)
-        ts(v("z3", 0, 3), v("y5", 15, 48, 16), fixh, OP.add)
+        ts(v("z3", 0, 3), v("y1", 15, 48, 16), fixh, OP.add)
         tt(v("z3", 0, 3), v("z3", 0, 3), v("z2", 0, 3), OP.mult)
         tt(v("z2", 0, 3), v("z3", 0, 3), v("dX", 3, 6), OP.add)
         fo2 = v("uo", 16, 19)

@@ -3,9 +3,9 @@ from concourse.mybir import AluOpType as OP, AxisListType, ActivationFunctionTyp
 
 N = 8
 NP, NHD = 3072, 2048
-N3 = 52
-C1 = 38
-C3 = 26
+N3 = 56
+C1 = 36
+C3 = 28
 REPA = 4
 NENG = 8
 F, B, H, I, U = "float32", "bfloat16", "float16", "int32", "uint16"
@@ -19,10 +19,10 @@ SB = {
     "wr32": (256, F), "wrb": (256, B), "nthr": (256, B), "wC": (16, F), "dL": (80, F), "dW": (64, F), "K1": (64, F),
     "K2": (64, F), "dX": (12, F), "mk": (512, F), "need": (2, F),
     "hoff": (80, U), "Lu": (256, U), "Lg": (1280, F), "dd": (4096, B), "da": (4096, B), "h32": (1024, F), "ag": (1024, B),
-    "x0": (272, B), "xr": (4096, B), "pm": (256, F), "mn": (16, F), "st0": (144, B), "st1": (144, B), "OH": (1280, B),
-    "em": (1280, H), "es": (1280, F), "eoff": (80, U), "eC": (80, F), "hr": (1024, H), "hs": (1024, H), "hC": (80, F),
+    "x0": (272, B), "xr": (4096, B), "pm": (256, F), "mn": (256, F), "st0": (144, B), "st1": (144, B), "OH": (1280, B),
+    "em": (1280, H), "es": (1280, F), "eoff": (80, U), "eC": (80, F), "hr": (1024, H), "hs": (1024, F), "hC": (80, F),
     "E0": (272, F), "H5": (272, F), "Tv": (2064, F), "E": (2176, B), "vg": (512, B), "sg": (1024, B), "fl": (64, F),
-    "up": (16, F), "sv": (80, F), "pd": (80, F), "gt": (80, F), "wu": (16, F), "s1": (80, F), "s2": (80, F),
+    "up": (16, F), "sv": (80, F), "pd": (80, F), "gt": (128, F), "wu": (16, F), "s1": (80, F), "s2": (80, F),
     "s3": (240, F), "s4": (80, F), "s5": (80, F), "s6": (80, F), "oL": (80, U), "oT": (80, U), "oW": (64, U), "tl": (1280, F),
     "ed": (64, F), "e0d": (64, F), "uph": (16, H), "prb": (256, B), "jk": (768, B), "ac": (4, F), "uo": (32, U),
     "rd": (4, F), "rb": (4, B), "ri": (4, I),
@@ -38,15 +38,14 @@ for _k in PS:
 NDMA = 11
 SEMAPHORES = ["cD", "cA", "cP", "cG"] + ["dm%d" % k for k in range(NDMA)] + ["ar%d" % k for k in range(4)] + ["lc"]
 SIZE = {F: 4, I: 4, B: 2, H: 2, U: 2}
-COSTS = [dict(cyc=0.9, g=1.56, sc=3.8, pe=0.55, hop=150.0, rem=5000.0, fix=25.0, pfix=8.0),
-         dict(cyc=0.83, g=1.56, sc=3.8, pe=0.42, hop=250.0, rem=4000.0, fix=0.0, pfix=0.0),
-         dict(cyc=0.9, g=1.3, sc=2.5, pe=0.9, hop=100.0, rem=4000.0, fix=0.0, pfix=0.0),
-         dict(cyc=0.83, g=1.56, sc=3.8, pe=0.42, hop=100.0, rem=4000.0, fix=50.0, pfix=0.0),
-         dict(cyc=1.0, g=2.0, sc=5.5, pe=0.55, hop=120.0, rem=5000.0, fix=20.0, pfix=8.0)]
+COSTS = [dict(cyc=0.83, g=1.56, sc=3.8, pe=0.5, hop=200.0, rem=4000.0, fix=10.0, pfix=4.0),
+         dict(cyc=0.83, g=1.3, sc=2.5, pe=0.42, hop=260.0, rem=4000.0, fix=0.0, pfix=0.0),
+         dict(cyc=0.9, g=1.56, sc=3.8, pe=0.7, hop=150.0, rem=5000.0, fix=25.0, pfix=0.0),
+         dict(cyc=1.1, g=1.9, sc=5.0, pe=0.6, hop=220.0, rem=5000.0, fix=10.0, pfix=4.0)]
 RND = 1.5 * 2 ** 23
 NLOAD = 7
 BIAS = {"send": 5000.0, "came": 5000.0}
-TRIES, SEED, WIN = 4000, 1, 0.3
+TRIES, SEED, WIN = 5000, 1, 0.3
 
 
 def v(name, lo=0, hi=None, step=1, p=None):
@@ -185,11 +184,12 @@ def program(c):
     asel(v("idn"), v("ones", 0, 128), [[-1, 128]], OP.is_equal, 0, 1)
     iota(v("pi", 0, 1), [[0, 1]], 0, 1)
     iota(v("ar"), [[0, 16], [1, 16]], 0, 0)
+    iota(v("ii", 0, 8), [[16, 8]], 15, 0)
     iota(v("ii", 8, 56), [[1, 48]], 0, 0)
     iota(v("s1"), [[16, 80]], 0, 0)
     iota(v("s2", 0, 64), [[512, 4], [16, 16]], -2048, 0)
     ts(v("pi", 1, 2), v("pi", 0, 1), 15, OP.bitwise_and)
-    pa, pa1, fixe, fixh = v("pf", 0, 1), v("pf", 1, 2), v("pf", 2, 3), v("pf", 3, 4)
+    pa, pa1, fixe, fixh, fixr = v("pf", 0, 1), v("pf", 1, 2), v("pf", 2, 3), v("pf", 3, 4), v("pf", 6, 7)
     cp(pa, v("pi", 1, 2))
     ts(v("oh16"), v("ar", 0, 16), pa, OP.is_equal)
     cp(v("boh"), v("bo"))
@@ -206,6 +206,7 @@ def program(c):
     tt(pa1, pa, v("pf", 4, 5), OP.add)
     ts(fixe, v("oh16", 15, 16), -4096.0, OP.mult, 5120.0, OP.add)
     ts(fixh, v("oh16", 15, 16), -2048.0, OP.mult, 2048.0, OP.add)
+    ts(fixr, fixe, RND - 1056.0, OP.add)
     ts(v("pm", 0, 128), v("ar", 0, 128), pa, OP.is_equal, 8192.0, OP.mult)
     ts(v("es", 0, 128), v("ar", 0, 128), pa1, OP.is_equal, -2048.0, OP.mult)
     tt(v("pm", 128, 256), v("pm", 0, 128), v("es", 0, 128), OP.add)
@@ -222,7 +223,7 @@ def program(c):
     cp(v("sel"), v("bo", 0, 128, 16))
     ms(v("Q"), 0.0)
     cp(v("Q", 15, 143, 16), v("bo", 0, 128, 16))
-    cp(v("cu", 8, 56), v("ii", 8, 56))
+    cp(v("cu", 0, 56), v("ii", 0, 56))
     ms(v("mk", 0, 256), 1.0)
     ms(v("mk", 256, 512), 20.0)
     ms(v("es", 256, 512), 1.0 / 1.7)
@@ -255,6 +256,7 @@ def program(c):
     ms(v("st0", 0, 16), 1.0)
     ms(v("st1", 0, 16), 1.0)
     ms(v("gt", 64, 80), 0.0)
+    ms(v("s4", 64, 80), 0.0)
 
     Xw, Lw, Ww = v("X", 0, NP), v("L", 0, NHD), v("W", 0, NP)
     one1 = v("ones", 0, 128, 1, (0, 1))
@@ -265,9 +267,9 @@ def program(c):
         mm([jr + (True, False)])
         mm([(v(pk, j, 128, 16, (0, ns)), v("da", base + j, base + 16 * ns, 16), v("sel"), False, False) for j in range(16)] + [jr + (False, True)])
         scan(pmv, v("rst"), v(pk, 0, 128), 0.0, OP.add, OP.min)
-        mn = v("mn", pmv[1] // 16, pmv[1] // 16 + 8)
-        cp(mn, v("pm", pmv[1] + 15, pmv[2], 16))
-        tt(v(st, 16, 144), ind(mn, rep48(0, 8)), pmv, OP.is_equal)
+        mn = v("mn", pmv[1], pmv[2])
+        scan(mn, v("rst"), v(pk, 0, 128), 0.0, OP.add, OP.min)
+        tt(v(st, 16, 144), ind(mn, v("cu", 0, 8)), pmv, OP.is_equal)
         mm([(v(pk, 128, 128 + ns), v("p0", 0, 128, 1, (0, 1)), v("ones", 0, ns, 1, (0, 1)), True, False),
             (v(pk, 128, 128 + ns), v(st, 16, 144, 1, (0, ns)), v("idn", 0, ns, 1, (0, ns)), False, False),
             (v(pk, 128, 128 + ns), v(st, 15, 143, 1, (0, ns)), v("nidn", 0, ns, 1, (0, ns)), False, True)])
@@ -281,8 +283,8 @@ def program(c):
         if i < 4:
             act(v("h32", o, o + 128), ind(Ww, eo), AF.Copy)
             ts(v("hr", o, o + 128), v("h32", o, o + 128), RND - 32.0, OP.add, -RND, OP.add)
-            scan(v("hs", o, o + 128), v("csh"), v("hr", o, o + 128), 0.0, OP.add, OP.min)
-            ts(v("hoff", oc + 16, oc + 24), v("hs", o + 15, o + 128, 16), fixh, OP.add)
+            scan(v("hs", o, o + 128), v("cse"), v("h32", o, o + 128), 0.0, OP.add, OP.min)
+            ts(v("hoff", oc + 16, oc + 24), v("hs", o + 15, o + 128, 16), fixr, OP.add, -RND, OP.add)
         else:
             act(v("H5", 128 * hf, 128 * hf + 128), ind(Ww, eo), AF.Identity, bias=-32.0)
         if i == 0:
@@ -325,7 +327,7 @@ def program(c):
             tag[:] = ["death", 10 * t + i]
             hC, sv, dl, ol, pdi, eC = [v(nm, q, q + 16) for nm in ("hC", "sv", "dL", "oL", "pd", "eC")]
             so, fo, vg = 512 * (i % 2), 32 * (i % 2), v("vg", 256 * (i % 2), 256 * (i % 2) + 256)
-            ts(hC, v("hs", 256 * i - 241, 256 * i, 16), fixh, OP.add)
+            ts(hC, v("hs", 256 * i - 241, 256 * i, 16), fixr, OP.add, -RND, OP.add)
             act(vg, ind(v("V", 0, NHD), v("hoff", q, q + 16)), AF.Relu, bias=-0.25 - 0.75 * t)
             lst, o = [], 0
             for cc in range(16):
@@ -419,26 +421,32 @@ def program(c):
         eo0 = v("uo", 4, 7)
         cp(eo0, v("z1", 0, 3))
         tag[0] = "payl"
-        cp(v("gt", 48, 64), v("pd", 64, 80))
-        for i in (2, 1, 0):
-            tt(v("gt", 16 * i, 16 * i + 16), v("gt", 16 * i + 16, 16 * i + 32), v("pd", 16 * i + 16, 16 * i + 32), OP.add)
-        tt(v("s4", 0, 64), v("gt", 0, 64), v("K1"), OP.mult)
-        ms(v("s4", 64, 80), 0.0)
-        tt(v("s5", 16, 80), v("pd", 16, 80), v("K2"), OP.mult)
-        tt(v("s4", 16, 80), v("s4", 16, 80), v("s5", 16, 80), OP.add)
-        ts(v("oT"), v("s4"), 2048.0, OP.add)
-        for a, b in ((0, 8), (8, 20), (20, 32), (32, 48), (48, 64), (64, 80)):
+        cp(v("gt", 112, 128), v("pd", 48, 64))
+        for i in (1, 0):
+            tt(v("gt", 80 + 16 * i, 96 + 16 * i), v("gt", 96 + 16 * i, 112 + 16 * i), v("pd", 16 * i + 16, 16 * i + 32), OP.add)
+        tt(v("s4", 0, 48), v("gt", 80, 128), v("K1", 0, 48), OP.mult)
+        ms(v("s4", 48, 64), 0.0)
+        tt(v("s5", 16, 64), v("pd", 16, 64), v("K2", 0, 48), OP.mult)
+        tt(v("s4", 16, 64), v("s4", 16, 64), v("s5", 16, 64), OP.add)
+        for i in range(5):
+            tt(v("s2", 16 * i, 16 * i + 16), v("pd", 64, 80), v("K1", 16 * i, 16 * i + 16) if i < 4 else v("K2", 48, 64), OP.mult)
+        tt(v("s1"), v("s4"), v("s2"), OP.add)
+        ts(v("oT"), v("s1"), 2048.0, OP.add)
+        for a, b in ((0, 10), (10, 30), (30, 54), (54, 80)):
             act(v("tl", 16 * a, 16 * b), ind(v("Tv"), v("oT", a, b)), AF.Copy)
             tt(ind(v("L"), v("oL", a, b)), v("Lg", 16 * a, 16 * b), v("tl", 16 * a, 16 * b), OP.add)
         tag[0] = "payw"
+        cp(v("gt", 48, 64), v("pd", 64, 80))
+        for i in range(3):
+            tt(v("gt", 16 * i, 16 * i + 16), v("gt", 80 + 16 * i, 96 + 16 * i), v("pd", 64, 80), OP.add)
         tt(v("ed"), v("eC", 16, 80), v("dW"), OP.subtract)
         tt(v("s5", 0, 64), v("gt", 16, 80), v("ed"), OP.mult)
         tt(v("s6", 0, 64), v("pd", 16, 80), v("e0d"), OP.mult)
         tt(v("s5", 0, 64), v("s5", 0, 64), v("s6", 0, 64), OP.add)
         tt(v("s6", 0, 64), v("s5", 0, 64), v("dW"), OP.add)
         cp(v("oW"), v("s6", 0, 64))
-        for k in range(8):
-            act(ind(v("W"), v("oW", 8 * k, 8 * k + 8)), v("h32", 128 * k, 128 * k + 128), AF.Silu)
+        for k in range(0, 64, 16):
+            act(ind(v("W"), v("oW", k, k + 16)), v("h32", 16 * k, 16 * k + 256), AF.Silu)
         if t == 0:
             add("D", lambda g, T, x: g.vector.tensor_reduce(ap(T, v("rd", 0, 1)), ap(T, v("gt", 0, 16)), AxisListType.X, OP.add),
                 v("rd", 0, 1), [v("gt", 0, 16)], 64.0)
@@ -607,8 +615,10 @@ def plan(tries=None):
                 m &= kind == kind[k]
             if u[1] < 0.7 or u[0] >= 0.5:
                 m &= part == part[k]
-            if u[2] < 0.7:
+            if u[2] < 0.55:
                 m &= step == step[k]
+            elif u[2] < 0.75:
+                m &= step % 10 == step[k] % 10
             off[m] += rng.normal() * (3000.0 if u[3] < 0.5 else 600.0)
         order, start, end = schedule(ops, deps, succ, COSTS[0]["hop"], WIN, off)
         if best is not None and end > best[2][0] * 1.01:

@@ -1,54 +1,54 @@
+import math
 import numpy as np
 from concourse.mybir import AluOpType as OP, AxisListType, ActivationFunctionType as AF
 
 N = 8
 NP, NHD = 3072, 2048
-N3 = 56
-C1 = 36
-C3 = 28
-REPA = 4
+PRM = dict(NC=32, NB=64, C1=32, C3=32, REPA=0, QC=16, SG4=2, LCH=(6, 6, 6, 6, 8, 48), WCH=16, CUT=(), SGA=0, WGA=0)
 NENG = 8
 F, B, H, I, U = "float32", "bfloat16", "float16", "int32", "uint16"
 SB = {
-    "X": (NP + 96, B), "Li": (NHD, I), "L": (NHD + 1280, F), "Lo": (NHD, F), "W": (NP + 1024, F), "V": (NHD + 1280, F),
-    "wi": (192, I), "wc": (192, H), "hoi": (32, I), "hou": (32, U), "dem": (544, B),
-    "ones": (256, B), "idn": (128, B), "nidn": (128, B), "bo": (128, B), "boh": (128, H),
-    "nboh": (128, H), "bk": (256, B), "bob": (128, B), "sel": (8, B), "Q": (144, B), "ST": (2048, H),
-    "pi": (4, I), "pf": (8, F), "ar": (256, F), "oh16": (16, F), "cse": (128, B),
-    "csh": (128, H), "rst": (128, F), "jrow": (128, B), "p0": (128, B), "ii": (64, I), "cu": (64, U),
-    "wr32": (256, F), "wrb": (256, B), "nthr": (256, B), "wC": (16, F), "dL": (80, F), "dW": (64, F), "K1": (64, F),
-    "K2": (64, F), "dX": (12, F), "mk": (512, F), "need": (2, F),
-    "hoff": (80, U), "Lu": (256, U), "Lg": (1280, F), "dd": (4096, B), "da": (4096, B), "h32": (1024, F), "ag": (1024, B),
-    "x0": (272, B), "xr": (4096, B), "pm": (256, F), "mn": (256, F), "st0": (144, B), "st1": (144, B), "OH": (1280, B),
-    "em": (1280, H), "es": (1280, F), "eoff": (80, U), "eC": (80, F), "hr": (1024, H), "hs": (1024, F), "hC": (80, F),
-    "E0": (272, F), "H5": (272, F), "Tv": (2064, F), "E": (2176, B), "vg": (512, B), "sg": (1024, B), "fl": (64, F),
-    "up": (16, F), "sv": (80, F), "pd": (80, F), "gt": (128, F), "wu": (16, F), "s1": (80, F), "s2": (80, F),
-    "s3": (240, F), "s4": (80, F), "s5": (80, F), "s6": (80, F), "oL": (80, U), "oT": (80, U), "oW": (64, U), "tl": (1280, F),
-    "ed": (64, F), "e0d": (64, F), "uph": (16, H), "prb": (256, B), "jk": (768, B), "ac": (4, F), "uo": (32, U),
-    "rd": (4, F), "rb": (4, B), "ri": (4, I),
-    "rq0": (144, F), "rq1": (144, F), "lq0": (144, F), "lq1": (144, F), "rs0": (48, B), "rs1": (48, B),
-    "ls0": (48, B), "ls1": (48, B), "xs0": (48, B), "y1": (48, F), "y2": (48, F), "y3": (48, F),
-    "e0c": (4, F), "fC": (4, F), "z1": (4, F), "z2": (4, F), "z3": (4, F), "dx": (48, B), "fr": (48, F),
-    "b1": (48, B), "b2": (48, B), "b3": (48, B), "E2": (288, B),
+    "X": (NP + 96, B), "Li": (NHD, I), "L": (NHD + 1280, F), "Lo": (NHD, F), "W": (NP + 1024, F), "V": (NHD + 1280, F), "IT": (NP, F),
+    "wi": (192, I), "wc": (192, H), "hoi": (32, I), "hou": (32, U), "xd0": (544, B), "xd1": (544, B), "lx0": (544, B), "lx1": (544, B),
+    "ones": (512, B), "idn": (128, B), "nidn": (128, B), "bo": (128, B), "boh": (128, H), "bk": (256, B), "bob": (128, B),
+    "sel": (16, B), "Q": (288, B), "ST": (2048, H), "pi": (4, I), "pf": (12, F), "ar": (256, F), "oh16": (16, F),
+    "ncse": (128, B), "mA": (144, B), "csh": (128, H), "rst": (128, F), "jrow": (128, B), "p0": (128, B), "qrow": (128, B),
+    "Dm": (256, H), "ih": (384, H), "ii": (72, I), "cu": (72, U), "r0": (288, B),
+    "wr32": (256, F), "wrb": (256, B), "nthr": (256, B), "wC": (32, F), "dL": (240, F), "dW": (128, F),
+    "dX": (12, F), "mk": (512, F), "need": (8, F),
+    "hoff": (80, U), "Lu": (256, U), "nL": (1280, H), "dd": (4096, B), "da": (4096, B), "h32": (1024, F), "ag": (1024, B),
+    "xr": (4096, B), "pm": (256, F), "u0": (260, B), "u1": (260, B), "zb": (512, F), "Mh": (256, H), "rr": (1040, B),
+    "es": (256, F), "eoff": (80, U), "ev": (144, H), "eF": (80, F), "hr": (1024, H), "hs": (1024, H), "hC": (80, F),
+    "E0": (272, F), "H5": (272, F), "E": (2176, B), "vg": (512, B), "sg": (1024, B), "fl": (64, F), "un": (64, H),
+    "sv": (64, F), "pd": (80, F), "gt": (80, F), "wu": (16, F), "s1": (80, F), "s2": (80, F), "s3": (80, F), "s4": (80, F),
+    "s5": (128, F), "s6": (128, F), "oL": (64, U), "oP": (80, U), "oW": (64, U), "t1": (1280, F), "t2": (1280, F),
+    "prb": (256, B), "jk": (768, B), "ac": (4, F), "uo": (32, U), "rb": (4, B), "ri": (4, I),
+    "rq0": (56, U), "rq1": (56, U), "lq0": (56, U), "lq1": (56, U), "rs0": (48, B), "rs1": (48, B),
+    "ls0": (48, B), "ls1": (48, B), "xs0": (48, B), "yh": (144, H), "y1": (48, F), "y2": (48, F), "y3": (48, F),
+    "zz": (20, F), "dx": (48, B), "fr": (48, F), "xq": (96, B), "bb": (144, B), "E2": (288, B),
 }
+PART = {"e0c": ("zz", 0, 4), "fC": ("zz", 4, 4), "z1": ("zz", 8, 4), "z2": ("zz", 12, 4), "z3": ("zz", 16, 4),
+        "b1": ("bb", 0, 48), "b2": ("bb", 48, 48), "b3": ("bb", 96, 48)}
 PS = ["pa", "pb", "pk0", "pk1", "pc", "pdd", "pm0", "pm1"]
 SCRATCH = {k: ("sbuf", [128, w], d) for k, (w, d) in SB.items()}
 for _k in PS:
     SCRATCH[_k] = ("psum", [128, 512], F)
-NDMA = 11
-SEMAPHORES = ["cD", "cA", "cP", "cG"] + ["dm%d" % k for k in range(NDMA)] + ["ar%d" % k for k in range(4)] + ["lc"]
+NDMA, NREM = 12, 6
+SEMAPHORES = ["cD", "cA", "cP", "cG"] + ["dm%d" % k for k in range(NDMA)] + ["ar%d" % k for k in range(NREM)] + ["lc"]
 SIZE = {F: 4, I: 4, B: 2, H: 2, U: 2}
-COSTS = [dict(cyc=0.83, g=1.56, sc=3.8, pe=0.5, hop=200.0, rem=4000.0, fix=10.0, pfix=4.0),
-         dict(cyc=0.83, g=1.3, sc=2.5, pe=0.42, hop=260.0, rem=4000.0, fix=0.0, pfix=0.0),
-         dict(cyc=0.9, g=1.56, sc=3.8, pe=0.7, hop=150.0, rem=5000.0, fix=25.0, pfix=0.0),
-         dict(cyc=1.1, g=1.9, sc=5.0, pe=0.6, hop=220.0, rem=5000.0, fix=10.0, pfix=4.0)]
+COSTS = [dict(cyc=0.83, g=1.56, sc=3.8, pe=0.45, hop=200.0, rem=3000.0, fix=10.0, pfix=4.0, bw=200.0),
+         dict(cyc=0.83, g=1.3, sc=2.5, pe=0.42, hop=260.0, rem=2500.0, fix=0.0, pfix=0.0, bw=350.0),
+         dict(cyc=0.9, g=1.56, sc=3.8, pe=0.5, hop=150.0, rem=2000.0, fix=25.0, pfix=0.0, bw=300.0),
+         dict(cyc=1.1, g=1.9, sc=5.0, pe=0.6, hop=220.0, rem=4000.0, fix=10.0, pfix=4.0, bw=200.0)]
 RND = 1.5 * 2 ** 23
 NLOAD = 7
-BIAS = {"send": 5000.0, "came": 5000.0}
-TRIES, SEED, WIN = 5000, 1, 0.3
+TRIES, SEED, TEMP = 30000, 1, 8.0
 
 
 def v(name, lo=0, hi=None, step=1, p=None):
+    if name in PART:
+        name, o, w = PART[name]
+        return (name, o + lo, o + (w if hi is None else hi), step, p)
     if hi is None:
         hi = SB[name][0] if name in SB else 512
     return (name, lo, hi, step, p)
@@ -64,6 +64,8 @@ def ap(T, x):
     if x[0] == "I":
         return ap(T, x[1]).indirect(ap(T, x[2]))
     name, lo, hi, step, p = x
+    if p == "back":
+        return T[name][:, lo + (cnt(x) - 1) * step:lo - 1:-step]
     ps = slice(None) if p is None else slice(*p)
     return T[name][ps, lo:hi:step] if step > 1 else T[name][ps, lo:hi]
 
@@ -88,6 +90,7 @@ def regs(*xs):
 
 def program(c):
     ops, tag = [], ["", 0]
+    NC, NB = PRM["NC"], PRM["NB"]
 
     def add(eng, fn, out, ins, cost, lat=0.0, kind="c", extra=()):
         W = [out[1]] if out[0] == "I" else [out]
@@ -144,7 +147,7 @@ def program(c):
             for o, l, r, st, sp in lst:
                 ins = g.tensor.matmul(ap(T, o), ap(T, l), ap(T, r), st, sp)
             return ins
-        k = sum(max(min(64, cnt(l)), cnt(r)) * c["pe"] + c["pfix"] for o, l, r, st, sp in lst)
+        k = sum(max(min(64, cnt(l)), cnt(r)) * c["pe"] * (4 if wide(l) else 1) + c["pfix"] for o, l, r, st, sp in lst)
         add("P", fn, lst[0][0], [l for o, l, r, st, sp in lst] + [r for o, l, r, st, sp in lst], k, lat=60.0,
             extra=[o for o, l, r, st, sp in lst[1:]])
 
@@ -162,13 +165,13 @@ def program(c):
         add(q, lambda g, T, x: (g.sync if q == "S" else g.scalar).dma_start(dst(T), ap(T, a)), ("out%d" % len(ops), 0, 1, 1, None), [a],
             60.0, lat=nbytes, kind="d")
 
-    def send(k, out, a, shift):
+    def send(k, out, a, shift, more=0.0):
         def fn(g, T, x):
             dst = T.cores[(x["rank"] + shift) % N]
             rid, pid, _ = x["topo"].addr(dst)
             m = sum(1 << e for e in x["topo"].engines(x["core"], dst)[:NENG])
             return g.remote_dma(ap(T, out), ap(T, a), T.sem["ar%d" % k], T.sem.lc, pid, rid, m)
-        add("G", fn, out, [a], 300.0, lat=c["rem"], kind="r")
+        add("G", fn, out, [a], 300.0, lat=c["rem"] + more, kind="r")
         ops[-1]["k"] = k
 
     load("S", v("wi"), lambda T: T.wr[:], 98e3)
@@ -176,20 +179,20 @@ def program(c):
     load("S", v("Li", 0, 1024), lambda T: T.hl[:, 0:1024], 524e3)
     load("A", v("Li", 1024, 2048), lambda T: T.hl[:, 1024:2048], 524e3)
     load("S", v("X", 0, NP), lambda T: T.xs[:], 786e3)
-    load("S", v("dem", 0, 256), lambda T: T.dm[:, 0:256], 65e3)
-    load("S", v("dem", 272, 528), lambda T: T.dm[:, 256:512], 65e3)
+    load("S", v("xd0", 272, 528), lambda T: T.dm[:, 0:256], 65e3)
+    load("S", v("xd1", 272, 528), lambda T: T.dm[:, 256:512], 65e3)
     ms(v("ones"), 1.0)
     asel(v("jk", 0, 128), v("ones", 0, 128), [[-16, 8], [0, 16]], OP.is_ge, 0, 1)
     asel(v("bo"), v("jk", 0, 128), [[16, 8], [0, 16]], OP.is_ge, 15, -1)
     asel(v("idn"), v("ones", 0, 128), [[-1, 128]], OP.is_equal, 0, 1)
+    asel(v("jk", 128, 256), v("ones", 0, 128), [[-1, 128]], OP.is_equal, 1, 1)
     iota(v("pi", 0, 1), [[0, 1]], 0, 1)
     iota(v("ar"), [[0, 16], [1, 16]], 0, 0)
-    iota(v("ii", 0, 8), [[16, 8]], 15, 0)
+    iota(v("ii", 0, 8), [[32, 8]], 31, 0)
     iota(v("ii", 8, 56), [[1, 48]], 0, 0)
     iota(v("s1"), [[16, 80]], 0, 0)
-    iota(v("s2", 0, 64), [[512, 4], [16, 16]], -2048, 0)
     ts(v("pi", 1, 2), v("pi", 0, 1), 15, OP.bitwise_and)
-    pa, pa1, fixe, fixh, fixr = v("pf", 0, 1), v("pf", 1, 2), v("pf", 2, 3), v("pf", 3, 4), v("pf", 6, 7)
+    pa, ncpc, fixe, fixh, cpc, thr = [v("pf", k, k + 1) for k in (0, 1, 2, 3, 6, 7)]
     cp(pa, v("pi", 1, 2))
     ts(v("oh16"), v("ar", 0, 16), pa, OP.is_equal)
     cp(v("boh"), v("bo"))
@@ -202,132 +205,188 @@ def program(c):
     cp(v("hou"), v("hoi"))
     for k in range(2):
         ts(v("L", 1024 * k, 1024 * k + 1024), v("Li", 1024 * k, 1024 * k + 1024), -1024.0, OP.add)
-    ts(v("pf", 4, 5), v("oh16", 15, 16), -16.0, OP.mult, 1.0, OP.add)
-    tt(pa1, pa, v("pf", 4, 5), OP.add)
-    ts(fixe, v("oh16", 15, 16), -4096.0, OP.mult, 5120.0, OP.add)
-    ts(fixh, v("oh16", 15, 16), -2048.0, OP.mult, 2048.0, OP.add)
-    ts(fixr, fixe, RND - 1056.0, OP.add)
-    ts(v("pm", 0, 128), v("ar", 0, 128), pa, OP.is_equal, 8192.0, OP.mult)
-    ts(v("es", 0, 128), v("ar", 0, 128), pa1, OP.is_equal, -2048.0, OP.mult)
-    tt(v("pm", 128, 256), v("pm", 0, 128), v("es", 0, 128), OP.add)
-    cp(v("csh"), v("pm", 128, 256))
-    tt(v("cse"), v("pm", 128, 256), v("es", 0, 128), OP.add)
-    ts(v("rst"), v("ar", 0, 128), 0.0, OP.is_equal, 8192.0, OP.mult)
-    ts(v("p0"), v("ar", 0, 128), 0.0, OP.is_equal)
-    ts(v("jrow"), v("ar", 0, 128), 1.0 / 32, OP.mult)
-    ts(v("nidn"), v("idn"), -1.0, OP.mult)
-    ts(v("nboh"), v("bo"), -1.0, OP.mult)
+
+
+    def lin(out, a, scale, bias=None):
+        act(out, a, AF.Copy if bias is None else AF.Identity, bias=bias, scale=scale)
+
+    def fill(out, val):
+        lin(out, v("ones", 0, cnt(out)), val)
+
+    lin(fixe, v("oh16", 15, 16), -4096.0, 5120.0)
+    lin(fixh, v("oh16", 15, 16), -2048.0, 2048.0)
+    lin(cpc, v("oh16", 15, 16), -16.0, 96.0)
+    lin(ncpc, v("oh16", 15, 16), 16.0, -96.0)
+    lin(thr, v("oh16", 15, 16), 16.0, -72.0)
+    ts(v("mA"), v("ar", 0, 144), pa, OP.is_equal)
+    for k, f in enumerate((8192.0, 2048.0, 4096.0)):
+        lin(v("jk", 256 + 144 * k, 400 + 144 * k), v("mA"), f)
+    tt(v("csh"), v("jk", 272, 400), v("jk", 415, 543), OP.subtract)
+    tt(v("ncse"), v("jk", 559, 687), v("jk", 272, 400), OP.subtract)
+    fill(v("r0", 0, 144), 8192.0)
+    asel(v("r0", 144, 288), v("r0", 0, 144), [[0, 9], [1, 16]], OP.is_ge, -1, 0)
+    asel(v("p0"), v("r0", 0, 128), [[0, 8], [1, 16]], OP.is_equal, 0, 0)
+    lin(v("rst"), v("p0"), 1.0)
+    lin(v("qrow"), v("p0"), 0.5, -3072.0)
+    lin(v("jrow"), v("ar", 0, 128), 1.0 / 32)
+    lin(v("nidn"), v("idn"), -1.0)
+    for k, f in enumerate((1.0 / 128, 1.0, -1.0)):
+        ts(v("ih", 128 * k, 128 * k + 128), v("idn"), f, OP.mult)
+    ms(v("Dm"), 0.0)
+    tt(v("Dm", 0, 256, 2), v("idn"), v("jk", 128, 256), OP.subtract)
+    cp(v("Dm", 31, 256, 32), v("nidn", 15, 128, 16))
     ts(v("bob"), v("bo"), 2.0 ** 55, OP.mult, 2.0 ** 55, OP.mult)
     for k in (1, 2):
-        ts(v("bk", 128 * k - 128, 128 * k), v("bo"), 1.7 ** (-16 * k), OP.mult)
-    cp(v("sel"), v("bo", 0, 128, 16))
-    ms(v("Q"), 0.0)
-    cp(v("Q", 15, 143, 16), v("bo", 0, 128, 16))
+        lin(v("bk", 128 * k - 128, 128 * k), v("bo"), 1.7 ** (-16 * k))
+    lin(v("sel", 0, 8), v("bo", 0, 128, 16), 1.0)
+    lin(v("sel", 8, 16), v("bo", 0, 128, 16), -1.0)
+    fill(v("Q"), 0.0)
+    lin(v("Q", 15, 143, 16), v("bo", 0, 128, 16), 1.0)
+    lin(v("Q", 159, 287, 16), v("bo", 0, 128, 16), -1.0)
     cp(v("cu", 0, 56), v("ii", 0, 56))
-    ms(v("mk", 0, 256), 1.0)
-    ms(v("mk", 256, 512), 20.0)
-    ms(v("es", 256, 512), 1.0 / 1.7)
-    scan(v("wr32"), v("es", 256, 512), v("mk", 0, 256), 1.7 ** 129, OP.mult, OP.mult)
-    cp(v("wrb"), v("wr32"))
-    ts(v("nthr"), v("wrb"), -2.56, OP.mult)
+    ts(v("cu", 56, 62), v("ar", 0, 96, 16), pa, OP.add)
+    fill(v("mk", 0, 256), 1.0)
+    fill(v("mk", 256, 512), 20.0)
+    fill(v("t1", 0, 256), 1.0 / 1.7)
+    scan(v("wr32"), v("t1", 0, 256), v("mk", 0, 256), 1.7 ** 129, OP.mult, OP.mult)
+    lin(v("wrb"), v("wr32"), 1.0)
+    lin(v("nthr"), v("wrb"), -2.56)
 
-    def S(a):
-        return v("Q", 15 - a, 143 - a)
+    def S(a, neg=0):
+        return v("Q", 144 * neg + 15 - a, 144 * neg + 143 - a)
 
-    def rep48(lo, hi):
-        return v("cu", 8 + lo, 8 + hi)
+    def ST(a):
+        return v("ST", 128 * a, 128 * a + 128)
 
     mm([(v("pdd", 0, 16), S(a), v("wrb", a, 256, 16), a == 0, a == 15) for a in range(16)])
-    ts(v("wC"), v("pdd", 0, 16), 1.0 / 16, OP.mult)
-    ts(v("dL"), v("s1"), pa, OP.add, 2048.0, OP.add)
-    ts(v("dW"), v("s1", 0, 64), pa, OP.add, 3072.0, OP.add)
-    ts(v("K1"), v("s2", 0, 64), pa, OP.add)
-    ts(v("K2"), v("s2", 0, 64), pa, OP.add, 256.0, OP.add)
-    ts(v("dX", 0, 6), v("s1", 0, 6), pa, OP.add, 3072.0, OP.add)
-    ts(v("dX", 8, 11), v("dL", 0, 3), -1.0, OP.mult, 2047.5, OP.add)
+    lin(v("wC", 0, 16), v("pdd", 0, 16), 1.0 / 16)
+    lin(v("wC", 16, 32), v("pdd", 0, 16), -1.0 / 1024)
+    ts(v("dL", 0, 80), v("s1"), pa, OP.add, 2048.0, OP.add)
+    lin(v("dL", 80, 160), v("dL", 0, 80), 64.0)
+    lin(v("dL", 160, 240), v("dL", 0, 80), 1.0 / 128, ncpc)
+    lin(v("dW", 0, 64), v("dL", 0, 64), 1.0, 1024.0)
+    lin(v("dW", 64, 128), v("dL", 0, 64), 64.0, 65536.0)
+    lin(v("dX", 0, 6), v("dL", 0, 6), 1.0, 1024.0)
+    lin(v("dX", 8, 11), v("dL", 0, 3), -1.0, 2047.5)
     iota(v("V", 0, NHD), [[0, NHD]], 0, 0)
-    ms(v("need", 0, 1), 8.5)
-    ms(v("dem", 256, 272), 300.0)
-    ms(v("dem", 528, 544), 300.0)
-    ms(v("x0", 256, 272), 0.0)
-    ms(v("E0", 256, 272), 2500.0)
-    ms(v("H5", 256, 272), 0.0)
-    ms(v("Tv", 2048, 2064), 0.0)
-    ms(v("st0", 0, 16), 1.0)
-    ms(v("st1", 0, 16), 1.0)
-    ms(v("gt", 64, 80), 0.0)
-    ms(v("s4", 64, 80), 0.0)
+    iota(v("IT"), [[1, NP]], 0, 0)
+    fill(v("need", 0, 1), 8.5)
+    fill(v("need", 2, 3), 88.5)
+    fill(v("need", 4, 5), 1.0)
+    for k in ("xd0", "xd1"):
+        iota(v(k, 256, 272), [[0, 16]], 0, 0)
+        iota(v(k, 528, 544), [[0, 16]], 300, 0)
+    iota(v("E0", 256, 272), [[0, 16]], -2500, 0)
+    iota(v("H5", 256, 272), [[0, 16]], 0, 0)
+    for k in ("u0", "u1"):
+        fill(v(k), 1.0)
+    iota(v("rr", 0, 16), [[0, 16]], 8192, 0)
+    iota(v("gt", 64, 80), [[0, 16]], 0, 0)
+    iota(v("s5", 48, 64), [[0, 16]], 0, 0)
+    ms(v("un", 0, 16), -64.0)
+    for k in ("rq0", "rq1"):
+        ms(v(k, 0, 8), 0)
 
     Xw, Lw, Ww = v("X", 0, NP), v("L", 0, NHD), v("W", 0, NP)
     one1 = v("ones", 0, 128, 1, (0, 1))
     rot = [0]
 
-    def argmin(pk, st, base, ns, pmv):
-        jr = (v(pk, 0, 128), one1, v("jrow", 0, 128, 1, (0, 1)))
-        mm([jr + (True, False)])
-        mm([(v(pk, j, 128, 16, (0, ns)), v("da", base + j, base + 16 * ns, 16), v("sel"), False, False) for j in range(16)] + [jr + (False, True)])
-        scan(pmv, v("rst"), v(pk, 0, 128), 0.0, OP.add, OP.min)
-        mn = v("mn", pmv[1], pmv[2])
-        scan(mn, v("rst"), v(pk, 0, 128), 0.0, OP.add, OP.min)
-        tt(v(st, 16, 144), ind(mn, v("cu", 0, 8)), pmv, OP.is_equal)
-        mm([(v(pk, 128, 128 + ns), v("p0", 0, 128, 1, (0, 1)), v("ones", 0, ns, 1, (0, 1)), True, False),
-            (v(pk, 128, 128 + ns), v(st, 16, 144, 1, (0, ns)), v("idn", 0, ns, 1, (0, ns)), False, False),
-            (v(pk, 128, 128 + ns), v(st, 15, 143, 1, (0, ns)), v("nidn", 0, ns, 1, (0, ns)), False, True)])
+    def rep16(k):
+        return v("cu", 56, 56 + k)
 
-    def after_e(t, i, hf):
-        pk, o, oc = PS[2 + hf], 256 * i + 128 * hf, 16 * i + 8 * hf
-        mm([(v(pk, 256, 384), v("boh"), v("em", o, o + 128), True, True)])
-        scan(v("es", o, o + 128), v("cse"), v(pk, 256, 384), 0.0, OP.add, OP.min)
+    def nearest(hf, base, ns, nc, nl):
+        pk, u, o = PS[2 + hf], "u%d" % hf, 128 * hf
+        key, pm, z = v(pk, 0, 128), v("pm", o, o + 128), v("zb", 2 * o, 2 * o + 256)
+        mm([(v(pk, 128, 384, 1, (0, ns)), nl, v("Dm"), True, True)])
+        jr = (key, one1, v("jrow", 0, 128, 1, (0, 1)))
+        mm([jr + (True, False)])
+        if nc:
+            mm([(v(pk, j, 128, 16, (0, nc)), v("dd", base + j, base + 16 * nc, 16), v("sel", 8, 16), False, False) for j in range(16)])
+        cut = [0] + [x for x in PRM["CUT"] if x < ns] + [ns]
+        for a, b in zip(cut, cut[1:]):
+            mm([(v(pk, j, 128, 16, (a, b)), v("da", base + 16 * a + j, base + 16 * b, 16), v("sel", 0, 8), False, False) for j in range(16)] +
+               ([jr + (False, True)] if b == ns else []))
+        scan(pm, v("rst"), key, 0.0, OP.add, OP.min)
+        tt(v(u, 0, 256, 2), key, pm, OP.is_gt)
+        scan(z, v(pk, 128, 384), v(u, 0, 256), 0.0, OP.add, OP.mult)
+        tt(v("Mh", o, o + 128), ind(z, v("cu", 0, 8)), v("mA", 0, 128), OP.mult)
+        ec = v(pk, 384, 384 + ns // 16)
+        mm([(ec, v("Mh", o, o + 128, 1, (0, ns)), v("boh", 0, ns, 16, (0, ns)), True, True)])
+        return ec
+
+    def after_e(i, hf):
+        o, oc = 256 * i + 128 * hf, 16 * i + 8 * hf
         eo = v("eoff", oc, oc + 8)
-        ts(eo, v("es", o + 15, o + 128, 16), fixe, OP.add)
-        if i < 4:
+        if i < 4 and PRM["WGA"]:
             act(v("h32", o, o + 128), ind(Ww, eo), AF.Copy)
             ts(v("hr", o, o + 128), v("h32", o, o + 128), RND - 32.0, OP.add, -RND, OP.add)
-            scan(v("hs", o, o + 128), v("cse"), v("h32", o, o + 128), 0.0, OP.add, OP.min)
-            ts(v("hoff", oc + 16, oc + 24), v("hs", o + 15, o + 128, 16), fixr, OP.add, -RND, OP.add)
+            scan(v("hs", o, o + 128), v("csh"), v("hr", o, o + 128), 0.0, OP.add, OP.min)
+            ts(v("hoff", oc + 16, oc + 24), v("hs", o + 15, o + 128, 16), fixh, OP.add)
+        elif i < 4:
+            ts(v("hr", o, o + 128), ind(Ww, eo), RND - 32.0, OP.add, -RND, OP.add)
+            scan(v("hs", o, o + 128), v("csh"), v("hr", o, o + 128), 0.0, OP.add, OP.min)
+            ts(v("hoff", oc + 16, oc + 24), v("hs", o + 15, o + 128, 16), fixh, OP.add)
         else:
             act(v("H5", 128 * hf, 128 * hf + 128), ind(Ww, eo), AF.Identity, bias=-32.0)
-        if i == 0:
-            act(v("x0", o, o + 128), ind(Xw, eo), AF.Copy)
-            act(v("E0", o, o + 128), v(pk, 256, 384), AF.Copy)
-        else:
-            q = 512 * (i % 2) + 256 + 128 * hf
-            tt(v("sg", q, q + 128), ind(Xw, eo), v("dem", 272 * t + 128 * hf, 272 * t + 128 * hf + 128), OP.is_ge)
-            act(v("OH", o, o + 128), v(pk, 128, 256), AF.Copy)
 
     def chunks(lo, hi, k):
         m = (hi - lo + k - 1) // k
         return [(lo + (hi - lo) * q // m // 2 * 2, lo + (hi - lo) * (q + 1) // m // 2 * 2) for q in range(m)] if m else []
 
+    def columns(t, l0, l1):
+        w = 256 * (l1 - l0)
+        half = (v("pm0", 0, w), v("qrow", 0, 128, 1, (0, 1)), v("ones", 0, w, 1, (0, 1)))
+        lst = [half + (True, False)]
+        for l in range(l0, l1):
+            for hf in range(2):
+                nm, o = ("rr", 16 + 256 * (l - 1) + 128 * hf) if l else ("r0", 144 * t + 16)
+                out = v("pm0", 256 * (l - l0) + 128 * hf, 256 * (l - l0) + 128 * hf + 128)
+                lst += [(out, v(nm, o, o + 128), v("idn"), False, False), (out, v(nm, o - 1, o + 127), v("nidn"), False, False)]
+        mm(lst)
+        mm([(v("pm0", a, w, 16), ST(a), v("ev", 16 * l0, 16 * l1), False, False) for a in range(16)] + [half + (False, True)])
+        for l in range(l0, l1):
+            q = v("pm0", 256 * (l - l0), 256 * (l - l0 + 1))
+            tt(v("t1", 256 * l, 256 * l + 256), v("nL", 256 * l, 256 * l + 256), q, OP.max)
+        act(v("t2", 256 * l0, 256 * l1), v("pm0", 0, w), AF.Relu, bias=-2048.0, scale=2.0)
+
     for t in range(2):
-        need = v("need", t, t + 1)
+        need, need80 = v("need", t, t + 1), v("need", 2 + t, 3 + t)
+        xd, lx = "xd%d" % t, "lx%d" % t
         tag[:] = ["first", 10 * t]
         mark = v("mk", 256 * t, 256 * t + 256)
         h0 = v("hou", 16 * t, 16 * t + 16)
-        cp(v("oL", 0, 16), v("hoi", 16 * t, 16 * t + 16))
+        cp(v("hC", 0, 16), v("hoi", 16 * t, 16 * t + 16))
         act(ind(v("V"), h0), mark, AF.Silu, more=1300.0 if t == 0 else 0.0)
-        ts(v("OH", 0, 256), v("ones"), v("oh16", t, t + 1), OP.mult)
         if t == 0:
-            ts(v("Lg", 0, 256), ind(v("Li"), h0), -1024.0, OP.add)
+            ts(v("nL", 0, 256), ind(v("Li"), h0), -1.0, OP.mult, 1024.0, OP.add)
         else:
-            act(v("Lg", 0, 256), ind(Lw, h0), AF.Copy)
-        ts(v("em", 0, 256), v("Lg", 0, 256), v("oh16", t, t + 1), OP.mult)
+            ts(v("nL", 0, 256), ind(Lw, h0), -1.0, OP.mult)
         for hf in range(2):
-            after_e(t, 0, hf)
-        ts(v("eC", 0, 16), v("es", 15, 256, 16), fixe, OP.add)
+            o, er = 128 * hf, v(PS[2 + hf], 384, 512)
+            mm([(er, ST(t), v("nL", o, o + 128), True, True)])
+            scan(v("es", o, o + 128), v("ncse"), er, 0.0, OP.add, OP.max)
+            eo = v("eoff", 8 * hf, 8 * hf + 8)
+            ts(eo, v("es", o + 15, o + 128, 16), -1.0, OP.mult, fixe, OP.add)
+            after_e(0, hf)
+            act(v(xd, o, o + 128), ind(Xw, eo), AF.Copy)
+            act(v("E0", o, o + 128), er, AF.Copy)
+        for k in (64, 80):
+            ts(v("ev", k, k + 16), v("eoff", 0, 16), -1024.0, OP.add)
+        send(3 * t, v(lx), v(xd), t + 1, 2000.0)
         for j in range(32):
             hf, j = j // 16, j % 16
-            o, a = v("xr", 2048 * hf + j, 2048 * hf + 2048, 16), v("x0", 128 * hf, 128 * hf + 128)
-            if j < REPA:
+            o, a = v("xr", 2048 * hf + j, 2048 * hf + 2048, 16), v(xd, 128 * hf, 128 * hf + 128)
+            if j < PRM["REPA"]:
                 act(o, a, AF.Copy)
             else:
                 cp(o, a)
         for i in range(1, 5):
             q = 16 * i
             tag[:] = ["death", 10 * t + i]
-            hC, sv, dl, ol, pdi, eC = [v(nm, q, q + 16) for nm in ("hC", "sv", "dL", "oL", "pd", "eC")]
-            so, fo, vg = 512 * (i % 2), 32 * (i % 2), v("vg", 256 * (i % 2), 256 * (i % 2) + 256)
-            ts(hC, v("hs", 256 * i - 241, 256 * i, 16), fixr, OP.add, -RND, OP.add)
+            hC = v("hC", q, q + 16)
+            so, vg = 512 * (i % 2), v("vg", 256 * (i % 2), 256 * (i % 2) + 256)
+            hs, un = v("hs", 256 * i - 241, 256 * i, 16), v("un", q - 16, q)
+            ts(hC, hs, fixh, OP.add)
             act(vg, ind(v("V", 0, NHD), v("hoff", q, q + 16)), AF.Relu, bias=-0.25 - 0.75 * t)
             lst, o = [], 0
             for cc in range(16):
@@ -340,33 +399,20 @@ def program(c):
                     mm(lst)
                     lst = []
             mm([(v("pc", 0, 256), v("idn"), v("nthr"), False, False), (v("pc", 0, 256), v("bob"), vg, False, True)])
-            act(v("sg", so, so + 256), v("pc", 0, 256), AF.Sign, scale=-1.0)
-            mm([(v("pdd", 0, 16), S(a), v("sg", so + a, so + 256, 16), a == 0, a == 15) for a in range(16)])
-            if i == 1:
-                ts(sv, v("pdd", 0, 16), 0.0, OP.is_ge)
-            else:
-                ts(v("fl", fo, fo + 16), v("pdd", 0, 16), 0.0, OP.is_ge)
-                tt(sv, v("fl", fo, fo + 16), v("up"), OP.mult)
-            tt(v("s3", q, q + 16), hC, dl, OP.subtract)
-            tt(v("s3", 80 + q, 96 + q), v("s3", q, q + 16), sv, OP.mult)
-            tt(v("s3", 160 + q, 176 + q), v("s3", 80 + q, 96 + q), dl, OP.add)
-            cp(ol, v("s3", 160 + q, 176 + q))
-            if i < 4:
-                act(ind(v("V"), ol), mark, AF.Silu)
-            else:
-                ts(v("uph"), sv, -32.0, OP.mult)
-                mm([(v("pm1", 0, 256), one1, v("ones", 0, 256, 1, (0, 1)), True, False)] +
-                   [(v("pm1", a, 256, 16), v("ST", 128 * a, 128 * a + 128), v("uph"), False, False) for a in range(16)])
+            act(v("sg", so, so + 256), v("pc", 0, 256), AF.Sign)
+            if i == 4:
+                mm([(v("pm1", 0, 256), v("bo"), v("sg", so, so + 256), True, False)] +
+                   [(v("pm1", a, 256, 16), ST(a), un, False, False) for a in range(16)])
+                mm([(v("pdd", 0, 16), S(a, 1), v("sg", so + a, so + 256, 16), a == 0, False) for a in range(16)] +
+                   [(v("pdd", 0, 16), v("ih", 256, 384), un, False, False)])
             for hf in range(2):
-                pk, st, o = PS[2 + hf], "st%d" % hf, 128 * hf
+                o = 128 * hf
                 tag[0] = "near%d" % hf
                 ho = v("hoff", q + 8 * hf, q + 8 * hf + 8)
-                lg = v("Lg", 256 * i + o, 256 * i + o + 128)
-                act(lg, ind(Lw, ho), AF.Copy)
-                ts(v("Lu", o, o + 128), ind(Lw, ho), 1024.0, OP.add)
-                c3 = chunks(0, N3, C3) if hf == 0 else chunks(256 - N3, 256, C3)
-                c1 = chunks(N3, 128, C1) if hf == 0 else chunks(128, 256 - N3, C1)
-                for a, b in c3:
+                ts(v("Lu", o, o + 128), ind(Lw if t or i > 1 else v("Li"), ho), 1024.0 if t or i > 1 else 0.0, OP.add)
+                nl = v("nL", 256 * i + o, 256 * i + o + 128)
+                ts(nl, v("Lu", o, o + 128), -1.0, OP.mult, 1024.0, OP.add)
+                for a, b in chunks(o + 128 - NB, o + 128, PRM["C3"]):
                     r = rot[0] % 2
                     rot[0] += 1
                     w = 16 * (b - a)
@@ -375,116 +421,150 @@ def program(c):
                     mm([(v(PS[r], 0, w), v("nidn"), v("xr", 16 * a, 16 * b), True, False)])
                     mm([(v(PS[r], 0, w), v("idn"), ag, False, True)])
                     act(v("da", 16 * a, 16 * b), v(PS[r], 0, w), AF.Abs)
-                for a, b in c1:
+                for a, b in chunks(o + NC, o + 128 - NB, PRM["C1"]) + chunks(o, o + NC, PRM["C1"]):
                     d = v("dd", 16 * a, 16 * b)
                     tt(d, ind(Xw, v("Lu", a, b)), v("xr", 16 * a, 16 * b), OP.subtract)
-                    act(v("da", 16 * a, 16 * b), d, AF.Abs)
+                    if a < o + NC:
+                        ts(v("da", 16 * a, 16 * b), d, 0.0, OP.max, 2.0, OP.mult)
+                    else:
+                        act(v("da", 16 * a, 16 * b), d, AF.Abs)
                 tag[0] = "chain%d" % hf
-                argmin(pk, st, 16 * o, 128, v("pm", o, o + 128))
-                tt(v("em", 256 * i + o, 256 * i + o + 128), lg, v(pk, 128, 256), OP.mult)
-                after_e(t, i, hf)
-            tag[0] = "tv"
-            ts(eC, v("es", 256 * i + 15, 256 * i + 256, 16), fixe, OP.add)
-            emi, emp, em0 = v("em", 256 * i, 256 * i + 256), v("em", 256 * i - 256, 256 * i), v("em", 0, 256)
-            mm([(v("pm0", 0, 256), v("boh"), emi, True, False), (v("pm0", 0, 256), v("nboh"), emp, False, True),
-                (v("pm0", 256, 512), v("boh"), em0, True, False), (v("pm0", 256, 512), v("nboh"), emi, False, True)])
-            tt(v("Tv", 512 * i - 512, 512 * i - 256), v("OH", 256 * i - 256, 256 * i), v("pm0", 0, 256), OP.mult)
-            tt(v("Tv", 512 * i - 256, 512 * i), v("OH", 256 * i, 256 * i + 256), v("pm0", 256, 512), OP.mult)
-            tt(v("e0d", q - 16, q), v("eC", 0, 16), v("dW", q - 16, q), OP.subtract)
+                ec = nearest(hf, 16 * o, 128, NC, nl)
+                ts(v("eoff", q + 8 * hf, q + 8 * hf + 8), ec, 1024.0, OP.add)
+                after_e(i, hf)
+                r = 16 + 256 * (i - 1) + o
+                scan(v("rr", r, r + 128, 1, "back"), v("u%d" % hf, 2, 258, 2, "back"), v("p0"), 0.0, OP.mult, OP.max)
             tag[0] = "paid"
-            if i == 4:
-                mm([(v("pm1", 0, 256), v("bo"), v("sg", so + 256, so + 512), False, True)])
-            mm([(v("pdd", 16, 32), S(a), v("sg", so + 256 + a, so + 512, 16), a == 0, a == 15) for a in range(16)])
-            ts(v("fl", fo + 16, fo + 32), v("pdd", 16, 32), need, OP.is_ge)
-            tt(pdi, sv, v("fl", fo + 16, fo + 32), OP.mult)
+            m = PRM["SG4"] if i == 4 else 1
+            sga = PRM["SGA"] and i < 4
+            for k in range(m):
+                a, b = 256 * k // m, 256 * (k + 1) // m
+                if sga:
+                    act(v("jk", 0, 256), ind(Xw, v("eoff", q, q + 16)), AF.Copy)
+                    mm([(v("pm1", 0, 256), v("nidn"), v(xd, 272, 528), True, False), (v("pm1", 0, 256), v("idn"), v("jk", 0, 256), False, True)])
+                    act(v("sg", so + 256, so + 512), v("pm1", 0, 256), AF.Sign, bias=0.5)
+                else:
+                    tt(v("sg", so + 256 + a, so + 256 + b), ind(Xw, v("eoff", q + a // 16, q + b // 16)), v(xd, 272 + a, 272 + b), OP.is_ge)
             if i < 4:
-                tt(v("up"), sv, pdi, OP.subtract)
-                tt(v("wu"), v("wC"), v("up"), OP.mult)
+                lst = [(v("pdd", 0, 32), S(a), v("sg", so + a, so + 512, 16), a == 0, a == 15) for a in range(16)]
+                mm(lst[:1] + [(v("pdd", 0, 16), v("ih", 0, 128), hs, False, False), (v("pdd", 0, 16), v("ih", 128, 256), un, False, False)] + lst[1:])
+                sv, fl = v("sv", q, q + 16), v("fl", q, q + 16)
+                ts(sv, v("pdd", 0, 16), thr, OP.is_lt, -64.0, OP.mult)
+                ts(fl, v("pdd", 16, 32), v("need", 4 + t, 5 + t) if sga else need, OP.is_lt)
+                tt(v("s2", 0, 16), v("pdd", 0, 16), v("dL", 160 + q, 176 + q), OP.min)
+                ts(v("oL", q, q + 16), v("s2", 0, 16), cpc, OP.add, 128.0, OP.mult)
+                act(ind(v("V"), v("oL", q, q + 16)), mark, AF.Silu)
+                tt(v("un", q, q + 16), sv, fl, OP.mult)
+                tt(v("wu"), v("un", q, q + 16), v("wC", 16, 32), OP.mult)
+            else:
+                mm([(v("pm1", 0, 256), v("bo"), v("sg", so + 256, so + 512), False, True)])
+                mm([(v("pdd", 0, 16), S(a), v("sg", so + 256 + a, so + 512, 16), False, a == 15) for a in range(16)])
+                ts(v("pd", 64, 80), v("pdd", 0, 16), need80, OP.is_ge, -64.0, OP.mult)
+            tag[0] = "cols"
+            k = (0, 96, 112, 128)[i - 1]
+            ts(v("ev", k, k + 16), v("eoff", q, q + 16), -1024.0, OP.add)
+            if i == 1:
+                columns(t, 0, 1)
+            if i >= 3:
+                l, w = (1, 32) if i == 3 else (3, 16)
+                tt(v("s3", 0, w), v("ev", 80 + 16 * l, 80 + 16 * l + w), v("ev", 64, 64 + w), OP.subtract)
+                tt(v("s3", 32, 32 + w), v("s3", 0, w), v("fl", 16 * l, 16 * l + w), OP.mult)
+                tt(v("ev", 16 * l, 16 * l + w), v("s3", 32, 32 + w), v("ev", 64, 64 + w), OP.add)
+                columns(t, l, l + 2)
         tag[:] = ["send", 10 * t + 5]
         rq, lq, rs, ls = "rq%d" % t, "lq%d" % t, "rs%d" % t, "ls%d" % t
-        ts(v("vg", 0, 256), v("pm1", 0, 256), 31.0, OP.add, need, OP.is_lt)
-        scan(v("prb"), v("ones"), v("vg", 0, 256), 0.0, OP.mult, OP.add)
+        ts(v("vg", 0, 256), v("pm1", 0, 256), 80.0, OP.add, need, OP.is_lt)
+        scan(v("prb"), v("ones", 0, 256), v("vg", 0, 256), 0.0, OP.mult, OP.add)
         for k in range(3):
             act(v("jk", 256 * k, 256 * k + 256), v("prb"), AF.Sign, bias=v("dX", 8 + k, 9 + k), accum=v("ac", k, k + 1))
-        ix = v("uo", 0, 3)
+        ix = v(rq, 4, 7)
         ts(ix, v("ac", 0, 3), -0.5, OP.mult, 128.0, OP.add)
-        ts(v("y1"), ind(v("H5"), ix), RND, OP.add, -RND, OP.add)
-        scan(v(rq, 96, 144), v("csh", 0, 48), v("y1"), 0.0, OP.add, OP.min)
-        act(v(rq, 0, 48), ind(v("x0"), ix), AF.Copy)
-        act(v(rq, 48, 96), ind(v("dem", 272 * t, 272 * t + 272), ix), AF.Copy)
-        send(2 * t, v(lq), v(rq), t + 1)
-        act(v("xs0"), ind(v("x0"), ix), AF.Copy)
+        ts(v("yh", 0, 48), ind(v("H5"), ix), RND, OP.add, -RND, OP.add)
+        scan(v("yh", 48, 96), v("csh", 0, 48), v("yh", 0, 48), 0.0, OP.add, OP.min)
+        ts(v(rq, 0, 3), v("yh", 48 + 15, 96, 16), fixh, OP.add)
+        ts(v(rq, 8, 56), ind(v("IT", 0, 272), ix), 0.0, OP.add)
+        send(3 * t + 1, v(lq), v(rq), t + 1)
+        act(v("xs0"), ind(v(xd, 0, 272), ix), AF.Copy)
         act(v("y2"), ind(v("E0"), ix), AF.Copy)
-        scan(v("y3"), v("cse", 0, 48), v("y2"), 0.0, OP.add, OP.min)
-        ts(v("e0c", 0, 3), v("y3", 15, 48, 16), fixe, OP.add)
+        scan(v("y3"), v("ncse", 0, 48), v("y2"), 0.0, OP.add, OP.max)
+        ts(v("e0c", 0, 3), v("y3", 15, 48, 16), -1.0, OP.mult, fixe, OP.add)
         tt(v("z1", 0, 3), v("e0c", 0, 3), v("dX", 0, 3), OP.min)
         eo0 = v("uo", 4, 7)
         cp(eo0, v("z1", 0, 3))
         tag[0] = "payl"
-        cp(v("gt", 112, 128), v("pd", 48, 64))
-        for i in (1, 0):
-            tt(v("gt", 80 + 16 * i, 96 + 16 * i), v("gt", 96 + 16 * i, 112 + 16 * i), v("pd", 16 * i + 16, 16 * i + 32), OP.add)
-        tt(v("s4", 0, 48), v("gt", 80, 128), v("K1", 0, 48), OP.mult)
-        ms(v("s4", 48, 64), 0.0)
-        tt(v("s5", 16, 64), v("pd", 16, 64), v("K2", 0, 48), OP.mult)
-        tt(v("s4", 16, 64), v("s4", 16, 64), v("s5", 16, 64), OP.add)
-        for i in range(5):
-            tt(v("s2", 16 * i, 16 * i + 16), v("pd", 64, 80), v("K1", 16 * i, 16 * i + 16) if i < 4 else v("K2", 48, 64), OP.mult)
-        tt(v("s1"), v("s4"), v("s2"), OP.add)
-        ts(v("oT"), v("s1"), 2048.0, OP.add)
-        for a, b in ((0, 10), (10, 30), (30, 54), (54, 80)):
-            act(v("tl", 16 * a, 16 * b), ind(v("Tv"), v("oT", a, b)), AF.Copy)
-            tt(ind(v("L"), v("oL", a, b)), v("Lg", 16 * a, 16 * b), v("tl", 16 * a, 16 * b), OP.add)
+        tt(v("pd", 16, 64), v("sv", 16, 64), v("un", 16, 64), OP.subtract)
+        cp(v("gt", 48, 64), v("pd", 48, 64))
+        tt(v("gt", 32, 48), v("pd", 32, 48), v("pd", 48, 64), OP.add)
+        for k in (16, 0):
+            tt(v("gt", k, k + 16), v("gt", 32, 48), v("pd", 16, 32), OP.add)
+        tt(v("s1"), v("dL", 0, 80), v("hC"), OP.subtract)
+        tt(v("s2"), v("gt"), v("s1"), OP.mult)
+        tt(v("s2"), v("s2"), v("dL", 80, 160), OP.add)
+        pd4 = v("pd", 64, 80)
+        tt(v("s4"), ind(pd4, rep16(5)), v("s1"), OP.mult)
+        tt(v("s4"), v("s4"), v("s2"), OP.add)
+        ts(v("oP"), v("s4"), 1.0 / 64, OP.mult)
+        a = 0
+        for k in PRM["LCH"]:
+            tt(ind(v("L"), v("oP", a, a + k)), v("t2", 16 * a, 16 * (a + k)), v("t1", 16 * a, 16 * (a + k)), OP.subtract)
+            a += k
         tag[0] = "payw"
-        cp(v("gt", 48, 64), v("pd", 64, 80))
-        for i in range(3):
-            tt(v("gt", 16 * i, 16 * i + 16), v("gt", 80 + 16 * i, 96 + 16 * i), v("pd", 64, 80), OP.add)
-        tt(v("ed"), v("eC", 16, 80), v("dW"), OP.subtract)
-        tt(v("s5", 0, 64), v("gt", 16, 80), v("ed"), OP.mult)
-        tt(v("s6", 0, 64), v("pd", 16, 80), v("e0d"), OP.mult)
-        tt(v("s5", 0, 64), v("s5", 0, 64), v("s6", 0, 64), OP.add)
-        tt(v("s6", 0, 64), v("s5", 0, 64), v("dW"), OP.add)
-        cp(v("oW"), v("s6", 0, 64))
-        for k in range(0, 64, 16):
-            act(ind(v("W"), v("oW", k, k + 16)), v("h32", 16 * k, 16 * k + 256), AF.Silu)
+        for k in range(0, 64 * (not PRM["WGA"]), 16):
+            act(v("h32", 16 * k, 16 * k + 256), ind(Ww, v("eoff", k, k + 16)), AF.Copy)
+        cp(v("eF"), v("eoff"))
+        tt(v("s5", 64, 128), v("dW", 0, 64), v("eF", 16, 80), OP.subtract)
+        tt(v("s6", 64, 128), ind(v("eF", 0, 16), rep16(4)), v("dW", 0, 64), OP.subtract)
+        tt(v("s5", 0, 48), ind(pd4, rep16(3)), v("gt", 32, 80), OP.add)
+        tt(v("s3", 0, 64), v("s5", 0, 64), v("s5", 64, 128), OP.mult)
+        tt(v("s6", 0, 64), v("pd", 16, 80), v("s6", 64, 128), OP.mult)
+        tt(v("s3", 0, 64), v("s3", 0, 64), v("s6", 0, 64), OP.subtract)
+        tt(v("s6", 0, 64), v("s3", 0, 64), v("dW", 64, 128), OP.add)
+        ts(v("oW"), v("s6", 0, 64), 1.0 / 64, OP.mult)
+        for k in range(0, 64, PRM["WCH"]):
+            act(ind(v("W"), v("oW", k, k + PRM["WCH"])), v("h32", 16 * k, 16 * (k + PRM["WCH"])), AF.Silu)
         if t == 0:
-            add("D", lambda g, T, x: g.vector.tensor_reduce(ap(T, v("rd", 0, 1)), ap(T, v("gt", 0, 16)), AxisListType.X, OP.add),
-                v("rd", 0, 1), [v("gt", 0, 16)], 64.0)
-            cp(v("rb", 0, 1), v("rd", 0, 1))
+            tt(v("s1", 0, 16), v("gt", 0, 16), pd4, OP.add)
+            add("D", lambda g, T, x: g.vector.tensor_reduce(ap(T, v("ac", 3, 4)), ap(T, v("s1", 0, 16)), AxisListType.X, OP.add),
+                v("ac", 3, 4), [v("s1", 0, 16)], 64.0)
+            cp(v("rb", 0, 1), v("ac", 3, 4))
             mm([(v("pm0", 0, 1), v("ones", 0, 128), v("rb", 0, 1), True, True)])
-            cp(v("ri", 0, 1), v("pm0", 0, 1))
+            ts(v("ri", 0, 1), v("pm0", 0, 1), -1.0 / 64, OP.mult)
             ts(v("ri", 1, 2), v("ri", 0, 1), 1, OP.bitwise_and)
             ts(v("need", 1, 2), v("ri", 1, 2), 8.5, OP.add)
+            lin(v("need", 3, 4), v("need", 1, 2), 1.0, 80.0)
+            lin(v("need", 5, 6), v("need", 1, 2), 2.0, -16.0)
         else:
             act(v("Lo", 0, 1024), v("L", 0, 1024), AF.Identity, bias=1024.0)
             act(v("Lo", 1024, 2048), v("L", 1024, 2048), AF.Identity, bias=1024.0)
             store("S", lambda T: T.yl[:], v("Lo"), 1048e3)
-            for k in range(6):
-                w = v("W", 512 * k, 512 * k + 512)
-                ts(w, w, RND - 32.0, OP.add, -RND, OP.add)
-            store("S", lambda T: T.yw[:], v("W", 0, NP, 1, (0, 128, 16)), 98e3)
+            wf, w8 = v("wr32", 0, 192), v("W", 0, NP, 1, (0, 128, 16))
+            add("S", lambda g, T, x: g.sync.dma_start(ap(T, wf), ap(T, w8)), wf, [w8], 60.0, lat=98e3, kind="d")
+            ts(wf, wf, RND - 32.0, OP.add, -RND, OP.add)
+            store("S", lambda T: T.yw[:], wf, 98e3)
         tag[0] = "came"
-        hq = v("uo", 8, 11)
-        ts(hq, v(lq, 96 + 15, 144, 16), fixh, OP.add)
+        hq, ixc = v(lq, 0, 3), v(lq, 4, 7)
         ts(v("Lu", 0, 48), ind(Lw, hq), 1024.0, OP.add)
-        for k in range(2):
-            a, b = 384 * k, 384 * k + 384
-            act(v("xr", a, b), ind(v(lq, 0, 48), rep48(24 * k, 24 * k + 24)), AF.Copy)
-            tt(v("dd", a, b), ind(Xw, v("Lu", 24 * k, 24 * k + 24)), v("xr", a, b), OP.subtract)
-        for k in range(2):
-            a, b = 384 * k, 384 * k + 384
-            act(v("da", a, b), v("dd", a, b), AF.Abs)
-        cp(v("y1"), ind(Lw, hq))
-        argmin("pk0", "st0", 0, 48, v("pm", 0, 128))
-        tt(v("em", 0, 48), v("y1"), v("pk0", 128, 176), OP.mult)
-        mm([(v("pk0", 256, 304), v("boh"), v("em", 0, 48), True, True)])
-        scan(v("y3"), v("cse", 0, 48), v("pk0", 256, 304), 0.0, OP.add, OP.min)
+        nl = v("yh", 96, 144)
+        ts(nl, v("Lu", 0, 48), -1.0, OP.mult, 1024.0, OP.add)
+        qc = PRM["QC"]
+        for a, b in chunks(qc, 48, 16) + chunks(0, qc, 16):
+            xr, d = v("xr", 16 * a, 16 * b), v("dd", 16 * a, 16 * b)
+            act(xr, ind(v(lx, 0, 272), v(lq, 8 + a, 8 + b)), AF.Copy)
+            tt(d, ind(Xw, v("Lu", a, b)), xr, OP.subtract)
+            if a < qc:
+                ts(v("da", 16 * a, 16 * b), d, 0.0, OP.max, 2.0, OP.mult)
+            else:
+                act(v("da", 16 * a, 16 * b), d, AF.Abs)
+        xq, dq = v("xq", 0, 48), v("xq", 48, 96)
+        act(xq, ind(v(lx, 0, 272), ixc), AF.Copy)
+        act(dq, ind(v(lx, 272, 544), ixc), AF.Copy)
+        ec = nearest(0, 0, 48, qc, nl)
         fo = v("uo", 12, 15)
-        ts(fo, v("y3", 15, 48, 16), fixe, OP.add)
-        act(v("fr"), v("pk0", 256, 304), AF.Identity, bias=1024.0)
-        tt(v("b1"), ind(Xw, fo), v(lq, 48, 96), OP.is_ge)
-        tt(v("dx"), ind(Xw, fo), v(lq, 0, 48), OP.subtract)
-        ts(v("fC", 0, 3), v("y3", 15, 48, 16), fixe, OP.add)
+        ts(fo, ec, 1024.0, OP.add)
+        ts(v("fC", 0, 3), ec, 1024.0, OP.add)
+        act(v("fr"), ind(v("IT"), fo), AF.Copy)
+        tt(v("b1"), ind(Xw, fo), dq, OP.is_ge)
+        tt(v("dx"), ind(Xw, fo), xq, OP.subtract)
         mm([(v("pk1", 0, 48), v("bo"), v("b1"), True, True)])
         scan(v("y2"), v("csh", 0, 48), v("pk1", 0, 48), 0.0, OP.add, OP.min)
         ts(v("b2"), v("pk1", 0, 48), need, OP.is_lt)
@@ -504,7 +584,7 @@ def program(c):
         mm(lst)
         ts(v("b3"), v("pc", 0, 48), 0.0, OP.is_lt)
         tt(v(rs), v("dx"), v("b3"), OP.mult)
-        send(2 * t + 1, v(ls), v(rs), -(t + 1))
+        send(3 * t + 2, v(ls), v(rs), -(t + 1))
         scan(v("y1"), v("csh", 0, 48), v("b3"), 0.0, OP.add, OP.min)
         tt(v("z2", 0, 3), v("fC", 0, 3), v("dX", 3, 6), OP.subtract)
         ts(v("z3", 0, 3), v("y1", 15, 48, 16), fixh, OP.add)
@@ -512,7 +592,7 @@ def program(c):
         tt(v("z2", 0, 3), v("z3", 0, 3), v("dX", 3, 6), OP.add)
         fo2 = v("uo", 16, 19)
         cp(fo2, v("z2", 0, 3))
-        cp(ind(v("X"), fo2), v(lq, 0, 48))
+        cp(ind(v("X"), fo2), xq)
         tt(ind(v("X"), eo0), v("xs0"), v(ls), OP.add)
     store("S", lambda T: T.yx[:, 0:NP // 2], v("X", 0, NP // 2), 393e3)
     store("A", lambda T: T.yx[:, NP // 2:NP], v("X", NP // 2, NP), 393e3)
@@ -546,87 +626,165 @@ def depend(ops):
     return deps, full
 
 
-def schedule(ops, deps, succ, hop, win, rnd, order=None):
+def schedule(alts, deps, tries):
+    ops = alts[0]
     n = len(ops)
-    late = [2000.0 + o["lat"] / 200.0 if o["kind"] == "d" else o["lat"] for o in ops]
-    eng = [o["e"] for o in ops]
-    cost = [o["cost"] for o in ops]
+    succ = [[] for _ in ops]
+    for k in range(n):
+        for p in deps[k]:
+            succ[p].append(k)
+    eng = ["DAPGS".index(o["e"]) for o in ops]
+    dma = [o["kind"] == "d" for o in ops]
+    pre = [[p for p in deps[k] if not (eng[p] == 2 and eng[k] == 2)] for k in range(n)]
+    models = [([o["cost"] for o in a], [o["lat"] / c["bw"] if o["kind"] == "d" else o["lat"] + c["hop"] for o in a], c["hop"])
+              for a, c in zip(alts, COSTS)]
 
-    def gap(p, k):
-        return 0.0 if eng[p] == "P" and eng[k] == "P" else late[p] + hop
+    def times(order, m):
+        cost, lat, hop = models[m]
+        free, rdy, st, dfree = [0.0] * 5, [0.0] * n, [0.0] * n, 0.0
+        for k in order:
+            e = eng[k]
+            t = free[e]
+            for p in pre[k]:
+                if rdy[p] > t:
+                    t = rdy[p]
+            st[k] = t
+            t += cost[k]
+            free[e] = t
+            if dma[k]:
+                dfree = max(dfree, t + 2000.0) + lat[k]
+                rdy[k] = dfree + hop
+            else:
+                rdy[k] = t + lat[k]
+        return max(rdy) - hop, st, rdy
 
+    cost, lat, hop = models[0]
+
+    def tails(order):
+        tl, nx = [0.0] * n, [0.0] * 5
+        for k in reversed(order):
+            la = lat[k] + (2000.0 + hop if dma[k] else 0.0)
+            t = la
+            for s in succ[k]:
+                x = tl[s] + (0.0 if eng[k] == 2 and eng[s] == 2 else la)
+                if x > t:
+                    t = x
+            tl[k] = cost[k] + max(t, nx[eng[k]])
+            nx[eng[k]] = tl[k]
+        return tl
+
+    def redo(order, st, rdy, lo, hi, pr, win):
+        i = 0
+        while i < n and st[order[i]] < lo:
+            i += 1
+        i = max(i, NLOAD)
+        done = [False] * n
+        free = [0.0] * 5
+        for k in order[:i]:
+            done[k] = True
+            free[eng[k]] = st[k] + cost[k]
+        rd = list(rdy)
+        left, est = {}, {}
+        ready = [[] for _ in range(5)]
+        for k in order[i:]:
+            if st[k] > hi + 6000:
+                break
+            left[k] = sum(not done[p] for p in deps[k])
+            if not left[k]:
+                est[k] = max([rd[p] for p in pre[k]], default=0.0)
+                ready[eng[k]].append(k)
+        out = order[:i]
+        while True:
+            tm, e = 1e18, -1
+            for x in range(5):
+                if ready[x]:
+                    t = max(free[x], min([est[q] for q in ready[x]]))
+                    if t < tm:
+                        tm, e = t, x
+            if tm > hi:
+                break
+            r = ready[e]
+            k, b = -1, -1e18
+            for q in r:
+                if est[q] <= tm + 40.0 and pr[q] > b:
+                    k, b = q, pr[q]
+            h, hb = -1, b
+            for q in r:
+                if pr[q] > hb and est[q] < tm + cost[k]:
+                    h, hb = q, pr[q]
+            if h >= 0:
+                f, fb = -1, -1e18
+                for q in r:
+                    if pr[q] > fb and max(est[q], tm) + cost[q] <= est[h] and q != h:
+                        f, fb = q, pr[q]
+                if f >= 0:
+                    k = f
+                elif est[h] <= tm + 40.0 + win * cost[k]:
+                    k = h
+            r.remove(k)
+            t = free[e] = max(est[k], free[e]) + cost[k]
+            rd[k] = t + lat[k] + (2000.0 + hop if dma[k] else 0.0)
+            done[k] = True
+            out.append(k)
+            for q in succ[k]:
+                if q in left:
+                    left[q] -= 1
+                    if not left[q]:
+                        est[q] = max([rd[p] for p in pre[q]], default=0.0)
+                        ready[eng[q]].append(q)
+        return out + [k for k in order[i:] if not done[k]]
+
+    def state(o, first):
+        ends = [first[0]] + [times(o, m)[0] for m in range(1, len(models))]
+        return [o, first[1], first[2], ends, (sum(ends) + ends[0]) / (len(ends) + 1), None]
+
+    rng = np.random.default_rng(SEED)
+    names = sorted(set(o["W"][0][0] for o in ops))
+    part, step = np.array([o["tag"][0] for o in ops]), np.array([o["tag"][1] for o in ops])
+    kind = np.array([names.index(o["W"][0][0]) for o in ops])
+    order = list(range(n))
     pr = [0.0] * n
-    if order is None:
-        for k in range(n - 1, -1, -1):
-            pr[k] = cost[k] + max([gap(k, s) + pr[s] for s in succ[k]] + [late[k]])
-        pr = [p + float(r) for p, r in zip(pr, rnd)]
-        for k in range(NLOAD):
-            pr[k] += 1e7 - 1e5 * k
-    left = [len(d) for d in deps]
-    est = [0.0] * n
-    ready = [k for k in range(n) if not left[k]]
-    free = {e: 0.0 for e in "DAPGS"}
-    dmafree = 0.0
-    out, start, end = [], [0.0] * n, 0.0
-    for it in range(n):
-        if order is None:
-            k0 = min(ready, key=lambda k: max(est[k], free[eng[k]]))
-            e = eng[k0]
-            tm = max(est[k0], free[e])
-            now = max((k for k in ready if eng[k] == e and est[k] <= tm + 40.0), key=lambda k: (pr[k], -k))
-            k = max((k for k in ready if eng[k] == e and est[k] <= tm + 40.0 + win * cost[now]), key=lambda k: (pr[k], -k))
-            ready.remove(k)
-        else:
-            k = order[it]
-        start[k] = max(est[k], free[eng[k]])
-        fin = free[eng[k]] = start[k] + cost[k]
-        if ops[k]["kind"] == "d":
-            dmafree = max(dmafree, fin + 2000.0) + ops[k]["lat"] / 200.0
-            late[k] = dmafree - fin
-        end = max(end, fin + late[k])
-        out.append(k)
-        for s in succ[k]:
-            est[s] = max(est[s], fin + gap(k, s))
-            left[s] -= 1
-            if not left[s] and order is None:
-                ready.append(s)
-    return out, start, end
+    for k in range(n - 1, -1, -1):
+        pr[k] = cost[k] + max([pr[s] + lat[k] for s in succ[k]], default=0.0)
+    order = redo(order, [0.0] * n, times(order, 0)[2], -1.0, 1e17, pr, 0.3)
+    best = cur = state(order, times(order, 0))
+    for it in range(tries):
+        if cur[5] is None:
+            cur[0] = sorted(cur[0], key=lambda k: cur[1][k])
+            cur[5] = (np.array(cur[1]), np.array(tails(cur[0])))
+        st, tl = cur[5]
+        lo = rng.random() * cur[3][0] - 2000
+        hi = lo + 3000 + rng.random() * 11000
+        x, u = rng.random(), rng.random(4)
+        pr = -st * x + tl * (1 - x)
+        if u[0] < 0.5:
+            pr = pr + rng.normal(size=n) * 400 * u[1]
+        c = np.flatnonzero((st >= lo) & (st < hi))
+        if u[2] < 0.7 and len(c):
+            k = c[rng.integers(len(c))]
+            m = (part == part[k]) & (step == step[k])
+            if u[3] < 0.6:
+                m &= kind == kind[k]
+            pr[m] += rng.normal() * 1500
+        o = redo(cur[0], cur[1], cur[2], lo, hi, list(pr), rng.random() * 0.6)
+        lim = cur[4] - TEMP * (1 - it / tries) * math.log(rng.random())
+        f = times(o, 0)
+        if f[0] - cur[3][0] > lim - cur[4] + 400:
+            continue
+        new = state(o, f)
+        if new[4] <= lim:
+            cur = new
+            if cur[4] < best[4]:
+                best = cur
+    return best
 
 
 def plan(tries=None):
     alts = [program(c) for c in COSTS]
     ops = alts[0]
     deps, full = depend(ops)
-    succ = [[] for _ in ops]
-    for k in range(len(ops)):
-        for p in deps[k]:
-            succ[p].append(k)
-    best = None
-    rng = np.random.default_rng(SEED)
-    names = sorted(set(o["W"][0][0] for o in ops))
-    part, step = np.array([o["tag"][0] for o in ops]), np.array([o["tag"][1] for o in ops])
-    kind = np.array([names.index(o["W"][0][0]) for o in ops])
-    for it in range(tries or TRIES):
-        off = np.array([BIAS.get(o["tag"][0], 0.0) for o in ops]) if best is None else best[3].copy()
-        if it:
-            k, u = rng.integers(len(ops)), rng.random(4)
-            m = np.ones(len(ops), bool)
-            if u[0] < 0.5:
-                m &= kind == kind[k]
-            if u[1] < 0.7 or u[0] >= 0.5:
-                m &= part == part[k]
-            if u[2] < 0.55:
-                m &= step == step[k]
-            elif u[2] < 0.75:
-                m &= step % 10 == step[k] % 10
-            off[m] += rng.normal() * (3000.0 if u[3] < 0.5 else 600.0)
-        order, start, end = schedule(ops, deps, succ, COSTS[0]["hop"], WIN, off)
-        if best is not None and end > best[2][0] * 1.01:
-            continue
-        ends = [end] + [schedule(a, deps, succ, c["hop"], 0, 0, order)[2] for a, c in zip(alts[1:], COSTS[1:])]
-        if best is None or sum(ends) + end <= sum(best[2]) + best[2][0]:
-            best = (order, start, ends, off)
-    order, start, end = best[0], best[1], best[2][0]
+    best = schedule(alts, deps, TRIES if tries is None else tries)
+    order, start, end = best[0], best[1], best[3][0]
     count = {e: 0 for e in "DAPG"}
     known = {e: {} for e in "DAPGS"}
     nd = 0
@@ -652,8 +810,8 @@ def plan(tries=None):
         else:
             o["sig"], o["kn"] = ("ar%d" % o["k"], NENG), {}
     last = [("c" + e, count[e]) for e in "DAPG"] + [("dm%d" % k, 16) for k in range(nd)]
-    last += [("ar%d" % k, NENG) for k in range(4)] + [("lc", 4 * NENG)]
-    return dict(ops=ops, order=order, last=last, start=start, end=end, best=best[2:])
+    last += [("ar%d" % k, NENG) for k in range(NREM)] + [("lc", NREM * NENG)]
+    return dict(ops=ops, order=order, last=last, start=start, end=end, best=best[3:4])
 
 
 PLAN = {}

@@ -4,25 +4,25 @@ from concourse.mybir import AluOpType as OP, AxisListType, ActivationFunctionTyp
 
 N = 8
 NP, NHD = 3072, 2048
-PRM = dict(NC=32, NB=64, C1=32, C3=32, REPA=0, QC=16, SG4=2, LCH=(6, 6, 6, 6, 8, 48), WCH=16, CUT=(), SGA=0, WGA=0)
+PRM = dict(NC=(32,) * 8, NB=(64,) * 8, WV=0, C1=32, C3=32, REPA=(0, 0, 0, 0), QC=16, SG4=2, LCH=(8, 8, 16, 48), WCH=8, CUT=(), SGA=0, REPG=6, GCV=1, MHS=0, SURE=300.0, LA=0, XV=48, LINV=0, FAST=1, HG=0)
 NENG = 8
 F, B, H, I, U = "float32", "bfloat16", "float16", "int32", "uint16"
 SB = {
-    "X": (NP + 96, B), "Li": (NHD, I), "L": (NHD + 1280, F), "Lo": (NHD, F), "W": (NP + 1024, F), "V": (NHD + 1280, F), "IT": (NP, F),
+    "X": (NP + 96, B), "Li": (NHD, I), "L": (NHD + 1280, F), "W": (NP + 1024, F), "V": (NHD + 1280, F), "IT": (NP, F),
     "wi": (192, I), "wc": (192, H), "hoi": (32, I), "hou": (32, U), "xd0": (544, B), "xd1": (544, B), "lx0": (544, B), "lx1": (544, B),
-    "ones": (512, B), "idn": (128, B), "nidn": (128, B), "bo": (128, B), "boh": (128, H), "bk": (256, B), "bob": (128, B),
+    "ones": (256, B), "idn": (128, B), "nidn": (128, B), "bo": (128, B), "boh": (128, H), "bk": (256, B), "bob": (128, B),
     "sel": (16, B), "Q": (288, B), "ST": (2048, H), "pi": (4, I), "pf": (12, F), "ar": (256, F), "oh16": (16, F),
-    "ncse": (128, B), "mA": (144, B), "csh": (128, H), "rst": (128, F), "jrow": (128, B), "p0": (128, B), "qrow": (128, B),
-    "Dm": (256, H), "ih": (384, H), "ii": (72, I), "cu": (72, U), "r0": (288, B),
+    "ncse": (128, B), "mA": (144, B), "csh": (128, H), "rst": (128, F), "jrow": (128, B), "p0": (144, B),
+    "Dm": (256, H), "ih": (512, H), "ii": (72, I), "cu": (72, U),
     "wr32": (256, F), "wrb": (256, B), "nthr": (256, B), "wC": (32, F), "dL": (240, F), "dW": (128, F),
     "dX": (12, F), "mk": (512, F), "need": (8, F),
     "hoff": (80, U), "Lu": (256, U), "nL": (1280, H), "dd": (4096, B), "da": (4096, B), "h32": (1024, F), "ag": (1024, B),
-    "xr": (4096, B), "pm": (256, F), "u0": (260, B), "u1": (260, B), "zb": (512, F), "Mh": (256, H), "rr": (1040, B),
-    "es": (256, F), "eoff": (80, U), "ev": (144, H), "eF": (80, F), "hr": (1024, H), "hs": (1024, H), "hC": (80, F),
+    "xr": (4096, B), "pm": (256, F), "uu": (1032, B), "zb": (512, F), "Mh": (576, H), "nA": (152, H), "dv": (2176, H), "eT": (96, F), "Lu0": (256, U),
+    "es": (256, F), "eoff": (80, U), "eF": (80, F), "hr": (1024, H), "hs": (1024, H), "hC": (80, F),
     "E0": (272, F), "H5": (272, F), "E": (2176, B), "vg": (512, B), "sg": (1024, B), "fl": (64, F), "un": (64, H),
     "sv": (64, F), "pd": (80, F), "gt": (80, F), "wu": (16, F), "s1": (80, F), "s2": (80, F), "s3": (80, F), "s4": (80, F),
-    "s5": (128, F), "s6": (128, F), "oL": (64, U), "oP": (80, U), "oW": (64, U), "t1": (1280, F), "t2": (1280, F),
-    "prb": (256, B), "jk": (768, B), "ac": (4, F), "uo": (32, U), "rb": (4, B), "ri": (4, I),
+    "s5": (128, F), "s6": (128, F), "oL": (64, U), "oP": (80, U), "oW": (64, U), "nc": (1280, F),
+    "prb": (256, B), "jk": (768, B), "r3": (768, B), "ac": (4, F), "uo": (32, U), "rb": (4, B), "ri": (4, I),
     "rq0": (56, U), "rq1": (56, U), "lq0": (56, U), "lq1": (56, U), "rs0": (48, B), "rs1": (48, B),
     "ls0": (48, B), "ls1": (48, B), "xs0": (48, B), "yh": (144, H), "y1": (48, F), "y2": (48, F), "y3": (48, F),
     "zz": (20, F), "dx": (48, B), "fr": (48, F), "xq": (96, B), "bb": (144, B), "E2": (288, B),
@@ -36,13 +36,14 @@ for _k in PS:
 NDMA, NREM = 12, 6
 SEMAPHORES = ["cD", "cA", "cP", "cG"] + ["dm%d" % k for k in range(NDMA)] + ["ar%d" % k for k in range(NREM)] + ["lc"]
 SIZE = {F: 4, I: 4, B: 2, H: 2, U: 2}
-COSTS = [dict(cyc=0.83, g=1.56, sc=3.8, pe=0.45, hop=200.0, rem=3000.0, fix=10.0, pfix=4.0, bw=200.0),
-         dict(cyc=0.83, g=1.3, sc=2.5, pe=0.42, hop=260.0, rem=2500.0, fix=0.0, pfix=0.0, bw=350.0),
-         dict(cyc=0.9, g=1.56, sc=3.8, pe=0.5, hop=150.0, rem=2000.0, fix=25.0, pfix=0.0, bw=300.0),
-         dict(cyc=1.1, g=1.9, sc=5.0, pe=0.6, hop=220.0, rem=4000.0, fix=10.0, pfix=4.0, bw=200.0)]
+COSTS = [dict(cyc=0.83, g=1.56, sc=3.8, pe=0.43, hop=220.0, rem=2200.0, fix=0.0, afix=30.0, pfix=2.0, bw=380.0),
+         dict(cyc=0.83, g=1.3, sc=2.5, pe=0.42, hop=270.0, rem=2000.0, fix=0.0, afix=30.0, pfix=0.0, bw=330.0),
+         dict(cyc=1.0, g=1.4, sc=4.5, pe=0.52, hop=180.0, rem=1800.0, fix=5.0, afix=30.0, pfix=0.0, bw=450.0),
+         dict(cyc=1.2, g=1.9, sc=3.5, pe=0.6, hop=240.0, rem=3000.0, fix=0.0, afix=30.0, pfix=4.0, bw=250.0)]
+DFIX = 1300.0
 RND = 1.5 * 2 ** 23
 NLOAD = 7
-TRIES, SEED, TEMP = 30000, 1, 8.0
+TRIES, SEED, TEMP = 55000, 5, 8.0
 
 
 def v(name, lo=0, hi=None, step=1, p=None):
@@ -90,7 +91,6 @@ def regs(*xs):
 
 def program(c):
     ops, tag = [], ["", 0]
-    NC, NB = PRM["NC"], PRM["NB"]
 
     def add(eng, fn, out, ins, cost, lat=0.0, kind="c", extra=()):
         W = [out[1]] if out[0] == "I" else [out]
@@ -139,7 +139,7 @@ def program(c):
             if accum is not None:
                 kw["accum_out"] = ap(T, accum)
             return g.scalar.activation(ap(T, out), ap(T, a), func, **kw)
-        k = vcost(out, a, [], fix=65.0) if "I" in (out[0], a[0]) else max(64, cnt(out)) * c["cyc"] + 30
+        k = vcost(out, a, [], fix=65.0) if "I" in (out[0], a[0]) else max(64, cnt(out)) * c["cyc"] + c["afix"]
         add("A", fn, out, [a, bias], k + more, extra=[accum] if accum else [])
 
     def mm(lst):
@@ -157,6 +157,9 @@ def program(c):
 
     def asel(out, a, pat, cmp, base, ch):
         add("G", lambda g, T, x: g.affine_select(ap(T, out), ap(T, a), pat, cmp, 0.0, base, ch), out, [a], 170 + 2 * cnt(out) * c["cyc"])
+
+    def gcp(out, a):
+        asel(out, a, [[0, cnt(out)]], OP.is_ge, 0, 0)
 
     def load(q, out, src, nbytes):
         add(q, lambda g, T, x: (g.sync if q == "S" else g.scalar).dma_start(ap(T, out), src(T)), out, [], 60.0, lat=nbytes, kind="d")
@@ -201,14 +204,22 @@ def program(c):
     cp(v("wc"), v("wi"))
     for b in range(8):
         mm([(v(PS[b], 192 * k, 192 * k + 192), v("ST", 128 * (2 * b + k), 128 * (2 * b + k + 1)), v("wc"), True, True) for k in range(2)])
-        act(v("W", 384 * b, 384 * b + 384), v(PS[b], 0, 384), AF.Identity, bias=32.0)
+        if b < PRM["WV"]:
+            cp(v("W", 384 * b, 384 * b + 384), v(PS[b], 0, 384))
+        else:
+            act(v("W", 384 * b, 384 * b + 384), v(PS[b], 0, 384), AF.Copy)
     cp(v("hou"), v("hoi"))
-    for k in range(2):
-        ts(v("L", 1024 * k, 1024 * k + 1024), v("Li", 1024 * k, 1024 * k + 1024), -1024.0, OP.add)
+    for k in range(0, NHD * (not PRM["GCV"]), 1024):
+        cp(v("L", k, k + 1024), v("Li", k, k + 1024))
 
 
     def lin(out, a, scale, bias=None):
-        act(out, a, AF.Copy if bias is None else AF.Identity, bias=bias, scale=scale)
+        if cnt(out) > PRM["LINV"]:
+            act(out, a, AF.Copy if bias is None else AF.Identity, bias=bias, scale=scale)
+        elif bias is None:
+            ts(out, a, scale, OP.mult)
+        else:
+            ts(out, a, scale, OP.mult, bias, OP.add)
 
     def fill(out, val):
         lin(out, v("ones", 0, cnt(out)), val)
@@ -223,14 +234,16 @@ def program(c):
         lin(v("jk", 256 + 144 * k, 400 + 144 * k), v("mA"), f)
     tt(v("csh"), v("jk", 272, 400), v("jk", 415, 543), OP.subtract)
     tt(v("ncse"), v("jk", 559, 687), v("jk", 272, 400), OP.subtract)
-    fill(v("r0", 0, 144), 8192.0)
-    asel(v("r0", 144, 288), v("r0", 0, 144), [[0, 9], [1, 16]], OP.is_ge, -1, 0)
-    asel(v("p0"), v("r0", 0, 128), [[0, 8], [1, 16]], OP.is_equal, 0, 0)
-    lin(v("rst"), v("p0"), 1.0)
-    lin(v("qrow"), v("p0"), 0.5, -3072.0)
+    asel(v("p0"), v("ones", 0, 144), [[0, 9], [1, 16]], OP.is_equal, 0, 0)
+    lin(v("rst"), v("p0", 0, 128), 8192.0)
+    if PRM["MHS"]:
+        tt(v("es", 0, 144), v("mA"), v("p0"), OP.max)
+        ts(v("nA", 0, 144), v("es", 0, 144), -1.0, OP.mult, 1.0, OP.add)
+        ts(v("nA", 144, 152), v("bo", 0, 128, 16), -1.0, OP.mult)
+        ms(v("Mh"), 0.0)
     lin(v("jrow"), v("ar", 0, 128), 1.0 / 32)
     lin(v("nidn"), v("idn"), -1.0)
-    for k, f in enumerate((1.0 / 128, 1.0, -1.0)):
+    for k, f in enumerate((1.0 / 128, 1.0, -1.0, -0.5)):
         ts(v("ih", 128 * k, 128 * k + 128), v("idn"), f, OP.mult)
     ms(v("Dm"), 0.0)
     tt(v("Dm", 0, 256, 2), v("idn"), v("jk", 128, 256), OP.subtract)
@@ -240,15 +253,15 @@ def program(c):
         lin(v("bk", 128 * k - 128, 128 * k), v("bo"), 1.7 ** (-16 * k))
     lin(v("sel", 0, 8), v("bo", 0, 128, 16), 1.0)
     lin(v("sel", 8, 16), v("bo", 0, 128, 16), -1.0)
-    fill(v("Q"), 0.0)
+    iota(v("Q"), [[0, 288]], 0, 0)
     lin(v("Q", 15, 143, 16), v("bo", 0, 128, 16), 1.0)
     lin(v("Q", 159, 287, 16), v("bo", 0, 128, 16), -1.0)
     cp(v("cu", 0, 56), v("ii", 0, 56))
     ts(v("cu", 56, 62), v("ar", 0, 96, 16), pa, OP.add)
     fill(v("mk", 0, 256), 1.0)
-    fill(v("mk", 256, 512), 20.0)
-    fill(v("t1", 0, 256), 1.0 / 1.7)
-    scan(v("wr32"), v("t1", 0, 256), v("mk", 0, 256), 1.7 ** 129, OP.mult, OP.mult)
+    iota(v("mk", 256, 512), [[0, 256]], 20, 0)
+    fill(v("nc", 0, 256), 1.0 / 1.7)
+    scan(v("wr32"), v("nc", 0, 256), v("mk", 0, 256), 1.7 ** 129, OP.mult, OP.mult)
     lin(v("wrb"), v("wr32"), 1.0)
     lin(v("nthr"), v("wrb"), -2.56)
 
@@ -267,9 +280,15 @@ def program(c):
     lin(v("dW", 0, 64), v("dL", 0, 64), 1.0, 1024.0)
     lin(v("dW", 64, 128), v("dL", 0, 64), 64.0, 65536.0)
     lin(v("dX", 0, 6), v("dL", 0, 6), 1.0, 1024.0)
-    lin(v("dX", 8, 11), v("dL", 0, 3), -1.0, 2047.5)
+    if PRM["LA"]:
+        lin(v("dX", 8, 11), v("dL", 0, 3), 1.0, -2047.5)
+        iota(v("r3"), [[0, 768]], 1, 0)
+        iota(v("r3", 0, 768, 256), [[0, 3]], 0, 0)
+    else:
+        if PRM["FAST"]:
+            iota(v("r3", 0, 512), [[0, 512]], 0, 0)
+        lin(v("dX", 8, 11), v("dL", 0, 3), -1.0, 2047.5)
     iota(v("V", 0, NHD), [[0, NHD]], 0, 0)
-    iota(v("IT"), [[1, NP]], 0, 0)
     fill(v("need", 0, 1), 8.5)
     fill(v("need", 2, 3), 88.5)
     fill(v("need", 4, 5), 1.0)
@@ -278,9 +297,10 @@ def program(c):
         iota(v(k, 528, 544), [[0, 16]], 300, 0)
     iota(v("E0", 256, 272), [[0, 16]], -2500, 0)
     iota(v("H5", 256, 272), [[0, 16]], 0, 0)
-    for k in ("u0", "u1"):
-        fill(v(k), 1.0)
-    iota(v("rr", 0, 16), [[0, 16]], 8192, 0)
+    for k in range(2):
+        iota(v("uu", 516 * k, 516 * k + 516), [[0, 516]], 1, 0)
+    for k in range(4):
+        ms(v("dv", 544 * k, 544 * k + 288), 0.0)
     iota(v("gt", 64, 80), [[0, 16]], 0, 0)
     iota(v("s5", 48, 64), [[0, 16]], 0, 0)
     ms(v("un", 0, 16), -64.0)
@@ -294,8 +314,8 @@ def program(c):
     def rep16(k):
         return v("cu", 56, 56 + k)
 
-    def nearest(hf, base, ns, nc, nl):
-        pk, u, o = PS[2 + hf], "u%d" % hf, 128 * hf
+    def nearest(hf, base, ns, nc, nl, u):
+        pk, o = PS[2 + hf], 128 * hf
         key, pm, z = v(pk, 0, 128), v("pm", o, o + 128), v("zb", 2 * o, 2 * o + 256)
         mm([(v(pk, 128, 384, 1, (0, ns)), nl, v("Dm"), True, True)])
         jr = (key, one1, v("jrow", 0, 128, 1, (0, 1)))
@@ -307,47 +327,60 @@ def program(c):
             mm([(v(pk, j, 128, 16, (a, b)), v("da", base + 16 * a + j, base + 16 * b, 16), v("sel", 0, 8), False, False) for j in range(16)] +
                ([jr + (False, True)] if b == ns else []))
         scan(pm, v("rst"), key, 0.0, OP.add, OP.min)
-        tt(v(u, 0, 256, 2), key, pm, OP.is_gt)
-        scan(z, v(pk, 128, 384), v(u, 0, 256), 0.0, OP.add, OP.mult)
-        tt(v("Mh", o, o + 128), ind(z, v("cu", 0, 8)), v("mA", 0, 128), OP.mult)
+        tt(v("uu", u, u + 256, 2), key, pm, OP.is_gt)
+        scan(z, v(pk, 128, 384), v("uu", u, u + 256), 0.0, OP.add, OP.mult)
         ec = v(pk, 384, 384 + ns // 16)
-        mm([(ec, v("Mh", o, o + 128, 1, (0, ns)), v("boh", 0, ns, 16, (0, ns)), True, True)])
+        r, d = 16 + 144 * hf, 304 + 144 * hf
+        if ns < 128 or not PRM["MHS"]:
+            tt(v("Mh", r, r + 128), ind(z, v("cu", 0, 8)), v("mA", 0, 128), OP.mult)
+            mm([(ec, v("Mh", r, r + 128, 1, (0, ns)), v("boh", 0, ns, 16, (0, ns)), True, True)])
+            return ec
+        cp(v("Mh", d + 15, d + 128, 16), v("zb", 2 * o + 31, 2 * o + 256, 32))
+        scan(v("Mh", r, r + 128, 1, "back"), v("nA", 1, 129, 1, "back"), v("Mh", d, d + 128, 1, "back"), 0.0, OP.mult, OP.add)
+        mm([(ec, v("Mh", r, r + 128), v("boh", 0, 128, 16), True, False), (ec, v("Mh", r - 1, r + 127), v("nA", 144, 152), False, False),
+            (ec, v("Mh", d - 1, d + 127), v("boh", 0, 128, 16), False, True)])
         return ec
 
     def after_e(i, hf):
         o, oc = 256 * i + 128 * hf, 16 * i + 8 * hf
         eo = v("eoff", oc, oc + 8)
-        if i < 4 and PRM["WGA"]:
-            act(v("h32", o, o + 128), ind(Ww, eo), AF.Copy)
-            ts(v("hr", o, o + 128), v("h32", o, o + 128), RND - 32.0, OP.add, -RND, OP.add)
-            scan(v("hs", o, o + 128), v("csh"), v("hr", o, o + 128), 0.0, OP.add, OP.min)
-            ts(v("hoff", oc + 16, oc + 24), v("hs", o + 15, o + 128, 16), fixh, OP.add)
-        elif i < 4:
-            ts(v("hr", o, o + 128), ind(Ww, eo), RND - 32.0, OP.add, -RND, OP.add)
+        if i < 4:
+            ts(v("hr", o, o + 128), ind(Ww, eo), RND, OP.add, -RND, OP.add)
             scan(v("hs", o, o + 128), v("csh"), v("hr", o, o + 128), 0.0, OP.add, OP.min)
             ts(v("hoff", oc + 16, oc + 24), v("hs", o + 15, o + 128, 16), fixh, OP.add)
         else:
-            act(v("H5", 128 * hf, 128 * hf + 128), ind(Ww, eo), AF.Identity, bias=-32.0)
+            act(v("H5", 128 * hf, 128 * hf + 128), ind(Ww, eo), AF.Copy)
 
     def chunks(lo, hi, k):
         m = (hi - lo + k - 1) // k
         return [(lo + (hi - lo) * q // m // 2 * 2, lo + (hi - lo) * (q + 1) // m // 2 * 2) for q in range(m)] if m else []
 
-    def columns(t, l0, l1):
-        w = 256 * (l1 - l0)
-        half = (v("pm0", 0, w), v("qrow", 0, 128, 1, (0, 1)), v("ones", 0, w, 1, (0, 1)))
+    def at15(k):
+        return v("dv", 544 * k + 31, 544 * k + 272, 16)
+
+    def spread(k, l):
+        u = 516 * (l % 2)
+        scan(v("dv", 544 * k + 288, 544 * k + 544, 1, "back"), v("uu", u + 2, u + 514, 2, "back"), v("dv", 544 * k + 16, 544 * k + 272, 1, "back"),
+             0.0, OP.mult, OP.add)
+
+    def columns(t, levels):
+        w, l0 = 256 * len(levels), levels[0][0]
+        half = (v("pm0", 0, w), v("ih", 384, 512), v("nL", 256 * l0, 256 * l0 + w))
         lst = [half + (True, False)]
-        for l in range(l0, l1):
+        for l, new, old in levels:
             for hf in range(2):
-                nm, o = ("rr", 16 + 256 * (l - 1) + 128 * hf) if l else ("r0", 144 * t + 16)
                 out = v("pm0", 256 * (l - l0) + 128 * hf, 256 * (l - l0) + 128 * hf + 128)
-                lst += [(out, v(nm, o, o + 128), v("idn"), False, False), (out, v(nm, o - 1, o + 127), v("nidn"), False, False)]
-        mm(lst)
-        mm([(v("pm0", a, w, 16), ST(a), v("ev", 16 * l0, 16 * l1), False, False) for a in range(16)] + [half + (False, True)])
-        for l in range(l0, l1):
-            q = v("pm0", 256 * (l - l0), 256 * (l - l0 + 1))
-            tt(v("t1", 256 * l, 256 * l + 256), v("nL", 256 * l, 256 * l + 256), q, OP.max)
-        act(v("t2", 256 * l0, 256 * l1), v("pm0", 0, w), AF.Relu, bias=-2048.0, scale=2.0)
+                for k, p, m in ((new, 128, 256), (old, 256, 128)):
+                    d, r = 544 * k + 16 + 128 * hf, 544 * k + 288 + 128 * hf
+                    for o, sign in ((r, p), (r - 1, m), (d - 1, p)) if l else ((d + 15 - t, p),):
+                        lst.append((out, v("dv", o, o + 128), v("ih", sign, sign + 128), False, False))
+                mm(lst)
+                lst = []
+        mm([half + (False, True)])
+        if l0 < 3 or not PRM["LA"]:
+            act(v("nc", 256 * l0, 256 * l0 + w), v("pm0", 0, w), AF.Identity, bias=1024.0)
+        else:
+            ts(v("nc", 256 * l0, 256 * l0 + w), v("pm0", 0, w), 1024.0, OP.add)
 
     for t in range(2):
         need, need80 = v("need", t, t + 1), v("need", 2 + t, 3 + t)
@@ -355,12 +388,16 @@ def program(c):
         tag[:] = ["first", 10 * t]
         mark = v("mk", 256 * t, 256 * t + 256)
         h0 = v("hou", 16 * t, 16 * t + 16)
-        cp(v("hC", 0, 16), v("hoi", 16 * t, 16 * t + 16))
+        gcp(v("hC", 0, 16), v("hoi", 16 * t, 16 * t + 16))
         act(ind(v("V"), h0), mark, AF.Silu, more=1300.0 if t == 0 else 0.0)
-        if t == 0:
-            ts(v("nL", 0, 256), ind(v("Li"), h0), -1.0, OP.mult, 1024.0, OP.add)
+        if t:
+            ops[-1]["R"].append(v("oP"))
+        lists = Lw if t else v("Li")
+        if t and PRM["LA"]:
+            ts(v("Lu0"), ind(lists, h0), 0.0, OP.add)
+            ts(v("nL", 0, 256), v("Lu0"), -1.0, OP.mult, 1024.0, OP.add)
         else:
-            ts(v("nL", 0, 256), ind(Lw, h0), -1.0, OP.mult)
+            ts(v("nL", 0, 256), ind(lists, h0), -1.0, OP.mult, 1024.0, OP.add)
         for hf in range(2):
             o, er = 128 * hf, v(PS[2 + hf], 384, 512)
             mm([(er, ST(t), v("nL", o, o + 128), True, True)])
@@ -370,23 +407,39 @@ def program(c):
             after_e(0, hf)
             act(v(xd, o, o + 128), ind(Xw, eo), AF.Copy)
             act(v("E0", o, o + 128), er, AF.Copy)
-        for k in (64, 80):
-            ts(v("ev", k, k + 16), v("eoff", 0, 16), -1024.0, OP.add)
+        mm([(v("pdd", 48 + 8 * hf, 56 + 8 * hf), v("nL", 128 * hf, 128 * hf + 128), v("ST", 128 * t, 128 * t + 128, 16), True, True) for hf in range(2)])
+        e0T, zend = v("eT", 0, 16), v("zb", 31, 512, 32)
+        lin(e0T, v("pdd", 48, 64), -1.0)
+        for k in (0, 3):
+            gcp(at15(k), e0T)
         send(3 * t, v(lx), v(xd), t + 1, 2000.0)
         for j in range(32):
             hf, j = j // 16, j % 16
             o, a = v("xr", 2048 * hf + j, 2048 * hf + 2048, 16), v(xd, 128 * hf, 128 * hf + 128)
-            if j < PRM["REPA"]:
+            if j < PRM["REPA"][2 * t + hf]:
                 act(o, a, AF.Copy)
+            elif hf and j >= 16 - PRM["REPG"]:
+                asel(o, a, [[0, 128]], OP.is_ge, 0, 0)
             else:
                 cp(o, a)
+        if t == 0:
+            for k in range(0, NP, 1024):
+                iota(v("IT", k, k + 1024), [[1, 1024]], k, 0)
+                ops[-1]["R"].append(v("xr"))
+            for k in range(0, NHD * PRM["GCV"], 1024):
+                asel(v("L", k, k + 1024), v("Li", k, k + 1024), [[0, 1024]], OP.is_ge, 0, 0)
+                ops[-1]["R"].append(v("xr"))
         for i in range(1, 5):
             q = 16 * i
+            NC, NB = PRM["NC"][4 * t + i - 1], PRM["NB"][4 * t + i - 1]
             tag[:] = ["death", 10 * t + i]
             hC = v("hC", q, q + 16)
             so, vg = 512 * (i % 2), v("vg", 256 * (i % 2), 256 * (i % 2) + 256)
             hs, un = v("hs", 256 * i - 241, 256 * i, 16), v("un", q - 16, q)
-            ts(hC, hs, fixh, OP.add)
+            if PRM["HG"]:
+                gcp(hC, v("hoff", q, q + 16))
+            else:
+                ts(hC, hs, fixh, OP.add)
             act(vg, ind(v("V", 0, NHD), v("hoff", q, q + 16)), AF.Relu, bias=-0.25 - 0.75 * t)
             lst, o = [], 0
             for cc in range(16):
@@ -409,7 +462,7 @@ def program(c):
                 o = 128 * hf
                 tag[0] = "near%d" % hf
                 ho = v("hoff", q + 8 * hf, q + 8 * hf + 8)
-                ts(v("Lu", o, o + 128), ind(Lw if t or i > 1 else v("Li"), ho), 1024.0 if t or i > 1 else 0.0, OP.add)
+                ts(v("Lu", o, o + 128), ind(lists, ho), 0.0, OP.add)
                 nl = v("nL", 256 * i + o, 256 * i + o + 128)
                 ts(nl, v("Lu", o, o + 128), -1.0, OP.mult, 1024.0, OP.add)
                 for a, b in chunks(o + 128 - NB, o + 128, PRM["C3"]):
@@ -418,7 +471,11 @@ def program(c):
                     w = 16 * (b - a)
                     ag = v("ag", 512 * r, 512 * r + w)
                     act(ag, ind(Xw, v("Lu", a, b)), AF.Copy)
-                    mm([(v(PS[r], 0, w), v("nidn"), v("xr", 16 * a, 16 * b), True, False)])
+                    if i == 1 and hf < PRM["FAST"]:
+                        mm([(v(PS[r], 0, w), v("Q", 16, 144, 1, (0, 1)), v("r3", 0, w, 1, (0, 1)), True, False)])
+                        mm([(v(PS[r], j, w, 16), v("nidn"), v(xd, a, b), False, False) for j in range(16)])
+                    else:
+                        mm([(v(PS[r], 0, w), v("nidn"), v("xr", 16 * a, 16 * b), True, False)])
                     mm([(v(PS[r], 0, w), v("idn"), ag, False, True)])
                     act(v("da", 16 * a, 16 * b), v(PS[r], 0, w), AF.Abs)
                 for a, b in chunks(o + NC, o + 128 - NB, PRM["C1"]) + chunks(o, o + NC, PRM["C1"]):
@@ -429,11 +486,9 @@ def program(c):
                     else:
                         act(v("da", 16 * a, 16 * b), d, AF.Abs)
                 tag[0] = "chain%d" % hf
-                ec = nearest(hf, 16 * o, 128, NC, nl)
+                ec = nearest(hf, 16 * o, 128, NC, nl, 516 * (i % 2) + 2 * o)
                 ts(v("eoff", q + 8 * hf, q + 8 * hf + 8), ec, 1024.0, OP.add)
                 after_e(i, hf)
-                r = 16 + 256 * (i - 1) + o
-                scan(v("rr", r, r + 128, 1, "back"), v("u%d" % hf, 2, 258, 2, "back"), v("p0"), 0.0, OP.mult, OP.max)
             tag[0] = "paid"
             m = PRM["SG4"] if i == 4 else 1
             sga = PRM["SGA"] and i < 4
@@ -447,10 +502,12 @@ def program(c):
                     tt(v("sg", so + 256 + a, so + 256 + b), ind(Xw, v("eoff", q + a // 16, q + b // 16)), v(xd, 272 + a, 272 + b), OP.is_ge)
             if i < 4:
                 lst = [(v("pdd", 0, 32), S(a), v("sg", so + a, so + 512, 16), a == 0, a == 15) for a in range(16)]
-                mm(lst[:1] + [(v("pdd", 0, 16), v("ih", 0, 128), hs, False, False), (v("pdd", 0, 16), v("ih", 128, 256), un, False, False)] + lst[1:])
+                mm(lst[:1] + [(v("pdd", 0, 16), v("ih", 0, 128), hs, False, False), (v("pdd", 0, 16), v("ih", 128, 256), un, False, False)] + lst[1:] +
+                   [(v("pdd", 32 + 8 * hf, 40 + 8 * hf), v("sg", so + 256 + 128 * hf, so + 384 + 128 * hf), v("sel", 0, 8), True, True) for hf in range(2)])
                 sv, fl = v("sv", q, q + 16), v("fl", q, q + 16)
                 ts(sv, v("pdd", 0, 16), thr, OP.is_lt, -64.0, OP.mult)
                 ts(fl, v("pdd", 16, 32), v("need", 4 + t, 5 + t) if sga else need, OP.is_lt)
+                ts(v("eT", 16 + q, 32 + q), v("pdd", 32, 48), v("need", 4 + t, 5 + t) if sga else need, OP.is_lt)
                 tt(v("s2", 0, 16), v("pdd", 0, 16), v("dL", 160 + q, 176 + q), OP.min)
                 ts(v("oL", q, q + 16), v("s2", 0, 16), cpc, OP.add, 128.0, OP.mult)
                 act(ind(v("V"), v("oL", q, q + 16)), mark, AF.Silu)
@@ -461,24 +518,34 @@ def program(c):
                 mm([(v("pdd", 0, 16), S(a), v("sg", so + 256 + a, so + 512, 16), False, a == 15) for a in range(16)])
                 ts(v("pd", 64, 80), v("pdd", 0, 16), need80, OP.is_ge, -64.0, OP.mult)
             tag[0] = "cols"
-            k = (0, 96, 112, 128)[i - 1]
-            ts(v("ev", k, k + 16), v("eoff", q, q + 16), -1024.0, OP.add)
             if i == 1:
-                columns(t, 0, 1)
-            if i >= 3:
-                l, w = (1, 32) if i == 3 else (3, 16)
-                tt(v("s3", 0, w), v("ev", 80 + 16 * l, 80 + 16 * l + w), v("ev", 64, 64 + w), OP.subtract)
-                tt(v("s3", 32, 32 + w), v("s3", 0, w), v("fl", 16 * l, 16 * l + w), OP.mult)
-                tt(v("ev", 16 * l, 16 * l + w), v("s3", 32, 32 + w), v("ev", 64, 64 + w), OP.add)
-                columns(t, l, l + 2)
+                gcp(at15(2), zend)
+            else:
+                tt(v("s3", 0, 16), zend, e0T, OP.subtract)
+                tt(v("s3", 16, 32), v("s3", 0, 16), v("eT", q, q + 16), OP.mult)
+                tt(at15(2), v("s3", 16, 32), e0T, OP.add)
+                spread(2, i - 1)
+            if i < 4:
+                columns(t, [(i - 1, 2, (i - 1) % 2)])
+            (gcp if i < 4 else cp)(at15(i % 2), zend)
+            spread(i % 2, i)
+            if i == 4:
+                spread(3, 4)
+                columns(t, [(3, 2, 1), (4, 3, 0)])
         tag[:] = ["send", 10 * t + 5]
         rq, lq, rs, ls = "rq%d" % t, "lq%d" % t, "rs%d" % t, "ls%d" % t
         ts(v("vg", 0, 256), v("pm1", 0, 256), 80.0, OP.add, need, OP.is_lt)
         scan(v("prb"), v("ones", 0, 256), v("vg", 0, 256), 0.0, OP.mult, OP.add)
-        for k in range(3):
-            act(v("jk", 256 * k, 256 * k + 256), v("prb"), AF.Sign, bias=v("dX", 8 + k, 9 + k), accum=v("ac", k, k + 1))
         ix = v(rq, 4, 7)
-        ts(ix, v("ac", 0, 3), -0.5, OP.mult, 128.0, OP.add)
+        if PRM["LA"]:
+            for k in range(3):
+                ts(v("jk", 256 * k, 256 * k + 256), v("prb"), v("dX", 8 + k, 9 + k), OP.is_lt)
+            scan(v("E", 0, 768), v("r3"), v("jk"), 0.0, OP.mult, OP.add)
+            cp(ix, v("E", 255, 768, 256))
+        else:
+            for k in range(3):
+                act(v("jk", 256 * k, 256 * k + 256), v("prb"), AF.Sign, bias=v("dX", 8 + k, 9 + k), accum=v("ac", k, k + 1))
+            ts(ix, v("ac", 0, 3), -0.5, OP.mult, 128.0, OP.add)
         ts(v("yh", 0, 48), ind(v("H5"), ix), RND, OP.add, -RND, OP.add)
         scan(v("yh", 48, 96), v("csh", 0, 48), v("yh", 0, 48), 0.0, OP.add, OP.min)
         ts(v(rq, 0, 3), v("yh", 48 + 15, 96, 16), fixh, OP.add)
@@ -493,7 +560,7 @@ def program(c):
         cp(eo0, v("z1", 0, 3))
         tag[0] = "payl"
         tt(v("pd", 16, 64), v("sv", 16, 64), v("un", 16, 64), OP.subtract)
-        cp(v("gt", 48, 64), v("pd", 48, 64))
+        gcp(v("gt", 48, 64), v("pd", 48, 64))
         tt(v("gt", 32, 48), v("pd", 32, 48), v("pd", 48, 64), OP.add)
         for k in (16, 0):
             tt(v("gt", k, k + 16), v("gt", 32, 48), v("pd", 16, 32), OP.add)
@@ -506,12 +573,16 @@ def program(c):
         ts(v("oP"), v("s4"), 1.0 / 64, OP.mult)
         a = 0
         for k in PRM["LCH"]:
-            tt(ind(v("L"), v("oP", a, a + k)), v("t2", 16 * a, 16 * (a + k)), v("t1", 16 * a, 16 * (a + k)), OP.subtract)
+            if PRM["LA"]:
+                act(ind(v("L"), v("oP", a, a + k)), v("nc", 16 * a, 16 * (a + k)), AF.Silu)
+            else:
+                cp(ind(v("L"), v("oP", a, a + k)), v("nc", 16 * a, 16 * (a + k)))
             a += k
         tag[0] = "payw"
-        for k in range(0, 64 * (not PRM["WGA"]), 16):
-            act(v("h32", 16 * k, 16 * k + 256), ind(Ww, v("eoff", k, k + 16)), AF.Copy)
-        cp(v("eF"), v("eoff"))
+        for k in range(0, 64, 16):
+            gcp(v("h32", 16 * k, 16 * k + 256), v("hr", 16 * k, 16 * k + 256))
+        gcp(v("eF", 0, 64), v("eoff", 0, 64))
+        gcp(v("eF", 64, 80), v("eoff", 64, 80))
         tt(v("s5", 64, 128), v("dW", 0, 64), v("eF", 16, 80), OP.subtract)
         tt(v("s6", 64, 128), ind(v("eF", 0, 16), rep16(4)), v("dW", 0, 64), OP.subtract)
         tt(v("s5", 0, 48), ind(pd4, rep16(3)), v("gt", 32, 80), OP.add)
@@ -534,22 +605,25 @@ def program(c):
             lin(v("need", 3, 4), v("need", 1, 2), 1.0, 80.0)
             lin(v("need", 5, 6), v("need", 1, 2), 2.0, -16.0)
         else:
-            act(v("Lo", 0, 1024), v("L", 0, 1024), AF.Identity, bias=1024.0)
-            act(v("Lo", 1024, 2048), v("L", 1024, 2048), AF.Identity, bias=1024.0)
-            store("S", lambda T: T.yl[:], v("Lo"), 1048e3)
+            for k in range(0, NHD * PRM["LA"], 256):
+                ts(v("V", k, k + 256), v("L", k, k + 256), RND, OP.add, -RND, OP.add)
+            store("S", lambda T: T.yl[:], v("V", 0, NHD) if PRM["LA"] else Lw, 1048e3)
             wf, w8 = v("wr32", 0, 192), v("W", 0, NP, 1, (0, 128, 16))
             add("S", lambda g, T, x: g.sync.dma_start(ap(T, wf), ap(T, w8)), wf, [w8], 60.0, lat=98e3, kind="d")
-            ts(wf, wf, RND - 32.0, OP.add, -RND, OP.add)
+            ts(wf, wf, RND, OP.add, -RND, OP.add)
             store("S", lambda T: T.yw[:], wf, 98e3)
         tag[0] = "came"
         hq, ixc = v(lq, 0, 3), v(lq, 4, 7)
-        ts(v("Lu", 0, 48), ind(Lw, hq), 1024.0, OP.add)
+        ts(v("Lu", 0, 48), ind(Lw, hq), 0.0, OP.add)
         nl = v("yh", 96, 144)
         ts(nl, v("Lu", 0, 48), -1.0, OP.mult, 1024.0, OP.add)
         qc = PRM["QC"]
         for a, b in chunks(qc, 48, 16) + chunks(0, qc, 16):
             xr, d = v("xr", 16 * a, 16 * b), v("dd", 16 * a, 16 * b)
-            act(xr, ind(v(lx, 0, 272), v(lq, 8 + a, 8 + b)), AF.Copy)
+            if a >= PRM["XV"]:
+                cp(xr, ind(v(lx, 0, 272), v(lq, 8 + a, 8 + b)))
+            else:
+                act(xr, ind(v(lx, 0, 272), v(lq, 8 + a, 8 + b)), AF.Copy)
             tt(d, ind(Xw, v("Lu", a, b)), xr, OP.subtract)
             if a < qc:
                 ts(v("da", 16 * a, 16 * b), d, 0.0, OP.max, 2.0, OP.mult)
@@ -558,7 +632,7 @@ def program(c):
         xq, dq = v("xq", 0, 48), v("xq", 48, 96)
         act(xq, ind(v(lx, 0, 272), ixc), AF.Copy)
         act(dq, ind(v(lx, 272, 544), ixc), AF.Copy)
-        ec = nearest(0, 0, 48, qc, nl)
+        ec = nearest(0, 0, 48, qc, nl, 0)
         fo = v("uo", 12, 15)
         ts(fo, ec, 1024.0, OP.add)
         ts(v("fC", 0, 3), ec, 1024.0, OP.add)
@@ -635,14 +709,21 @@ def schedule(alts, deps, tries):
             succ[p].append(k)
     eng = ["DAPGS".index(o["e"]) for o in ops]
     dma = [o["kind"] == "d" for o in ops]
+    dmas = [k for k in range(n) if dma[k]]
+    pos = [0] * n
     pre = [[p for p in deps[k] if not (eng[p] == 2 and eng[k] == 2)] for k in range(n)]
     models = [([o["cost"] for o in a], [o["lat"] / c["bw"] if o["kind"] == "d" else o["lat"] + c["hop"] for o in a], c["hop"])
               for a, c in zip(alts, COSTS)]
 
-    def times(order, m):
+    def times(order, m, i=0, old=None):
         cost, lat, hop = models[m]
         free, rdy, st, dfree = [0.0] * 5, [0.0] * n, [0.0] * n, 0.0
-        for k in order:
+        if i:
+            st, rdy = list(old[1]), list(old[2])
+            for k in order[:i]:
+                free[eng[k]] = st[k] + cost[k]
+            dfree = max([rdy[k] - hop for k in dmas if pos[k] < i])
+        for k in order[i:]:
             e = eng[k]
             t = free[e]
             for p in pre[k]:
@@ -652,7 +733,7 @@ def schedule(alts, deps, tries):
             t += cost[k]
             free[e] = t
             if dma[k]:
-                dfree = max(dfree, t + 2000.0) + lat[k]
+                dfree = max(dfree, t + DFIX) + lat[k]
                 rdy[k] = dfree + hop
             else:
                 rdy[k] = t + lat[k]
@@ -663,7 +744,7 @@ def schedule(alts, deps, tries):
     def tails(order):
         tl, nx = [0.0] * n, [0.0] * 5
         for k in reversed(order):
-            la = lat[k] + (2000.0 + hop if dma[k] else 0.0)
+            la = lat[k] + (DFIX + hop if dma[k] else 0.0)
             t = la
             for s in succ[k]:
                 x = tl[s] + (0.0 if eng[k] == 2 and eng[s] == 2 else la)
@@ -723,7 +804,7 @@ def schedule(alts, deps, tries):
                     k = h
             r.remove(k)
             t = free[e] = max(est[k], free[e]) + cost[k]
-            rd[k] = t + lat[k] + (2000.0 + hop if dma[k] else 0.0)
+            rd[k] = t + lat[k] + (DFIX + hop if dma[k] else 0.0)
             done[k] = True
             out.append(k)
             for q in succ[k]:
@@ -732,11 +813,12 @@ def schedule(alts, deps, tries):
                     if not left[q]:
                         est[q] = max([rd[p] for p in pre[q]], default=0.0)
                         ready[eng[q]].append(q)
-        return out + [k for k in order[i:] if not done[k]]
+        return out + [k for k in order[i:] if not done[k]], i
 
-    def state(o, first):
-        ends = [first[0]] + [times(o, m)[0] for m in range(1, len(models))]
-        return [o, first[1], first[2], ends, (sum(ends) + ends[0]) / (len(ends) + 1), None]
+    def state(o, first, i=0, old=None):
+        tms = [first] + [times(o, m, i, old and old[m]) for m in range(1, len(models))]
+        ends = [x[0] for x in tms]
+        return [o, first[1], first[2], ends, (sum(ends) + ends[0]) / (len(ends) + 1), None, tms]
 
     rng = np.random.default_rng(SEED)
     names = sorted(set(o["W"][0][0] for o in ops))
@@ -746,12 +828,14 @@ def schedule(alts, deps, tries):
     pr = [0.0] * n
     for k in range(n - 1, -1, -1):
         pr[k] = cost[k] + max([pr[s] + lat[k] for s in succ[k]], default=0.0)
-    order = redo(order, [0.0] * n, times(order, 0)[2], -1.0, 1e17, pr, 0.3)
+    order = redo(order, [0.0] * n, times(order, 0)[2], -1.0, 1e17, pr, 0.3)[0]
     best = cur = state(order, times(order, 0))
     for it in range(tries):
         if cur[5] is None:
             cur[0] = sorted(cur[0], key=lambda k: cur[1][k])
             cur[5] = (np.array(cur[1]), np.array(tails(cur[0])))
+            for i, k in enumerate(cur[0]):
+                pos[k] = i
         st, tl = cur[5]
         lo = rng.random() * cur[3][0] - 2000
         hi = lo + 3000 + rng.random() * 11000
@@ -766,12 +850,12 @@ def schedule(alts, deps, tries):
             if u[3] < 0.6:
                 m &= kind == kind[k]
             pr[m] += rng.normal() * 1500
-        o = redo(cur[0], cur[1], cur[2], lo, hi, list(pr), rng.random() * 0.6)
+        o, i = redo(cur[0], cur[1], cur[2], lo, hi, list(pr), rng.random() * 0.6)
         lim = cur[4] - TEMP * (1 - it / tries) * math.log(rng.random())
-        f = times(o, 0)
+        f = times(o, 0, i, cur[6][0])
         if f[0] - cur[3][0] > lim - cur[4] + 400:
             continue
-        new = state(o, f)
+        new = state(o, f, i, cur[6])
         if new[4] <= lim:
             cur = new
             if cur[4] < best[4]:
@@ -787,6 +871,7 @@ def plan(tries=None):
     order, start, end = best[0], best[1], best[3][0]
     count = {e: 0 for e in "DAPG"}
     known = {e: {} for e in "DAPGS"}
+    done = {e: [] for e in "DAPG"}
     nd = 0
     for k in order:
         o = ops[k]
@@ -796,6 +881,10 @@ def plan(tries=None):
                 continue
             s, val = ops[p]["sig"]
             if kn.get(s, 0) < val:
+                if s == "c" + o["e"]:
+                    for p2 in done[o["e"]][val:]:
+                        if start[p2] + ops[p2]["cost"] + PRM["SURE"] <= start[k]:
+                            p, val = p2, ops[p2]["sig"][1]
                 waits.append((s, val))
                 kn[s] = val
                 for s2, v2 in ops[p]["kn"].items():
@@ -803,6 +892,7 @@ def plan(tries=None):
         o["waits"], o["kn"] = waits, dict(kn)
         if o["kind"] == "c":
             count[o["e"]] += 1
+            done[o["e"]].append(k)
             o["sig"] = ("c" + o["e"], count[o["e"]])
         elif o["kind"] == "d":
             o["sig"] = ("dm%d" % nd, 16)

import math
import numpy as np
from concourse.mybir import AluOpType as OP, AxisListType, ActivationFunctionType as AF

N = 8
NP, NHD = 3072, 2048
PRM = dict(NC=(32,) * 8, NB=(64,) * 8, WV=0, C1=32, C3=32, REPA=(0, 0, 0, 0), QC=16, SG4=2, LCH=(8, 8, 16, 48), WCH=8, CUT=(), SGA=0, REPG=6, GCV=1, MHS=0, SURE=300.0, LA=0, XV=48, LINV=0, FAST=1, HG=0)
NENG = 8
F, B, H, I, U = "float32", "bfloat16", "float16", "int32", "uint16"
SB = {
    "X": (NP + 96, B), "Li": (NHD, I), "L": (NHD + 1280, F), "W": (NP + 1024, F), "V": (NHD + 1280, F), "IT": (NP, F),
    "wi": (192, I), "wc": (192, H), "hoi": (32, I), "hou": (32, U), "xd0": (544, B), "xd1": (544, B), "lx0": (544, B), "lx1": (544, B),
    "ones": (256, B), "idn": (128, B), "nidn": (128, B), "bo": (128, B), "boh": (128, H), "bk": (256, B), "bob": (128, B),
    "sel": (16, B), "Q": (288, B), "ST": (2048, H), "pi": (4, I), "pf": (12, F), "ar": (256, F), "oh16": (16, F),
    "ncse": (128, B), "mA": (144, B), "csh": (128, H), "rst": (128, F), "jrow": (128, B), "p0": (144, B),
    "Dm": (256, H), "ih": (512, H), "ii": (72, I), "cu": (72, U),
    "wr32": (256, F), "wrb": (256, B), "nthr": (256, B), "wC": (32, F), "dL": (240, F), "dW": (128, F),
    "dX": (12, F), "mk": (512, F), "need": (8, F),
    "hoff": (80, U), "Lu": (256, U), "nL": (1280, H), "dd": (4096, B), "da": (4096, B), "h32": (1024, F), "ag": (1024, B),
    "xr": (4096, B), "pm": (256, F), "uu": (1032, B), "zb": (512, F), "Mh": (576, H), "nA": (152, H), "dv": (2176, H), "eT": (96, F), "Lu0": (256, U),
    "es": (256, F), "eoff": (80, U), "eF": (80, F), "hr": (1024, H), "hs": (1024, H), "hC": (80, F),
    "E0": (272, F), "H5": (272, F), "E": (2176, B), "vg": (512, B), "sg": (1024, B), "fl": (64, F), "un": (64, H),
    "sv": (64, F), "pd": (80, F), "gt": (80, F), "wu": (16, F), "s1": (80, F), "s2": (80, F), "s3": (80, F), "s4": (80, F),
    "s5": (128, F), "s6": (128, F), "oL": (64, U), "oP": (80, U), "oW": (64, U), "nc": (1280, F),
    "prb": (256, B), "jk": (768, B), "r3": (768, B), "ac": (4, F), "uo": (32, U), "rb": (4, B), "ri": (4, I),
    "rq0": (56, U), "rq1": (56, U), "lq0": (56, U), "lq1": (56, U), "rs0": (48, B), "rs1": (48, B),
    "ls0": (48, B), "ls1": (48, B), "xs0": (48, B), "yh": (144, H), "y1": (48, F), "y2": (48, F), "y3": (48, F),
    "zz": (20, F), "dx": (48, B), "fr": (48, F), "xq": (96, B), "bb": (144, B), "E2": (288, B),
}
PART = {"e0c": ("zz", 0, 4), "fC": ("zz", 4, 4), "z1": ("zz", 8, 4), "z2": ("zz", 12, 4), "z3": ("zz", 16, 4),
        "b1": ("bb", 0, 48), "b2": ("bb", 48, 48), "b3": ("bb", 96, 48)}
PS = ["pa", "pb", "pk0", "pk1", "pc", "pdd", "pm0", "pm1"]
SCRATCH = {k: ("sbuf", [128, w], d) for k, (w, d) in SB.items()}
for _k in PS:
    SCRATCH[_k] = ("psum", [128, 512], F)
NDMA, NREM = 12, 6
SEMAPHORES = ["cD", "cA", "cP", "cG"] + ["dm%d" % k for k in range(NDMA)] + ["ar%d" % k for k in range(NREM)] + ["lc"]
SIZE = {F: 4, I: 4, B: 2, H: 2, U: 2}
COSTS = [dict(cyc=0.83, g=1.56, sc=3.8, pe=0.43, hop=220.0, rem=2200.0, fix=0.0, afix=30.0, pfix=2.0, bw=380.0),
         dict(cyc=0.83, g=1.3, sc=2.5, pe=0.42, hop=270.0, rem=2000.0, fix=0.0, afix=30.0, pfix=0.0, bw=330.0),
         dict(cyc=1.0, g=1.4, sc=4.5, pe=0.52, hop=180.0, rem=1800.0, fix=5.0, afix=30.0, pfix=0.0, bw=450.0),
         dict(cyc=1.2, g=1.9, sc=3.5, pe=0.6, hop=240.0, rem=3000.0, fix=0.0, afix=30.0, pfix=4.0, bw=250.0)]
DFIX = 1300.0
RND = 1.5 * 2 ** 23
NLOAD = 7
TRIES, SEED, TEMP = 55000, 5, 8.0


def v(name, lo=0, hi=None, step=1, p=None):
    if name in PART:
        name, o, w = PART[name]
        return (name, o + lo, o + (w if hi is None else hi), step, p)
    if hi is None:
        hi = SB[name][0] if name in SB else 512
    return (name, lo, hi, step, p)


def ind(win, off):
    return ("I", win, off)


def ap(T, x):
    if not isinstance(x, tuple):
        return x
    if x[0] == "I":
        return ap(T, x[1]).indirect(ap(T, x[2]))
    name, lo, hi, step, p = x
    if p == "back":
        return T[name][:, lo + (cnt(x) - 1) * step:lo - 1:-step]
    ps = slice(None) if p is None else slice(*p)
    return T[name][ps, lo:hi:step] if step > 1 else T[name][ps, lo:hi]


def cnt(x):
    if x[0] == "I":
        return 16 * cnt(x[2])
    return (x[2] - x[1] + x[3] - 1) // x[3]


def wide(x):
    return x[0] in PS or SIZE[SB[x[0]][1]] == 4


def regs(*xs):
    out = []
    for x in xs:
        if isinstance(x, tuple):
            out += [x[1], x[2]] if x[0] == "I" else [x]
    return out


def program(c):
    ops, tag = [], ["", 0]

    def add(eng, fn, out, ins, cost, lat=0.0, kind="c", extra=()):
        W = [out[1]] if out[0] == "I" else [out]
        R = regs(*ins) + ([out[2]] if out[0] == "I" else [])
        ops.append(dict(e=eng, fn=fn, R=R, W=W + list(extra), cost=cost + c["fix"] * (eng in "DA"), lat=lat, kind=kind, tag=tuple(tag)))

    def vcost(out, in0, others, two=False, fix=50.0):
        n = cnt(out)
        if out[0] == "I":
            return fix + n * c["sc"] * c["cyc"]
        if in0[0] == "I":
            return fix + n * c["g"] * c["cyc"]
        if two:
            f = 1.0 if any(x[0] in PS for x in [in0] + others) else 2.0
        else:
            f = 1.0 if any(wide(x) for x in [out, in0] + others) else 0.5
        return max(64, n * f) * c["cyc"]

    def tt(out, a, b, op):
        add("D", lambda g, T, x: g.vector.tensor_tensor(ap(T, out), ap(T, a), ap(T, b), op), out, [a, b], vcost(out, a, [b], True))

    def ts(out, a, s1, op0, s2=None, op1=None):
        if op1 is None:
            fn = lambda g, T, x: g.vector.tensor_scalar(ap(T, out), ap(T, a), ap(T, s1), None, op0)
        else:
            fn = lambda g, T, x: g.vector.tensor_scalar(ap(T, out), ap(T, a), ap(T, s1), ap(T, s2), op0, op1)
        add("D", fn, out, [a, s1, s2], vcost(out, a, []))

    def cp(out, a):
        add("D", lambda g, T, x: g.vector.tensor_copy(ap(T, out), ap(T, a)), out, [a], vcost(out, a, []))

    def scan(out, d0, d1, init, op0, op1):
        add("D", lambda g, T, x: g.vector.tensor_tensor_scan(ap(T, out), ap(T, d0), ap(T, d1), init, op0, op1), out, [d0, d1],
            vcost(out, d0, [d1]))

    def ms(out, val):
        add("D", lambda g, T, x: g.vector.memset(ap(T, out), val), out, [], vcost(out, out, []))

    def act(out, a, func, bias=None, scale=None, accum=None, more=0.0):
        def fn(g, T, x):
            kw = {}
            if bias is not None:
                kw["bias"] = ap(T, bias)
            if scale is not None:
                kw["scale"] = scale
            if accum is not None:
                kw["accum_out"] = ap(T, accum)
            return g.scalar.activation(ap(T, out), ap(T, a), func, **kw)
        k = vcost(out, a, [], fix=65.0) if "I" in (out[0], a[0]) else max(64, cnt(out)) * c["cyc"] + c["afix"]
        add("A", fn, out, [a, bias], k + more, extra=[accum] if accum else [])

    def mm(lst):
        def fn(g, T, x):
            for o, l, r, st, sp in lst:
                ins = g.tensor.matmul(ap(T, o), ap(T, l), ap(T, r), st, sp)
            return ins
        k = sum(max(min(64, cnt(l)), cnt(r)) * c["pe"] * (4 if wide(l) else 1) + c["pfix"] for o, l, r, st, sp in lst)
        add("P", fn, lst[0][0], [l for o, l, r, st, sp in lst] + [r for o, l, r, st, sp in lst], k, lat=60.0,
            extra=[o for o, l, r, st, sp in lst[1:]])

    def iota(out, pat, base, ch):
        kw = {} if SB[out[0]][1] == I else {"allow_small_or_imprecise_dtypes": True}
        add("G", lambda g, T, x: g.iota(ap(T, out), pat, base, ch, **kw), out, [], 130 + 2 * cnt(out) * c["cyc"])

    def asel(out, a, pat, cmp, base, ch):
        add("G", lambda g, T, x: g.affine_select(ap(T, out), ap(T, a), pat, cmp, 0.0, base, ch), out, [a], 170 + 2 * cnt(out) * c["cyc"])

    def gcp(out, a):
        asel(out, a, [[0, cnt(out)]], OP.is_ge, 0, 0)

    def load(q, out, src, nbytes):
        add(q, lambda g, T, x: (g.sync if q == "S" else g.scalar).dma_start(ap(T, out), src(T)), out, [], 60.0, lat=nbytes, kind="d")

    def store(q, dst, a, nbytes):
        add(q, lambda g, T, x: (g.sync if q == "S" else g.scalar).dma_start(dst(T), ap(T, a)), ("out%d" % len(ops), 0, 1, 1, None), [a],
            60.0, lat=nbytes, kind="d")

    def send(k, out, a, shift, more=0.0):
        def fn(g, T, x):
            dst = T.cores[(x["rank"] + shift) % N]
            rid, pid, _ = x["topo"].addr(dst)
            m = sum(1 << e for e in x["topo"].engines(x["core"], dst)[:NENG])
            return g.remote_dma(ap(T, out), ap(T, a), T.sem["ar%d" % k], T.sem.lc, pid, rid, m)
        add("G", fn, out, [a], 300.0, lat=c["rem"] + more, kind="r")
        ops[-1]["k"] = k

    load("S", v("wi"), lambda T: T.wr[:], 98e3)
    load("A", v("hoi"), lambda T: T.ho[:], 16e3)
    load("S", v("Li", 0, 1024), lambda T: T.hl[:, 0:1024], 524e3)
    load("A", v("Li", 1024, 2048), lambda T: T.hl[:, 1024:2048], 524e3)
    load("S", v("X", 0, NP), lambda T: T.xs[:], 786e3)
    load("S", v("xd0", 272, 528), lambda T: T.dm[:, 0:256], 65e3)
    load("S", v("xd1", 272, 528), lambda T: T.dm[:, 256:512], 65e3)
    ms(v("ones"), 1.0)
    asel(v("jk", 0, 128), v("ones", 0, 128), [[-16, 8], [0, 16]], OP.is_ge, 0, 1)
    asel(v("bo"), v("jk", 0, 128), [[16, 8], [0, 16]], OP.is_ge, 15, -1)
    asel(v("idn"), v("ones", 0, 128), [[-1, 128]], OP.is_equal, 0, 1)
    asel(v("jk", 128, 256), v("ones", 0, 128), [[-1, 128]], OP.is_equal, 1, 1)
    iota(v("pi", 0, 1), [[0, 1]], 0, 1)
    iota(v("ar"), [[0, 16], [1, 16]], 0, 0)
    iota(v("ii", 0, 8), [[32, 8]], 31, 0)
    iota(v("ii", 8, 56), [[1, 48]], 0, 0)
    iota(v("s1"), [[16, 80]], 0, 0)
    ts(v("pi", 1, 2), v("pi", 0, 1), 15, OP.bitwise_and)
    pa, ncpc, fixe, fixh, cpc, thr = [v("pf", k, k + 1) for k in (0, 1, 2, 3, 6, 7)]
    cp(pa, v("pi", 1, 2))
    ts(v("oh16"), v("ar", 0, 16), pa, OP.is_equal)
    cp(v("boh"), v("bo"))
    for a in range(16):
        ts(v("ST", 128 * a, 128 * a + 128), v("boh"), v("oh16", a, a + 1), OP.mult)
    cp(v("wc"), v("wi"))
    for b in range(8):
        mm([(v(PS[b], 192 * k, 192 * k + 192), v("ST", 128 * (2 * b + k), 128 * (2 * b + k + 1)), v("wc"), True, True) for k in range(2)])
        if b < PRM["WV"]:
            cp(v("W", 384 * b, 384 * b + 384), v(PS[b], 0, 384))
        else:
            act(v("W", 384 * b, 384 * b + 384), v(PS[b], 0, 384), AF.Copy)
    cp(v("hou"), v("hoi"))
    for k in range(0, NHD * (not PRM["GCV"]), 1024):
        cp(v("L", k, k + 1024), v("Li", k, k + 1024))


    def lin(out, a, scale, bias=None):
        if cnt(out) > PRM["LINV"]:
            act(out, a, AF.Copy if bias is None else AF.Identity, bias=bias, scale=scale)
        elif bias is None:
            ts(out, a, scale, OP.mult)
        else:
            ts(out, a, scale, OP.mult, bias, OP.add)

    def fill(out, val):
        lin(out, v("ones", 0, cnt(out)), val)

    lin(fixe, v("oh16", 15, 16), -4096.0, 5120.0)
    lin(fixh, v("oh16", 15, 16), -2048.0, 2048.0)
    lin(cpc, v("oh16", 15, 16), -16.0, 96.0)
    lin(ncpc, v("oh16", 15, 16), 16.0, -96.0)
    lin(thr, v("oh16", 15, 16), 16.0, -72.0)
    ts(v("mA"), v("ar", 0, 144), pa, OP.is_equal)
    for k, f in enumerate((8192.0, 2048.0, 4096.0)):
        lin(v("jk", 256 + 144 * k, 400 + 144 * k), v("mA"), f)
    tt(v("csh"), v("jk", 272, 400), v("jk", 415, 543), OP.subtract)
    tt(v("ncse"), v("jk", 559, 687), v("jk", 272, 400), OP.subtract)
    asel(v("p0"), v("ones", 0, 144), [[0, 9], [1, 16]], OP.is_equal, 0, 0)
    lin(v("rst"), v("p0", 0, 128), 8192.0)
    if PRM["MHS"]:
        tt(v("es", 0, 144), v("mA"), v("p0"), OP.max)
        ts(v("nA", 0, 144), v("es", 0, 144), -1.0, OP.mult, 1.0, OP.add)
        ts(v("nA", 144, 152), v("bo", 0, 128, 16), -1.0, OP.mult)
        ms(v("Mh"), 0.0)
    lin(v("jrow"), v("ar", 0, 128), 1.0 / 32)
    lin(v("nidn"), v("idn"), -1.0)
    for k, f in enumerate((1.0 / 128, 1.0, -1.0, -0.5)):
        ts(v("ih", 128 * k, 128 * k + 128), v("idn"), f, OP.mult)
    ms(v("Dm"), 0.0)
    tt(v("Dm", 0, 256, 2), v("idn"), v("jk", 128, 256), OP.subtract)
    cp(v("Dm", 31, 256, 32), v("nidn", 15, 128, 16))
    ts(v("bob"), v("bo"), 2.0 ** 55, OP.mult, 2.0 ** 55, OP.mult)
    for k in (1, 2):
        lin(v("bk", 128 * k - 128, 128 * k), v("bo"), 1.7 ** (-16 * k))
    lin(v("sel", 0, 8), v("bo", 0, 128, 16), 1.0)
    lin(v("sel", 8, 16), v("bo", 0, 128, 16), -1.0)
    iota(v("Q"), [[0, 288]], 0, 0)
    lin(v("Q", 15, 143, 16), v("bo", 0, 128, 16), 1.0)
    lin(v("Q", 159, 287, 16), v("bo", 0, 128, 16), -1.0)
    cp(v("cu", 0, 56), v("ii", 0, 56))
    ts(v("cu", 56, 62), v("ar", 0, 96, 16), pa, OP.add)
    fill(v("mk", 0, 256), 1.0)
    iota(v("mk", 256, 512), [[0, 256]], 20, 0)
    fill(v("nc", 0, 256), 1.0 / 1.7)
    scan(v("wr32"), v("nc", 0, 256), v("mk", 0, 256), 1.7 ** 129, OP.mult, OP.mult)
    lin(v("wrb"), v("wr32"), 1.0)
    lin(v("nthr"), v("wrb"), -2.56)

    def S(a, neg=0):
        return v("Q", 144 * neg + 15 - a, 144 * neg + 143 - a)

    def ST(a):
        return v("ST", 128 * a, 128 * a + 128)

    mm([(v("pdd", 0, 16), S(a), v("wrb", a, 256, 16), a == 0, a == 15) for a in range(16)])
    lin(v("wC", 0, 16), v("pdd", 0, 16), 1.0 / 16)
    lin(v("wC", 16, 32), v("pdd", 0, 16), -1.0 / 1024)
    ts(v("dL", 0, 80), v("s1"), pa, OP.add, 2048.0, OP.add)
    lin(v("dL", 80, 160), v("dL", 0, 80), 64.0)
    lin(v("dL", 160, 240), v("dL", 0, 80), 1.0 / 128, ncpc)
    lin(v("dW", 0, 64), v("dL", 0, 64), 1.0, 1024.0)
    lin(v("dW", 64, 128), v("dL", 0, 64), 64.0, 65536.0)
    lin(v("dX", 0, 6), v("dL", 0, 6), 1.0, 1024.0)
    if PRM["LA"]:
        lin(v("dX", 8, 11), v("dL", 0, 3), 1.0, -2047.5)
        iota(v("r3"), [[0, 768]], 1, 0)
        iota(v("r3", 0, 768, 256), [[0, 3]], 0, 0)
    else:
        if PRM["FAST"]:
            iota(v("r3", 0, 512), [[0, 512]], 0, 0)
        lin(v("dX", 8, 11), v("dL", 0, 3), -1.0, 2047.5)
    iota(v("V", 0, NHD), [[0, NHD]], 0, 0)
    fill(v("need", 0, 1), 8.5)
    fill(v("need", 2, 3), 88.5)
    fill(v("need", 4, 5), 1.0)
    for k in ("xd0", "xd1"):
        iota(v(k, 256, 272), [[0, 16]], 0, 0)
        iota(v(k, 528, 544), [[0, 16]], 300, 0)
    iota(v("E0", 256, 272), [[0, 16]], -2500, 0)
    iota(v("H5", 256, 272), [[0, 16]], 0, 0)
    for k in range(2):
        iota(v("uu", 516 * k, 516 * k + 516), [[0, 516]], 1, 0)
    for k in range(4):
        ms(v("dv", 544 * k, 544 * k + 288), 0.0)
    iota(v("gt", 64, 80), [[0, 16]], 0, 0)
    iota(v("s5", 48, 64), [[0, 16]], 0, 0)
    ms(v("un", 0, 16), -64.0)
    for k in ("rq0", "rq1"):
        ms(v(k, 0, 8), 0)

    Xw, Lw, Ww = v("X", 0, NP), v("L", 0, NHD), v("W", 0, NP)
    one1 = v("ones", 0, 128, 1, (0, 1))
    rot = [0]

    def rep16(k):
        return v("cu", 56, 56 + k)

    def nearest(hf, base, ns, nc, nl, u):
        pk, o = PS[2 + hf], 128 * hf
        key, pm, z = v(pk, 0, 128), v("pm", o, o + 128), v("zb", 2 * o, 2 * o + 256)
        mm([(v(pk, 128, 384, 1, (0, ns)), nl, v("Dm"), True, True)])
        jr = (key, one1, v("jrow", 0, 128, 1, (0, 1)))
        mm([jr + (True, False)])
        if nc:
            mm([(v(pk, j, 128, 16, (0, nc)), v("dd", base + j, base + 16 * nc, 16), v("sel", 8, 16), False, False) for j in range(16)])
        cut = [0] + [x for x in PRM["CUT"] if x < ns] + [ns]
        for a, b in zip(cut, cut[1:]):
            mm([(v(pk, j, 128, 16, (a, b)), v("da", base + 16 * a + j, base + 16 * b, 16), v("sel", 0, 8), False, False) for j in range(16)] +
               ([jr + (False, True)] if b == ns else []))
        scan(pm, v("rst"), key, 0.0, OP.add, OP.min)
        tt(v("uu", u, u + 256, 2), key, pm, OP.is_gt)
        scan(z, v(pk, 128, 384), v("uu", u, u + 256), 0.0, OP.add, OP.mult)
        ec = v(pk, 384, 384 + ns // 16)
        r, d = 16 + 144 * hf, 304 + 144 * hf
        if ns < 128 or not PRM["MHS"]:
            tt(v("Mh", r, r + 128), ind(z, v("cu", 0, 8)), v("mA", 0, 128), OP.mult)
            mm([(ec, v("Mh", r, r + 128, 1, (0, ns)), v("boh", 0, ns, 16, (0, ns)), True, True)])
            return ec
        cp(v("Mh", d + 15, d + 128, 16), v("zb", 2 * o + 31, 2 * o + 256, 32))
        scan(v("Mh", r, r + 128, 1, "back"), v("nA", 1, 129, 1, "back"), v("Mh", d, d + 128, 1, "back"), 0.0, OP.mult, OP.add)
        mm([(ec, v("Mh", r, r + 128), v("boh", 0, 128, 16), True, False), (ec, v("Mh", r - 1, r + 127), v("nA", 144, 152), False, False),
            (ec, v("Mh", d - 1, d + 127), v("boh", 0, 128, 16), False, True)])
        return ec

    def after_e(i, hf):
        o, oc = 256 * i + 128 * hf, 16 * i + 8 * hf
        eo = v("eoff", oc, oc + 8)
        if i < 4:
            ts(v("hr", o, o + 128), ind(Ww, eo), RND, OP.add, -RND, OP.add)
            scan(v("hs", o, o + 128), v("csh"), v("hr", o, o + 128), 0.0, OP.add, OP.min)
            ts(v("hoff", oc + 16, oc + 24), v("hs", o + 15, o + 128, 16), fixh, OP.add)
        else:
            act(v("H5", 128 * hf, 128 * hf + 128), ind(Ww, eo), AF.Copy)

    def chunks(lo, hi, k):
        m = (hi - lo + k - 1) // k
        return [(lo + (hi - lo) * q // m // 2 * 2, lo + (hi - lo) * (q + 1) // m // 2 * 2) for q in range(m)] if m else []

    def at15(k):
        return v("dv", 544 * k + 31, 544 * k + 272, 16)

    def spread(k, l):
        u = 516 * (l % 2)
        scan(v("dv", 544 * k + 288, 544 * k + 544, 1, "back"), v("uu", u + 2, u + 514, 2, "back"), v("dv", 544 * k + 16, 544 * k + 272, 1, "back"),
             0.0, OP.mult, OP.add)

    def columns(t, levels):
        w, l0 = 256 * len(levels), levels[0][0]
        half = (v("pm0", 0, w), v("ih", 384, 512), v("nL", 256 * l0, 256 * l0 + w))
        lst = [half + (True, False)]
        for l, new, old in levels:
            for hf in range(2):
                out = v("pm0", 256 * (l - l0) + 128 * hf, 256 * (l - l0) + 128 * hf + 128)
                for k, p, m in ((new, 128, 256), (old, 256, 128)):
                    d, r = 544 * k + 16 + 128 * hf, 544 * k + 288 + 128 * hf
                    for o, sign in ((r, p), (r - 1, m), (d - 1, p)) if l else ((d + 15 - t, p),):
                        lst.append((out, v("dv", o, o + 128), v("ih", sign, sign + 128), False, False))
                mm(lst)
                lst = []
        mm([half + (False, True)])
        if l0 < 3 or not PRM["LA"]:
            act(v("nc", 256 * l0, 256 * l0 + w), v("pm0", 0, w), AF.Identity, bias=1024.0)
        else:
            ts(v("nc", 256 * l0, 256 * l0 + w), v("pm0", 0, w), 1024.0, OP.add)

    for t in range(2):
        need, need80 = v("need", t, t + 1), v("need", 2 + t, 3 + t)
        xd, lx = "xd%d" % t, "lx%d" % t
        tag[:] = ["first", 10 * t]
        mark = v("mk", 256 * t, 256 * t + 256)
        h0 = v("hou", 16 * t, 16 * t + 16)
        gcp(v("hC", 0, 16), v("hoi", 16 * t, 16 * t + 16))
        act(ind(v("V"), h0), mark, AF.Silu, more=1300.0 if t == 0 else 0.0)
        if t:
            ops[-1]["R"].append(v("oP"))
        lists = Lw if t else v("Li")
        if t and PRM["LA"]:
            ts(v("Lu0"), ind(lists, h0), 0.0, OP.add)
            ts(v("nL", 0, 256), v("Lu0"), -1.0, OP.mult, 1024.0, OP.add)
        else:
            ts(v("nL", 0, 256), ind(lists, h0), -1.0, OP.mult, 1024.0, OP.add)
        for hf in range(2):
            o, er = 128 * hf, v(PS[2 + hf], 384, 512)
            mm([(er, ST(t), v("nL", o, o + 128), True, True)])
            scan(v("es", o, o + 128), v("ncse"), er, 0.0, OP.add, OP.max)
            eo = v("eoff", 8 * hf, 8 * hf + 8)
            ts(eo, v("es", o + 15, o + 128, 16), -1.0, OP.mult, fixe, OP.add)
            after_e(0, hf)
            act(v(xd, o, o + 128), ind(Xw, eo), AF.Copy)
            act(v("E0", o, o + 128), er, AF.Copy)
        mm([(v("pdd", 48 + 8 * hf, 56 + 8 * hf), v("nL", 128 * hf, 128 * hf + 128), v("ST", 128 * t, 128 * t + 128, 16), True, True) for hf in range(2)])
        e0T, zend = v("eT", 0, 16), v("zb", 31, 512, 32)
        lin(e0T, v("pdd", 48, 64), -1.0)
        for k in (0, 3):
            gcp(at15(k), e0T)
        send(3 * t, v(lx), v(xd), t + 1, 2000.0)
        for j in range(32):
            hf, j = j // 16, j % 16
            o, a = v("xr", 2048 * hf + j, 2048 * hf + 2048, 16), v(xd, 128 * hf, 128 * hf + 128)
            if j < PRM["REPA"][2 * t + hf]:
                act(o, a, AF.Copy)
            elif hf and j >= 16 - PRM["REPG"]:
                asel(o, a, [[0, 128]], OP.is_ge, 0, 0)
            else:
                cp(o, a)
        if t == 0:
            for k in range(0, NP, 1024):
                iota(v("IT", k, k + 1024), [[1, 1024]], k, 0)
                ops[-1]["R"].append(v("xr"))
            for k in range(0, NHD * PRM["GCV"], 1024):
                asel(v("L", k, k + 1024), v("Li", k, k + 1024), [[0, 1024]], OP.is_ge, 0, 0)
                ops[-1]["R"].append(v("xr"))
        for i in range(1, 5):
            q = 16 * i
            NC, NB = PRM["NC"][4 * t + i - 1], PRM["NB"][4 * t + i - 1]
            tag[:] = ["death", 10 * t + i]
            hC = v("hC", q, q + 16)
            so, vg = 512 * (i % 2), v("vg", 256 * (i % 2), 256 * (i % 2) + 256)
            hs, un = v("hs", 256 * i - 241, 256 * i, 16), v("un", q - 16, q)
            if PRM["HG"]:
                gcp(hC, v("hoff", q, q + 16))
            else:
                ts(hC, hs, fixh, OP.add)
            act(vg, ind(v("V", 0, NHD), v("hoff", q, q + 16)), AF.Relu, bias=-0.25 - 0.75 * t)
            lst, o = [], 0
            for cc in range(16):
                w = 256 - 16 * cc
                ts(v("E", o, o + w), v("hr", 256 * (i - 1) + 16 * cc, 256 * i), v("hC", q + cc, q + cc + 1), OP.is_equal,
                   v("wC" if i == 1 else "wu", cc, cc + 1), OP.mult)
                lst.append((v("pc", 16 * cc, 256), v("bo"), v("E", o, o + w), cc == 0, False))
                o += w
                if cc % 4 == 3:
                    mm(lst)
                    lst = []
            mm([(v("pc", 0, 256), v("idn"), v("nthr"), False, False), (v("pc", 0, 256), v("bob"), vg, False, True)])
            act(v("sg", so, so + 256), v("pc", 0, 256), AF.Sign)
            if i == 4:
                mm([(v("pm1", 0, 256), v("bo"), v("sg", so, so + 256), True, False)] +
                   [(v("pm1", a, 256, 16), ST(a), un, False, False) for a in range(16)])
                mm([(v("pdd", 0, 16), S(a, 1), v("sg", so + a, so + 256, 16), a == 0, False) for a in range(16)] +
                   [(v("pdd", 0, 16), v("ih", 256, 384), un, False, False)])
            for hf in range(2):
                o = 128 * hf
                tag[0] = "near%d" % hf
                ho = v("hoff", q + 8 * hf, q + 8 * hf + 8)
                ts(v("Lu", o, o + 128), ind(lists, ho), 0.0, OP.add)
                nl = v("nL", 256 * i + o, 256 * i + o + 128)
                ts(nl, v("Lu", o, o + 128), -1.0, OP.mult, 1024.0, OP.add)
                for a, b in chunks(o + 128 - NB, o + 128, PRM["C3"]):
                    r = rot[0] % 2
                    rot[0] += 1
                    w = 16 * (b - a)
                    ag = v("ag", 512 * r, 512 * r + w)
                    act(ag, ind(Xw, v("Lu", a, b)), AF.Copy)
                    if i == 1 and hf < PRM["FAST"]:
                        mm([(v(PS[r], 0, w), v("Q", 16, 144, 1, (0, 1)), v("r3", 0, w, 1, (0, 1)), True, False)])
                        mm([(v(PS[r], j, w, 16), v("nidn"), v(xd, a, b), False, False) for j in range(16)])
                    else:
                        mm([(v(PS[r], 0, w), v("nidn"), v("xr", 16 * a, 16 * b), True, False)])
                    mm([(v(PS[r], 0, w), v("idn"), ag, False, True)])
                    act(v("da", 16 * a, 16 * b), v(PS[r], 0, w), AF.Abs)
                for a, b in chunks(o + NC, o + 128 - NB, PRM["C1"]) + chunks(o, o + NC, PRM["C1"]):
                    d = v("dd", 16 * a, 16 * b)
                    tt(d, ind(Xw, v("Lu", a, b)), v("xr", 16 * a, 16 * b), OP.subtract)
                    if a < o + NC:
                        ts(v("da", 16 * a, 16 * b), d, 0.0, OP.max, 2.0, OP.mult)
                    else:
                        act(v("da", 16 * a, 16 * b), d, AF.Abs)
                tag[0] = "chain%d" % hf
                ec = nearest(hf, 16 * o, 128, NC, nl, 516 * (i % 2) + 2 * o)
                ts(v("eoff", q + 8 * hf, q + 8 * hf + 8), ec, 1024.0, OP.add)
                after_e(i, hf)
            tag[0] = "paid"
            m = PRM["SG4"] if i == 4 else 1
            sga = PRM["SGA"] and i < 4
            for k in range(m):
                a, b = 256 * k // m, 256 * (k + 1) // m
                if sga:
                    act(v("jk", 0, 256), ind(Xw, v("eoff", q, q + 16)), AF.Copy)
                    mm([(v("pm1", 0, 256), v("nidn"), v(xd, 272, 528), True, False), (v("pm1", 0, 256), v("idn"), v("jk", 0, 256), False, True)])
                    act(v("sg", so + 256, so + 512), v("pm1", 0, 256), AF.Sign, bias=0.5)
                else:
                    tt(v("sg", so + 256 + a, so + 256 + b), ind(Xw, v("eoff", q + a // 16, q + b // 16)), v(xd, 272 + a, 272 + b), OP.is_ge)
            if i < 4:
                lst = [(v("pdd", 0, 32), S(a), v("sg", so + a, so + 512, 16), a == 0, a == 15) for a in range(16)]
                mm(lst[:1] + [(v("pdd", 0, 16), v("ih", 0, 128), hs, False, False), (v("pdd", 0, 16), v("ih", 128, 256), un, False, False)] + lst[1:] +
                   [(v("pdd", 32 + 8 * hf, 40 + 8 * hf), v("sg", so + 256 + 128 * hf, so + 384 + 128 * hf), v("sel", 0, 8), True, True) for hf in range(2)])
                sv, fl = v("sv", q, q + 16), v("fl", q, q + 16)
                ts(sv, v("pdd", 0, 16), thr, OP.is_lt, -64.0, OP.mult)
                ts(fl, v("pdd", 16, 32), v("need", 4 + t, 5 + t) if sga else need, OP.is_lt)
                ts(v("eT", 16 + q, 32 + q), v("pdd", 32, 48), v("need", 4 + t, 5 + t) if sga else need, OP.is_lt)
                tt(v("s2", 0, 16), v("pdd", 0, 16), v("dL", 160 + q, 176 + q), OP.min)
                ts(v("oL", q, q + 16), v("s2", 0, 16), cpc, OP.add, 128.0, OP.mult)
                act(ind(v("V"), v("oL", q, q + 16)), mark, AF.Silu)
                tt(v("un", q, q + 16), sv, fl, OP.mult)
                tt(v("wu"), v("un", q, q + 16), v("wC", 16, 32), OP.mult)
            else:
                mm([(v("pm1", 0, 256), v("bo"), v("sg", so + 256, so + 512), False, True)])
                mm([(v("pdd", 0, 16), S(a), v("sg", so + 256 + a, so + 512, 16), False, a == 15) for a in range(16)])
                ts(v("pd", 64, 80), v("pdd", 0, 16), need80, OP.is_ge, -64.0, OP.mult)
            tag[0] = "cols"
            if i == 1:
                gcp(at15(2), zend)
            else:
                tt(v("s3", 0, 16), zend, e0T, OP.subtract)
                tt(v("s3", 16, 32), v("s3", 0, 16), v("eT", q, q + 16), OP.mult)
                tt(at15(2), v("s3", 16, 32), e0T, OP.add)
                spread(2, i - 1)
            if i < 4:
                columns(t, [(i - 1, 2, (i - 1) % 2)])
            (gcp if i < 4 else cp)(at15(i % 2), zend)
            spread(i % 2, i)
            if i == 4:
                spread(3, 4)
                columns(t, [(3, 2, 1), (4, 3, 0)])
        tag[:] = ["send", 10 * t + 5]
        rq, lq, rs, ls = "rq%d" % t, "lq%d" % t, "rs%d" % t, "ls%d" % t
        ts(v("vg", 0, 256), v("pm1", 0, 256), 80.0, OP.add, need, OP.is_lt)
        scan(v("prb"), v("ones", 0, 256), v("vg", 0, 256), 0.0, OP.mult, OP.add)
        ix = v(rq, 4, 7)
        if PRM["LA"]:
            for k in range(3):
                ts(v("jk", 256 * k, 256 * k + 256), v("prb"), v("dX", 8 + k, 9 + k), OP.is_lt)
            scan(v("E", 0, 768), v("r3"), v("jk"), 0.0, OP.mult, OP.add)
            cp(ix, v("E", 255, 768, 256))
        else:
            for k in range(3):
                act(v("jk", 256 * k, 256 * k + 256), v("prb"), AF.Sign, bias=v("dX", 8 + k, 9 + k), accum=v("ac", k, k + 1))
            ts(ix, v("ac", 0, 3), -0.5, OP.mult, 128.0, OP.add)
        ts(v("yh", 0, 48), ind(v("H5"), ix), RND, OP.add, -RND, OP.add)
        scan(v("yh", 48, 96), v("csh", 0, 48), v("yh", 0, 48), 0.0, OP.add, OP.min)
        ts(v(rq, 0, 3), v("yh", 48 + 15, 96, 16), fixh, OP.add)
        ts(v(rq, 8, 56), ind(v("IT", 0, 272), ix), 0.0, OP.add)
        send(3 * t + 1, v(lq), v(rq), t + 1)
        act(v("xs0"), ind(v(xd, 0, 272), ix), AF.Copy)
        act(v("y2"), ind(v("E0"), ix), AF.Copy)
        scan(v("y3"), v("ncse", 0, 48), v("y2"), 0.0, OP.add, OP.max)
        ts(v("e0c", 0, 3), v("y3", 15, 48, 16), -1.0, OP.mult, fixe, OP.add)
        tt(v("z1", 0, 3), v("e0c", 0, 3), v("dX", 0, 3), OP.min)
        eo0 = v("uo", 4, 7)
        cp(eo0, v("z1", 0, 3))
        tag[0] = "payl"
        tt(v("pd", 16, 64), v("sv", 16, 64), v("un", 16, 64), OP.subtract)
        gcp(v("gt", 48, 64), v("pd", 48, 64))
        tt(v("gt", 32, 48), v("pd", 32, 48), v("pd", 48, 64), OP.add)
        for k in (16, 0):
            tt(v("gt", k, k + 16), v("gt", 32, 48), v("pd", 16, 32), OP.add)
        tt(v("s1"), v("dL", 0, 80), v("hC"), OP.subtract)
        tt(v("s2"), v("gt"), v("s1"), OP.mult)
        tt(v("s2"), v("s2"), v("dL", 80, 160), OP.add)
        pd4 = v("pd", 64, 80)
        tt(v("s4"), ind(pd4, rep16(5)), v("s1"), OP.mult)
        tt(v("s4"), v("s4"), v("s2"), OP.add)
        ts(v("oP"), v("s4"), 1.0 / 64, OP.mult)
        a = 0
        for k in PRM["LCH"]:
            if PRM["LA"]:
                act(ind(v("L"), v("oP", a, a + k)), v("nc", 16 * a, 16 * (a + k)), AF.Silu)
            else:
                cp(ind(v("L"), v("oP", a, a + k)), v("nc", 16 * a, 16 * (a + k)))
            a += k
        tag[0] = "payw"
        for k in range(0, 64, 16):
            gcp(v("h32", 16 * k, 16 * k + 256), v("hr", 16 * k, 16 * k + 256))
        gcp(v("eF", 0, 64), v("eoff", 0, 64))
        gcp(v("eF", 64, 80), v("eoff", 64, 80))
        tt(v("s5", 64, 128), v("dW", 0, 64), v("eF", 16, 80), OP.subtract)
        tt(v("s6", 64, 128), ind(v("eF", 0, 16), rep16(4)), v("dW", 0, 64), OP.subtract)
        tt(v("s5", 0, 48), ind(pd4, rep16(3)), v("gt", 32, 80), OP.add)
        tt(v("s3", 0, 64), v("s5", 0, 64), v("s5", 64, 128), OP.mult)
        tt(v("s6", 0, 64), v("pd", 16, 80), v("s6", 64, 128), OP.mult)
        tt(v("s3", 0, 64), v("s3", 0, 64), v("s6", 0, 64), OP.subtract)
        tt(v("s6", 0, 64), v("s3", 0, 64), v("dW", 64, 128), OP.add)
        ts(v("oW"), v("s6", 0, 64), 1.0 / 64, OP.mult)
        for k in range(0, 64, PRM["WCH"]):
            act(ind(v("W"), v("oW", k, k + PRM["WCH"])), v("h32", 16 * k, 16 * (k + PRM["WCH"])), AF.Silu)
        if t == 0:
            tt(v("s1", 0, 16), v("gt", 0, 16), pd4, OP.add)
            add("D", lambda g, T, x: g.vector.tensor_reduce(ap(T, v("ac", 3, 4)), ap(T, v("s1", 0, 16)), AxisListType.X, OP.add),
                v("ac", 3, 4), [v("s1", 0, 16)], 64.0)
            cp(v("rb", 0, 1), v("ac", 3, 4))
            mm([(v("pm0", 0, 1), v("ones", 0, 128), v("rb", 0, 1), True, True)])
            ts(v("ri", 0, 1), v("pm0", 0, 1), -1.0 / 64, OP.mult)
            ts(v("ri", 1, 2), v("ri", 0, 1), 1, OP.bitwise_and)
            ts(v("need", 1, 2), v("ri", 1, 2), 8.5, OP.add)
            lin(v("need", 3, 4), v("need", 1, 2), 1.0, 80.0)
            lin(v("need", 5, 6), v("need", 1, 2), 2.0, -16.0)
        else:
            for k in range(0, NHD * PRM["LA"], 256):
                ts(v("V", k, k + 256), v("L", k, k + 256), RND, OP.add, -RND, OP.add)
            store("S", lambda T: T.yl[:], v("V", 0, NHD) if PRM["LA"] else Lw, 1048e3)
            wf, w8 = v("wr32", 0, 192), v("W", 0, NP, 1, (0, 128, 16))
            add("S", lambda g, T, x: g.sync.dma_start(ap(T, wf), ap(T, w8)), wf, [w8], 60.0, lat=98e3, kind="d")
            ts(wf, wf, RND, OP.add, -RND, OP.add)
            store("S", lambda T: T.yw[:], wf, 98e3)
        tag[0] = "came"
        hq, ixc = v(lq, 0, 3), v(lq, 4, 7)
        ts(v("Lu", 0, 48), ind(Lw, hq), 0.0, OP.add)
        nl = v("yh", 96, 144)
        ts(nl, v("Lu", 0, 48), -1.0, OP.mult, 1024.0, OP.add)
        qc = PRM["QC"]
        for a, b in chunks(qc, 48, 16) + chunks(0, qc, 16):
            xr, d = v("xr", 16 * a, 16 * b), v("dd", 16 * a, 16 * b)
            if a >= PRM["XV"]:
                cp(xr, ind(v(lx, 0, 272), v(lq, 8 + a, 8 + b)))
            else:
                act(xr, ind(v(lx, 0, 272), v(lq, 8 + a, 8 + b)), AF.Copy)
            tt(d, ind(Xw, v("Lu", a, b)), xr, OP.subtract)
            if a < qc:
                ts(v("da", 16 * a, 16 * b), d, 0.0, OP.max, 2.0, OP.mult)
            else:
                act(v("da", 16 * a, 16 * b), d, AF.Abs)
        xq, dq = v("xq", 0, 48), v("xq", 48, 96)
        act(xq, ind(v(lx, 0, 272), ixc), AF.Copy)
        act(dq, ind(v(lx, 272, 544), ixc), AF.Copy)
        ec = nearest(0, 0, 48, qc, nl, 0)
        fo = v("uo", 12, 15)
        ts(fo, ec, 1024.0, OP.add)
        ts(v("fC", 0, 3), ec, 1024.0, OP.add)
        act(v("fr"), ind(v("IT"), fo), AF.Copy)
        tt(v("b1"), ind(Xw, fo), dq, OP.is_ge)
        tt(v("dx"), ind(Xw, fo), xq, OP.subtract)
        mm([(v("pk1", 0, 48), v("bo"), v("b1"), True, True)])
        scan(v("y2"), v("csh", 0, 48), v("pk1", 0, 48), 0.0, OP.add, OP.min)
        ts(v("b2"), v("pk1", 0, 48), need, OP.is_lt)
        ts(v("pf", 5, 6), fixh, -1.0, OP.mult, need, OP.add)
        lst = [(v("pc", 0, 48), v("idn"), v("nthr", 0, 48), True, False)]
        for k in range(3):
            ts(v("E2", 48 * k, 48 * k + 48), v("fr"), v("e0c", k, k + 1), OP.is_equal)
            lst.append((v("pc", 0, 48), v("bob"), v("E2", 48 * k, 48 * k + 48), False, False))
        lst.append((v("pc", 0, 48), v("bob"), v("b2"), False, False))
        mm(lst)
        ts(v("z3", 0, 3), v("y2", 15, 48, 16), v("pf", 5, 6), OP.is_ge, v("wC", 0, 1), OP.mult)
        lst = []
        for k in (2, 1, 0):
            o = 144 + 48 * k
            ts(v("E2", o, o + 48 - 16 * k), v("fr", 16 * k, 48), v("fC", k, k + 1), OP.is_equal, v("z3", k, k + 1), OP.mult)
            lst.append((v("pc", 16 * k, 48), v("bk", 128 * k - 128, 128 * k) if k else v("bo"), v("E2", o, o + 48 - 16 * k), False, k == 0))
        mm(lst)
        ts(v("b3"), v("pc", 0, 48), 0.0, OP.is_lt)
        tt(v(rs), v("dx"), v("b3"), OP.mult)
        send(3 * t + 2, v(ls), v(rs), -(t + 1))
        scan(v("y1"), v("csh", 0, 48), v("b3"), 0.0, OP.add, OP.min)
        tt(v("z2", 0, 3), v("fC", 0, 3), v("dX", 3, 6), OP.subtract)
        ts(v("z3", 0, 3), v("y1", 15, 48, 16), fixh, OP.add)
        tt(v("z3", 0, 3), v("z3", 0, 3), v("z2", 0, 3), OP.mult)
        tt(v("z2", 0, 3), v("z3", 0, 3), v("dX", 3, 6), OP.add)
        fo2 = v("uo", 16, 19)
        cp(fo2, v("z2", 0, 3))
        cp(ind(v("X"), fo2), xq)
        tt(ind(v("X"), eo0), v("xs0"), v(ls), OP.add)
    store("S", lambda T: T.yx[:, 0:NP // 2], v("X", 0, NP // 2), 393e3)
    store("A", lambda T: T.yx[:, NP // 2:NP], v("X", NP // 2, NP), 393e3)
    return ops


def meet(a, b):
    if a[1] >= b[2] or b[1] >= a[2]:
        return False
    return not (a[3] == b[3] and a[3] > 1 and (a[1] - b[1]) % a[3])


def depend(ops):
    acc, deps = {}, []
    for k, o in enumerate(ops):
        d = set()
        for x, wr in [(x, False) for x in o["R"]] + [(x, True) for x in o["W"]]:
            for k2, y, wr2 in acc.get(x[0], ()):
                if x[0] in PS and (ops[k2]["e"] != o["e"] or o["e"] == "P"):
                    d.add(k2)
                elif (wr or wr2) and meet(x, y):
                    d.add(k2)
        for x, wr in [(x, False) for x in o["R"]] + [(x, True) for x in o["W"]]:
            acc.setdefault(x[0], []).append((k, x, wr))
        deps.append(sorted(d))
    full = [set(d) for d in deps]
    above = []
    for k in range(len(ops)):
        above.append(set(deps[k]).union(*[above[p] for p in deps[k]]))
        deps[k] = [p for p in deps[k] if not any(p in above[p2] for p2 in deps[k])]
    return deps, full


def schedule(alts, deps, tries):
    ops = alts[0]
    n = len(ops)
    succ = [[] for _ in ops]
    for k in range(n):
        for p in deps[k]:
            succ[p].append(k)
    eng = ["DAPGS".index(o["e"]) for o in ops]
    dma = [o["kind"] == "d" for o in ops]
    dmas = [k for k in range(n) if dma[k]]
    pos = [0] * n
    pre = [[p for p in deps[k] if not (eng[p] == 2 and eng[k] == 2)] for k in range(n)]
    models = [([o["cost"] for o in a], [o["lat"] / c["bw"] if o["kind"] == "d" else o["lat"] + c["hop"] for o in a], c["hop"])
              for a, c in zip(alts, COSTS)]

    def times(order, m, i=0, old=None):
        cost, lat, hop = models[m]
        free, rdy, st, dfree = [0.0] * 5, [0.0] * n, [0.0] * n, 0.0
        if i:
            st, rdy = list(old[1]), list(old[2])
            for k in order[:i]:
                free[eng[k]] = st[k] + cost[k]
            dfree = max([rdy[k] - hop for k in dmas if pos[k] < i])
        for k in order[i:]:
            e = eng[k]
            t = free[e]
            for p in pre[k]:
                if rdy[p] > t:
                    t = rdy[p]
            st[k] = t
            t += cost[k]
            free[e] = t
            if dma[k]:
                dfree = max(dfree, t + DFIX) + lat[k]
                rdy[k] = dfree + hop
            else:
                rdy[k] = t + lat[k]
        return max(rdy) - hop, st, rdy

    cost, lat, hop = models[0]

    def tails(order):
        tl, nx = [0.0] * n, [0.0] * 5
        for k in reversed(order):
            la = lat[k] + (DFIX + hop if dma[k] else 0.0)
            t = la
            for s in succ[k]:
                x = tl[s] + (0.0 if eng[k] == 2 and eng[s] == 2 else la)
                if x > t:
                    t = x
            tl[k] = cost[k] + max(t, nx[eng[k]])
            nx[eng[k]] = tl[k]
        return tl

    def redo(order, st, rdy, lo, hi, pr, win):
        i = 0
        while i < n and st[order[i]] < lo:
            i += 1
        i = max(i, NLOAD)
        done = [False] * n
        free = [0.0] * 5
        for k in order[:i]:
            done[k] = True
            free[eng[k]] = st[k] + cost[k]
        rd = list(rdy)
        left, est = {}, {}
        ready = [[] for _ in range(5)]
        for k in order[i:]:
            if st[k] > hi + 6000:
                break
            left[k] = sum(not done[p] for p in deps[k])
            if not left[k]:
                est[k] = max([rd[p] for p in pre[k]], default=0.0)
                ready[eng[k]].append(k)
        out = order[:i]
        while True:
            tm, e = 1e18, -1
            for x in range(5):
                if ready[x]:
                    t = max(free[x], min([est[q] for q in ready[x]]))
                    if t < tm:
                        tm, e = t, x
            if tm > hi:
                break
            r = ready[e]
            k, b = -1, -1e18
            for q in r:
                if est[q] <= tm + 40.0 and pr[q] > b:
                    k, b = q, pr[q]
            h, hb = -1, b
            for q in r:
                if pr[q] > hb and est[q] < tm + cost[k]:
                    h, hb = q, pr[q]
            if h >= 0:
                f, fb = -1, -1e18
                for q in r:
                    if pr[q] > fb and max(est[q], tm) + cost[q] <= est[h] and q != h:
                        f, fb = q, pr[q]
                if f >= 0:
                    k = f
                elif est[h] <= tm + 40.0 + win * cost[k]:
                    k = h
            r.remove(k)
            t = free[e] = max(est[k], free[e]) + cost[k]
            rd[k] = t + lat[k] + (DFIX + hop if dma[k] else 0.0)
            done[k] = True
            out.append(k)
            for q in succ[k]:
                if q in left:
                    left[q] -= 1
                    if not left[q]:
                        est[q] = max([rd[p] for p in pre[q]], default=0.0)
                        ready[eng[q]].append(q)
        return out + [k for k in order[i:] if not done[k]], i

    def state(o, first, i=0, old=None):
        tms = [first] + [times(o, m, i, old and old[m]) for m in range(1, len(models))]
        ends = [x[0] for x in tms]
        return [o, first[1], first[2], ends, (sum(ends) + ends[0]) / (len(ends) + 1), None, tms]

    rng = np.random.default_rng(SEED)
    names = sorted(set(o["W"][0][0] for o in ops))
    part, step = np.array([o["tag"][0] for o in ops]), np.array([o["tag"][1] for o in ops])
    kind = np.array([names.index(o["W"][0][0]) for o in ops])
    order = list(range(n))
    pr = [0.0] * n
    for k in range(n - 1, -1, -1):
        pr[k] = cost[k] + max([pr[s] + lat[k] for s in succ[k]], default=0.0)
    order = redo(order, [0.0] * n, times(order, 0)[2], -1.0, 1e17, pr, 0.3)[0]
    best = cur = state(order, times(order, 0))
    for it in range(tries):
        if cur[5] is None:
            cur[0] = sorted(cur[0], key=lambda k: cur[1][k])
            cur[5] = (np.array(cur[1]), np.array(tails(cur[0])))
            for i, k in enumerate(cur[0]):
                pos[k] = i
        st, tl = cur[5]
        lo = rng.random() * cur[3][0] - 2000
        hi = lo + 3000 + rng.random() * 11000
        x, u = rng.random(), rng.random(4)
        pr = -st * x + tl * (1 - x)
        if u[0] < 0.5:
            pr = pr + rng.normal(size=n) * 400 * u[1]
        c = np.flatnonzero((st >= lo) & (st < hi))
        if u[2] < 0.7 and len(c):
            k = c[rng.integers(len(c))]
            m = (part == part[k]) & (step == step[k])
            if u[3] < 0.6:
                m &= kind == kind[k]
            pr[m] += rng.normal() * 1500
        o, i = redo(cur[0], cur[1], cur[2], lo, hi, list(pr), rng.random() * 0.6)
        lim = cur[4] - TEMP * (1 - it / tries) * math.log(rng.random())
        f = times(o, 0, i, cur[6][0])
        if f[0] - cur[3][0] > lim - cur[4] + 400:
            continue
        new = state(o, f, i, cur[6])
        if new[4] <= lim:
            cur = new
            if cur[4] < best[4]:
                best = cur
    return best


def plan(tries=None):
    alts = [program(c) for c in COSTS]
    ops = alts[0]
    deps, full = depend(ops)
    best = schedule(alts, deps, TRIES if tries is None else tries)
    order, start, end = best[0], best[1], best[3][0]
    count = {e: 0 for e in "DAPG"}
    known = {e: {} for e in "DAPGS"}
    done = {e: [] for e in "DAPG"}
    nd = 0
    for k in order:
        o = ops[k]
        kn, waits = known[o["e"]], []
        for p in sorted(full[k], key=lambda p: -start[p]):
            if ops[p]["e"] == "P" and o["e"] == "P":
                continue
            s, val = ops[p]["sig"]
            if kn.get(s, 0) < val:
                if s == "c" + o["e"]:
                    for p2 in done[o["e"]][val:]:
                        if start[p2] + ops[p2]["cost"] + PRM["SURE"] <= start[k]:
                            p, val = p2, ops[p2]["sig"][1]
                waits.append((s, val))
                kn[s] = val
                for s2, v2 in ops[p]["kn"].items():
                    kn[s2] = max(kn.get(s2, 0), v2)
        o["waits"], o["kn"] = waits, dict(kn)
        if o["kind"] == "c":
            count[o["e"]] += 1
            done[o["e"]].append(k)
            o["sig"] = ("c" + o["e"], count[o["e"]])
        elif o["kind"] == "d":
            o["sig"] = ("dm%d" % nd, 16)
            nd += 1
        else:
            o["sig"], o["kn"] = ("ar%d" % o["k"], NENG), {}
    last = [("c" + e, count[e]) for e in "DAPG"] + [("dm%d" % k, 16) for k in range(nd)]
    last += [("ar%d" % k, NENG) for k in range(NREM)] + [("lc", NREM * NENG)]
    return dict(ops=ops, order=order, last=last, start=start, end=end, best=best[3:4])


PLAN = {}


def rank_program(g, core, T, topo):
    rank = T.rank_of(core)
    if rank is None:
        return
    if not PLAN:
        PLAN.update(plan())
    q = {"D": g.vector, "A": g.scalar, "P": g.tensor, "G": g, "S": g.sync}
    x = dict(rank=rank, core=core, topo=topo)
    for k in PLAN["order"]:
        o = PLAN["ops"][k]
        for s, val in o["waits"]:
            q[o["e"]].wait_ge(T.sem[s], val)
        ins = o["fn"](g, T, x)
        if o["kind"] == "c":
            ins.then_inc(T.sem[o["sig"][0]], 1)
        elif o["kind"] == "d":
            ins.then_inc(T.sem[o["sig"][0]], 16)
    for s, val in PLAN["last"]:
        g.wait_ge(T.sem[s], val)
